import numpy as np
import ml_dtypes


def mxq(x, axis, fmt="e4m3"):
    dtype, down = {"e4m3": (ml_dtypes.float8_e4m3fn, 7), "e5m2": (ml_dtypes.float8_e5m2, 14)}[fmt]
    v = np.moveaxis(np.asarray(x, np.float32).astype(ml_dtypes.bfloat16).astype(np.float64), axis, -1)
    blocks = v.reshape(v.shape[:-1] + (-1, 32))
    amax = np.abs(blocks).max(-1, keepdims=True)
    byte = np.maximum(np.where(amax > 0, np.frexp(amax)[1] - 1 + 127, 0) - down, 1)
    scale = np.exp2(byte - 127.0)
    codes = (blocks / scale).astype(np.float32).astype(dtype).astype(np.float64)
    return np.moveaxis((codes * scale).reshape(v.shape), -1, axis)


WIDE = False


def mx_kscale(k):
    if not WIDE:
        return np.ones(k)
    levels = np.array([24, -24, 12, -12, 0])
    if k % 512:
        return np.exp2(np.random.permutation(np.resize(levels, k // 32))).repeat(32)
    a = np.empty((k // 512, 16))
    for p in range(k // 512):
        a[p, :8] = np.random.permutation(np.resize(levels, 8))
        for g in range(8):
            far = levels[np.abs(levels - a[p, g]) >= 10]
            a[p, g + 8] = far[np.random.randint(len(far))]
    return np.exp2(a.ravel()).repeat(32)


def f64(x):
    return np.asarray(x).astype(np.float64)


def striped(idx):
    return np.tile(idx.reshape(-1, 16).T, (8, 1)).astype(np.uint16)


def unstriped(offs):
    return offs[:16].T.reshape(-1).astype(np.int64)


E2M1 = np.array([0.0, 0.5, 1.0, 1.5, 2.0, 3.0, 4.0, 6.0, -0.0, -0.5, -1.0, -1.5, -2.0, -3.0, -4.0, -6.0])


def pack_weight(w, fmt):
    k, n = w.shape
    w = f64(np.asarray(w, np.float32).astype(ml_dtypes.bfloat16)).reshape(k // 32, 32, n)
    amax = np.abs(w).max(1)
    if fmt == "e4m3":
        byte = np.frexp(amax)[1] - 1 + 127 - 7
    else:
        mant, ex = np.frexp(amax / 6.0)
        byte = np.where(mant > 0.5, ex, ex - 1) + 127
    byte = np.clip(np.where(amax > 0, byte, 1), 1, 254)
    scaled = (w * np.exp2(127.0 - byte)[:, None, :]).reshape(k, n).astype(np.float32)
    by_word = np.ascontiguousarray(scaled.reshape(k // 512, 128, 4, n).transpose(0, 1, 3, 2))
    if fmt == "e4m3":
        words = by_word.astype(ml_dtypes.float8_e4m3fn).view(np.uint8)
    else:
        c = by_word.astype(ml_dtypes.float4_e2m1fn).view(np.uint8) & 0xF
        words = (c[..., 0::2] | (c[..., 1::2] << 4)).reshape(k // 512, 128, 2 * n)
    return np.ascontiguousarray(words), np.ascontiguousarray(byte.astype(np.uint8).reshape(k // 512, 16, n))


def unpack_weight(words, scales, fmt):
    g, _, n = scales.shape
    words = np.ascontiguousarray(words).reshape(g, 128, n, -1)
    if fmt == "e4m3":
        vals = words.view(ml_dtypes.float8_e4m3fn).astype(np.float64)
    else:
        nib = np.empty((g, 128, n, 4), np.uint8)
        nib[..., 0::2] = words & 0xF
        nib[..., 1::2] = words >> 4
        vals = E2M1[nib]
    vals = vals * np.repeat(np.exp2(scales.astype(np.float64) - 127.0), 8, axis=1)[..., None]
    return vals.transpose(0, 1, 3, 2).reshape(g * 512, n)


def pack_table4(v):
    words, scales = pack_weight(v, "e2m1")
    g, t = words.shape[0] // 2, v.shape[1]
    return np.ascontiguousarray(words.reshape(g, 2, 128, t, 2).transpose(0, 2, 3, 1, 4).reshape(g, 128, t, 4)), scales


def unpack_table4(words, scales):
    g, _, t, _ = words.shape
    return unpack_weight(words.reshape(g, 128, t, 2, 2).transpose(0, 3, 1, 2, 4).reshape(2 * g, 128, 2 * t), scales, "e2m1")


K, R, N, T, J = 1024, 512, 256, 2048, 1024


def setup_inputs():
    n = np.random.standard_normal
    s = mx_kscale(K)[:, None]
    u = mx_kscale(R)[:, None]
    wb = 0.7 * n((K, N)) / np.sqrt(K) / s
    wb4 = pack_weight(wb, "e2m1")
    wbrest = wb - unpack_weight(*wb4, "e2m1")
    p_tab = pack_table4(n((K, T)) * s)
    p_wb8 = pack_weight(wbrest, "e4m3")
    p_dn = pack_weight(n((K, R)) / np.sqrt(K) / s * u.T, "e4m3")
    return {
        "tab_words": p_tab[0],
        "tab_scales": p_tab[1],
        "wb4_words": wb4[0],
        "wb4_scales": wb4[1],
        "wb8_words": p_wb8[0],
        "wb8_scales": p_wb8[1],
        "dn_words": p_dn[0],
        "dn_scales": p_dn[1],
        "upw": (2.0 * n((R, N)) / np.sqrt(R) / u).astype(np.float32),
        "x0T": (n((N, T))).astype(np.float32),
        "b": (0.3 * n(N)).astype(np.float32),
        "offs": striped(np.random.permutation(T)[:J]),
    }


def reference(tab_words, tab_scales, wb4_words, wb4_scales, wb8_words, wb8_scales, dn_words, dn_scales, upw, x0T, b, offs):
    idx = unstriped(offs)
    tab_ = unpack_table4(tab_words, tab_scales)[:, idx]
    wb4_ = unpack_weight(wb4_words, wb4_scales, "e2m1")
    wb8_ = unpack_weight(wb8_words, wb8_scales, "e4m3")
    dn_ = unpack_weight(dn_words, dn_scales, "e4m3")
    hs = dn_.T @ tab_
    h = hs
    h_ = mxq(h, 0, "e4m3")
    upw_ = mxq(f64(upw), 0, "e4m3")
    y = wb4_.T @ tab_ + wb8_.T @ tab_ + upw_.T @ h_
    return f64(x0T)[:, idx] * (y + f64(b)[:, None]) + f64(x0T)[:, idx]

@@ -1,0 +1,207 @@
+from contextlib import ExitStack
+
+import concourse.mybir as mybir
+
+K, R, N, T, J = 1024, 512, 256, 2048, 1024
+FLOPS = 2 * J * (K * R + 2 * K * N + R * N)
+
+F32 = mybir.dt.float32
+BF16 = mybir.dt.bfloat16
+I32 = mybir.dt.int32
+U32 = mybir.dt.uint32
+U16 = mybir.dt.uint16
+U8 = mybir.dt.uint8
+FP8X4 = mybir.dt.float8_e4m3fn_x4
+FP4X4 = mybir.dt.float4_e2m1fn_x4
+ADD = mybir.AluOpType.add
+MULT = mybir.AluOpType.mult
+
+P = 128
+PASSES = 2
+HALF = 512
+BLK = 128
+SROWS = 32
+OFF_TAB, OFF_DN, OFF_W4, OFF_W8, WA = 0, 1024, 1536, 1792, 2048
+
+
+def tile_list_xcross_res_none_kernel(
+    tc, tab_words, tab_scales, wb4_words, wb4_scales, wb8_words, wb8_scales, dn_words, dn_scales, upw, x0T, b, offs, out
+):
+    nc = tc.nc
+    with ExitStack() as ctx:
+        held = ctx.enter_context(tc.tile_pool(name="held", bufs=1))
+        reused = ctx.enter_context(tc.tile_pool(name="reused", bufs=1))
+        ybanks = ctx.enter_context(tc.psum_pool(name="ybanks", bufs=1))
+        hbanks = ctx.enter_context(tc.psum_pool(name="hbanks", bufs=4))
+
+        def sb(shape, dtype, name, tag=None):
+            return held.tile(shape, dtype, name=name, tag=tag or name, align_bytes=64)
+
+        def scale_rows(scales):
+            return scales.bitcast(I32).rearrange("a q n -> q a n")
+
+        lst = held.tile([P, J // 16], U16, name="lst")
+        nc.sync.dma_start(lst[:], offs)
+
+        tscale = sb([P, T], U8, "tscale")
+        nc.sync.dma_start(tscale[0:SROWS, :].bitcast(I32), scale_rows(tab_scales))
+        dn_sraw = sb([P, R], U8, "dn_sraw")
+        nc.sync.dma_start(dn_sraw[0:SROWS, :].bitcast(I32), scale_rows(dn_scales))
+        stage = sb([SROWS, WA], U8, "stage", "slot_x1")
+
+        twords = sb([P, T], U32, "twords")
+        nc.sync.dma_start(twords[:].bitcast(I32), tab_words[0].rearrange("p t c -> p (t c)").bitcast(I32))
+        nc.sync.dma_start(stage[:, OFF_W4 : OFF_W4 + N].bitcast(I32), scale_rows(wb4_scales))
+        nc.sync.dma_start(stage[:, OFF_W8 : OFF_W8 + N].bitcast(I32), scale_rows(wb8_scales))
+        w8 = sb([P, PASSES, N], I32, "w8")
+        nc.sync.dma_start(w8[:], wb8_words.rearrange("a p n c -> p a (n c)").bitcast(I32))
+        w4 = sb([P, PASSES * 2 * N], U8, "w4")
+        nc.sync.dma_start(
+            w4[:].bitcast(I32).rearrange("p (a c) -> p a c", a=PASSES),
+            wb4_words.bitcast(I32).rearrange("a p c -> p a c"),
+        )
+        dn_raw = sb([P, PASSES, R], I32, "dn_raw")
+        nc.sync.dma_start(dn_raw[:], dn_words.rearrange("a p n c -> p a (n c)").bitcast(I32))
+
+        bias = sb([P, 2], F32, "bias")
+        with nc.allow_non_contiguous_dma(reason="one bias value to a partition"):
+            nc.scalar.dma_start(bias[:], b.rearrange("(u p) -> p u", p=P))
+        bias1 = sb([P, 2], F32, "bias1")
+        nc.scalar.activation(bias1[:], bias[:], mybir.ActivationFunctionType.Copy, bias=1.0)
+
+        nc.vector.memset(tscale[32:64, :].bitcast(I32), 0)
+        nc.vector.memset(tscale[64:128, :].bitcast(I32), 0)
+        nc.vector.memset(dn_sraw[32:64, :].bitcast(I32), 0)
+        nc.vector.memset(dn_sraw[64:128, :].bitcast(I32), 0)
+        plane_a = sb([P, PASSES * WA], U8, "plane_a")
+        nc.vector.memset(plane_a[:].bitcast(I32), 0)
+
+        def picks(h):
+            return lst[:, h * (HALF // 16) : (h + 1) * (HALF // 16)]
+
+        def gather_words(h):
+            g = sb([P, HALF], U32, f"gwords{h}")
+            nc.vector.tensor_copy(g[:], twords[:].indirect(picks(h)))
+            v = sb([P, PASSES * 2 * HALF], U8, f"v{h}")
+            nc.vector.tensor_copy(
+                v[:].bitcast(U16).rearrange("p (d j) -> p d j", d=PASSES),
+                g[:].bitcast(U16).rearrange("p (j d) -> p d j", d=PASSES),
+            )
+            return v
+
+        nc.vector.tensor_copy(
+            stage[:, OFF_DN : OFF_DN + R].bitcast(I32).rearrange("p (t g i) -> p t g i", t=4, i=2),
+            dn_sraw[0:SROWS, :].bitcast(I32).rearrange("p (g t i) -> p t g i", t=4, i=2),
+        )
+        gscale = reused.tile([P, J], U8, name="gscale", offset=4096 - 512, align_bytes=64)
+        nc.vector.tensor_copy(gscale[:], tscale[:].indirect(lst[:]))
+        nc.vector.tensor_copy(stage[:, OFF_TAB : OFF_TAB + J].bitcast(I32), gscale[0:SROWS, :].bitcast(I32))
+        for q in range(4):
+            nc.sync.dma_start(plane_a[32 * q : 32 * q + 4, :].bitcast(I32), stage[8 * q : 8 * q + 8, :].bitcast(I32))
+
+        x0 = [reused.tile([P, T], F32, name="x0_0", offset=4096, align_bytes=64), sb([P, T], F32, "x0_1", "slot_x1")]
+        nc.sync.dma_start(x0[0][:], x0T[0:P, :])
+        up_raw = reused.tile([P, 4, N], F32, name="up_raw", offset=0, align_bytes=64)
+        up_rows = upw.rearrange("(g t i) n -> t g i n", t=4, i=8)
+        for t in range(4):
+            nc.sync.dma_start(up_raw[:, t, :], up_rows[t])
+        nc.sync.dma_start(x0[1][:], x0T[P : 2 * P, :])
+
+        v0 = gather_words(0)
+        dn = sb([P, PASSES, R], I32, "dn")
+        nc.vector.tensor_copy(
+            dn[:].rearrange("p a (t g i) -> p a t g i", t=4, i=8),
+            dn_raw[:].rearrange("p a (g t i) -> p a t g i", t=4, i=8),
+        )
+        v1 = gather_words(1)
+        v = [v0, v1]
+
+        def tab_op(h, a, c0, n):
+            codes = v[h][:, 2 * (a * HALF + c0) : 2 * (a * HALF + c0 + n)].bitcast(FP4X4)
+            s0 = a * WA + OFF_TAB + h * HALF + c0
+            return codes, plane_a[:, s0 : s0 + n]
+
+        def wscale(a, off, c0):
+            return plane_a[:, a * WA + off + c0 : a * WA + off + c0 + P]
+
+        y = {(u, h): ybanks.tile([P, HALF], F32, name=f"y{u}{h}") for u in range(2) for h in range(2)}
+        for i in range(3):
+            nc.tensor.matmul_mx(
+                y[1, 1][:], lhsT=w8[:, 0, 0:P].bitcast(FP8X4), lhsT_scale=dn_sraw[:, 0:P],
+                rhs=w4[:].bitcast(FP4X4), rhs_scale=dn_sraw[:], start=True, stop=True,
+            )
+
+        def y_base(u, h):
+            for a in range(PASSES):
+                codes, scales = tab_op(h, a, 0, HALF)
+                nc.tensor.matmul_mx(
+                    y[u, h][:], lhsT=w8[:, a, u * P : (u + 1) * P].bitcast(FP8X4), lhsT_scale=wscale(a, OFF_W8, u * P),
+                    rhs=codes, rhs_scale=scales, start=(a == 0), stop=False,
+                )
+                nc.tensor.matmul_mx(
+                    y[u, h][:], lhsT=w4[:, 2 * (a * N + u * P) : 2 * (a * N + (u + 1) * P)].bitcast(FP4X4),
+                    lhsT_scale=wscale(a, OFF_W4, u * P), rhs=codes, rhs_scale=scales, start=False, stop=False,
+                )
+
+        def down(h):
+            hb = sb([P, HALF * 4], BF16, f"hb{h}")
+            for c in range(HALF // BLK):
+                bank = hbanks.tile([P, 4, BLK], F32, name="hbank")
+                for t in range(4):
+                    for a in range(PASSES):
+                        codes, scales = tab_op(h, a, c * BLK, BLK)
+                        nc.tensor.matmul_mx(
+                            bank[:, t, :], lhsT=dn[:, a, t * P : (t + 1) * P].bitcast(FP8X4),
+                            lhsT_scale=wscale(a, OFF_DN, t * P), rhs=codes, rhs_scale=scales,
+                            start=(a == 0), stop=(a == PASSES - 1),
+                        )
+                nc.scalar.copy(
+                    hb[:, c * 4 * BLK : (c + 1) * 4 * BLK].rearrange("p (j t) -> p j t", t=4),
+                    bank[:].rearrange("p t j -> p j t"),
+                )
+            return hb
+
+        def quant(src, width, name):
+            codes = sb([P, width], U32, name + "_codes")
+            scales = sb([P, width], U8, name + "_scales")
+            nc.vector.quantize_mx(codes[:].bitcast(FP8X4), scales[:], src[:])
+            return codes, scales
+
+        xg = {}
+
+        def gather_x(u, h):
+            xg[u, h] = sb([P, HALF], F32, f"xg{u}{h}")
+            nc.vector.tensor_copy(xg[u, h][:], x0[u][:].indirect(picks(h)))
+
+        def y_up(u, h, upq, hq):
+            nc.tensor.matmul_mx(
+                y[u, h][:], lhsT=upq[0][:, u * P : (u + 1) * P].bitcast(FP8X4), lhsT_scale=upq[1][:, u * P : (u + 1) * P],
+                rhs=hq[0][:].bitcast(FP8X4), rhs_scale=hq[1][:], start=False, stop=True,
+            )
+
+        def finish(u, h):
+            res = sb([P, HALF], F32, f"res{u}{h}")
+            nc.vector.scalar_tensor_tensor(res[:], y[u, h][:], bias1[:, u : u + 1], xg[u, h][:], ADD, MULT)
+            nc.sync.dma_start(out[u * P : (u + 1) * P, h * HALF : (h + 1) * HALF], res[:])
+
+        up_bf = sb([P, N * 4], BF16, "up_bf")
+        nc.scalar.copy(up_bf[:].rearrange("p (n t) -> p n t", t=4), up_raw[:].rearrange("p t n -> p n t"))
+        y_base(0, 0)
+        y_base(1, 0)
+        hb0 = down(0)
+        gather_x(0, 0)
+        gather_x(0, 1)
+        upq = quant(up_bf, N, "up")
+        hb1 = down(1)
+        hq0 = quant(hb0, HALF, "h0")
+        gather_x(1, 0)
+        y_up(0, 0, upq, hq0)
+        y_up(1, 0, upq, hq0)
+        gather_x(1, 1)
+        hq1 = quant(hb1, HALF, "h1")
+        finish(0, 0)
+        finish(1, 0)
+        for u in range(2):
+            y_base(u, 1)
+            y_up(u, 1, upq, hq1)
+            finish(u, 1)

@@ -20,8 +20,8 @@ P = 128
 PASSES = 2
 HALF = 512
 BLK = 128
-SROWS = 32
-OFF_TAB, OFF_DN, OFF_W4, OFF_W8, WA = 0, 1024, 1536, 1792, 2048
+S0 = 96
+OFF_DN, OFF_W4, OFF_W8, WW = 0, 512, 768, 1024
 
 
 def tile_list_xcross_res_none_kernel(
@@ -40,47 +40,43 @@ def tile_list_xcross_res_none_kernel(
         def scale_rows(scales):
             return scales.bitcast(I32).rearrange("a q n -> q a n")
 
+        def shared(shape, dtype, name, offset):
+            return reused.tile(shape, dtype, name=name, offset=offset, align_bytes=64)
+
+        stage = sb([P, WW], U8, "stage")
+        nc.sync.dma_start(stage[S0:P, OFF_W4 : OFF_W4 + N].bitcast(I32), scale_rows(wb4_scales))
+        nc.sync.dma_start(stage[S0:P, OFF_W8 : OFF_W8 + N].bitcast(I32), scale_rows(wb8_scales))
+        dn_sraw = shared([P, R], U8, "dn_sraw", 2048 - 256)
+        nc.sync.dma_start(dn_sraw[S0:P, :].bitcast(I32), scale_rows(dn_scales))
         lst = held.tile([P, J // 16], U16, name="lst")
         nc.sync.dma_start(lst[:], offs)
-
-        tscale = sb([P, T], U8, "tscale")
-        nc.sync.dma_start(tscale[0:SROWS, :].bitcast(I32), scale_rows(tab_scales))
-        dn_sraw = sb([P, R], U8, "dn_sraw")
-        nc.sync.dma_start(dn_sraw[0:SROWS, :].bitcast(I32), scale_rows(dn_scales))
-        stage = sb([SROWS, WA], U8, "stage", "slot_x1")
-
+        tscale = shared([P, T], U8, "tscale", 16384 - 1024)
+        nc.sync.dma_start(tscale[S0:P, :].bitcast(I32), scale_rows(tab_scales))
         twords = sb([P, T], U32, "twords")
         nc.sync.dma_start(twords[:].bitcast(I32), tab_words[0].rearrange("p t c -> p (t c)").bitcast(I32))
-        nc.sync.dma_start(stage[:, OFF_W4 : OFF_W4 + N].bitcast(I32), scale_rows(wb4_scales))
-        nc.sync.dma_start(stage[:, OFF_W8 : OFF_W8 + N].bitcast(I32), scale_rows(wb8_scales))
-        w8 = sb([P, PASSES, N], I32, "w8")
-        nc.sync.dma_start(w8[:], wb8_words.rearrange("a p n c -> p a (n c)").bitcast(I32))
         w4 = sb([P, PASSES * 2 * N], U8, "w4")
         nc.sync.dma_start(
             w4[:].bitcast(I32).rearrange("p (a c) -> p a c", a=PASSES),
             wb4_words.bitcast(I32).rearrange("a p c -> p a c"),
         )
-        dn_raw = sb([P, PASSES, R], I32, "dn_raw")
-        nc.sync.dma_start(dn_raw[:], dn_words.rearrange("a p n c -> p a (n c)").bitcast(I32))
 
-        bias = sb([P, 2], F32, "bias")
-        with nc.allow_non_contiguous_dma(reason="one bias value to a partition"):
-            nc.scalar.dma_start(bias[:], b.rearrange("(u p) -> p u", p=P))
-        bias1 = sb([P, 2], F32, "bias1")
-        nc.scalar.activation(bias1[:], bias[:], mybir.ActivationFunctionType.Copy, bias=1.0)
-
-        nc.vector.memset(tscale[32:64, :].bitcast(I32), 0)
-        nc.vector.memset(tscale[64:128, :].bitcast(I32), 0)
-        nc.vector.memset(dn_sraw[32:64, :].bitcast(I32), 0)
-        nc.vector.memset(dn_sraw[64:128, :].bitcast(I32), 0)
-        plane_a = sb([P, PASSES * WA], U8, "plane_a")
-        nc.vector.memset(plane_a[:].bitcast(I32), 0)
+        nc.vector.memset(tscale[0:S0, :].bitcast(I32), 0)
+        plane_w = sb([P, PASSES * WW], U8, "plane_w")
+        nc.vector.memset(plane_w[:].bitcast(I32), 0)
+        plane_t = sb([P, PASSES * J], U8, "plane_t")
+        nc.vector.memset(plane_t[:].bitcast(I32), 0)
 
         def picks(h):
             return lst[:, h * (HALF // 16) : (h + 1) * (HALF // 16)]
 
+        def spread(plane, rows, queues):
+            for q in range(4):
+                queues[q].dma_start(
+                    plane[32 * q : 32 * q + 4, :].bitcast(I32), rows[S0 + 8 * q : S0 + 8 * q + 8, :].bitcast(I32)
+                )
+
         def gather_words(h):
-            g = sb([P, HALF], U32, f"gwords{h}")
+            g = shared([P, HALF], U32, f"gwords{h}", 6144 - 1024 * h)
             nc.vector.tensor_copy(g[:], twords[:].indirect(picks(h)))
             v = sb([P, PASSES * 2 * HALF], U8, f"v{h}")
             nc.vector.tensor_copy(
@@ -90,18 +86,27 @@ def tile_list_xcross_res_none_kernel(
             return v
 
         nc.vector.tensor_copy(
-            stage[:, OFF_DN : OFF_DN + R].bitcast(I32).rearrange("p (t g i) -> p t g i", t=4, i=2),
-            dn_sraw[0:SROWS, :].bitcast(I32).rearrange("p (g t i) -> p t g i", t=4, i=2),
+            stage[S0:P, OFF_DN : OFF_DN + R].bitcast(I32).rearrange("p (t g i) -> p t g i", t=4, i=2),
+            dn_sraw[S0:P, :].bitcast(I32).rearrange("p (g t i) -> p t g i", t=4, i=2),
         )
-        gscale = reused.tile([P, J], U8, name="gscale", offset=4096 - 512, align_bytes=64)
-        nc.vector.tensor_copy(gscale[:], tscale[:].indirect(lst[:]))
-        nc.vector.tensor_copy(stage[:, OFF_TAB : OFF_TAB + J].bitcast(I32), gscale[0:SROWS, :].bitcast(I32))
-        for q in range(4):
-            nc.sync.dma_start(plane_a[32 * q : 32 * q + 4, :].bitcast(I32), stage[8 * q : 8 * q + 8, :].bitcast(I32))
+        spread(plane_w, stage, [nc.sync] * 4)
+        dn_raw = shared([P, PASSES, R], I32, "dn_raw", 2048)
+        nc.sync.dma_start(dn_raw[:], dn_words.rearrange("a p n c -> p a (n c)").bitcast(I32))
+        w8 = shared([P, PASSES, N], I32, "w8", 0)
+        nc.sync.dma_start(w8[:], wb8_words.rearrange("a p n c -> p a (n c)").bitcast(I32))
 
-        x0 = [reused.tile([P, T], F32, name="x0_0", offset=4096, align_bytes=64), sb([P, T], F32, "x0_1", "slot_x1")]
+        gscale = sb([P, J], U8, "gscale", "slot_x1")
+        nc.vector.tensor_copy(gscale[:], tscale[:].indirect(lst[:]))
+        spread(plane_t, gscale, [nc.sync] * 4)
+        bias = shared([P, 2], F32, "bias", 16384)
+        with nc.allow_non_contiguous_dma(reason="one bias value to a partition"):
+            nc.sync.dma_start(bias[:], b.rearrange("(u p) -> p u", p=P))
+        bias1 = sb([P, 2], F32, "bias1")
+        nc.scalar.activation(bias1[:], bias[:], mybir.ActivationFunctionType.Copy, bias=1.0)
+
+        x0 = [shared([P, T], F32, "x0_0", 8192), sb([P, T], F32, "x0_1", "slot_x1")]
         nc.sync.dma_start(x0[0][:], x0T[0:P, :])
-        up_raw = reused.tile([P, 4, N], F32, name="up_raw", offset=0, align_bytes=64)
+        up_raw = shared([P, 4, N], F32, "up_raw", 16448)
         up_rows = upw.rearrange("(g t i) n -> t g i n", t=4, i=8)
         for t in range(4):
             nc.sync.dma_start(up_raw[:, t, :], up_rows[t])
@@ -118,17 +123,17 @@ def tile_list_xcross_res_none_kernel(
 
         def tab_op(h, a, c0, n):
             codes = v[h][:, 2 * (a * HALF + c0) : 2 * (a * HALF + c0 + n)].bitcast(FP4X4)
-            s0 = a * WA + OFF_TAB + h * HALF + c0
-            return codes, plane_a[:, s0 : s0 + n]
+            s0 = a * J + h * HALF + c0
+            return codes, plane_t[:, s0 : s0 + n]
 
         def wscale(a, off, c0):
-            return plane_a[:, a * WA + off + c0 : a * WA + off + c0 + P]
+            return plane_w[:, a * WW + off + c0 : a * WW + off + c0 + P]
 
         y = {(u, h): ybanks.tile([P, HALF], F32, name=f"y{u}{h}") for u in range(2) for h in range(2)}
         for i in range(3):
             nc.tensor.matmul_mx(
-                y[1, 1][:], lhsT=w8[:, 0, 0:P].bitcast(FP8X4), lhsT_scale=dn_sraw[:, 0:P],
-                rhs=w4[:].bitcast(FP4X4), rhs_scale=dn_sraw[:], start=True, stop=True,
+                y[1, 1][:], lhsT=w4[:, 0 : 2 * P].bitcast(FP4X4), lhsT_scale=wscale(0, OFF_W4, 0),
+                rhs=w4[:].bitcast(FP4X4), rhs_scale=plane_w[:, OFF_W4:WW], start=True, stop=True,
             )
 
         def y_base(u, h):
@@ -144,7 +149,7 @@ def tile_list_xcross_res_none_kernel(
                 )
 
         def down(h):
-            hb = sb([P, HALF * 4], BF16, f"hb{h}")
+            hb = shared([P, HALF * 4], BF16, f"hb{h}", 16448) if h else sb([P, HALF * 4], BF16, f"hb{h}")
             for c in range(HALF // BLK):
                 bank = hbanks.tile([P, 4, BLK], F32, name="hbank")
                 for t in range(4):
@@ -161,8 +166,8 @@ def tile_list_xcross_res_none_kernel(
                 )
             return hb
 
-        def quant(src, width, name):
-            codes = sb([P, width], U32, name + "_codes")
+        def quant(src, width, name, tag=None):
+            codes = sb([P, width], U32, name + "_codes", tag)
             scales = sb([P, width], U8, name + "_scales")
             nc.vector.quantize_mx(codes[:].bitcast(FP8X4), scales[:], src[:])
             return codes, scales
@@ -179,29 +184,27 @@ def tile_list_xcross_res_none_kernel(
                 rhs=hq[0][:].bitcast(FP8X4), rhs_scale=hq[1][:], start=False, stop=True,
             )
 
-        def finish(u, h):
-            res = sb([P, HALF], F32, f"res{u}{h}")
-            nc.vector.scalar_tensor_tensor(res[:], y[u, h][:], bias1[:, u : u + 1], xg[u, h][:], ADD, MULT)
-            nc.sync.dma_start(out[u * P : (u + 1) * P, h * HALF : (h + 1) * HALF], res[:])
+        def finish(u, h, pieces=1):
+            w = HALF // pieces
+            for i in range(pieces):
+                res = sb([P, w], F32, f"res{u}{h}{i}") if h else shared([P, w], F32, f"res{u}{h}{i}", 16448 + 2048 * u)
+                cols = slice(i * w, (i + 1) * w)
+                nc.vector.scalar_tensor_tensor(res[:], y[u, h][:, cols], bias1[:, u : u + 1], xg[u, h][:, cols], ADD, MULT)
+                nc.sync.dma_start(out[u * P : (u + 1) * P, h * HALF + i * w : h * HALF + (i + 1) * w], res[:])
 
-        up_bf = sb([P, N * 4], BF16, "up_bf")
-        nc.scalar.copy(up_bf[:].rearrange("p (n t) -> p n t", t=4), up_raw[:].rearrange("p t n -> p n t"))
-        y_base(0, 0)
-        y_base(1, 0)
         hb0 = down(0)
         gather_x(0, 0)
         gather_x(0, 1)
-        upq = quant(up_bf, N, "up")
-        hb1 = down(1)
         hq0 = quant(hb0, HALF, "h0")
+        up_bf = sb([P, N * 4], BF16, "up_bf")
+        nc.scalar.copy(up_bf[:].rearrange("p (n t) -> p n t", t=4), up_raw[:].rearrange("p t n -> p n t"))
+        hb1 = down(1)
         gather_x(1, 0)
-        y_up(0, 0, upq, hq0)
-        y_up(1, 0, upq, hq0)
+        upq = quant(up_bf, N, "up")
         gather_x(1, 1)
-        hq1 = quant(hb1, HALF, "h1")
-        finish(0, 0)
-        finish(1, 0)
-        for u in range(2):
-            y_base(u, 1)
-            y_up(u, 1, upq, hq1)
-            finish(u, 1)
+        hq1 = quant(hb1, HALF, "h1", "slot_x1")
+        for h, hq in enumerate((hq0, hq1)):
+            for u in range(2):
+                y_base(u, h)
+                y_up(u, h, upq, hq)
+                finish(u, h, 1 + u * h)

@@ -17,11 +17,26 @@ ADD = mybir.AluOpType.add
 MULT = mybir.AluOpType.mult
 
 P = 128
-PASSES = 2
-HALF = 512
-BLK = 128
-S0 = 96
-OFF_DN, OFF_W4, OFF_W8, WW = 0, 512, 768, 1024
+PACK = 4
+PASSES = K // (P * PACK)
+HALF = J // 2
+BLOCK = HALF // PACK
+ROW0 = P - 16 * PASSES
+H_BANKS = 4
+WARM_PASSES = 3
+
+DN_COL, W4_COL, W8_COL, W_COLS = 0, R, R + N, R + 2 * N
+
+AT_X1 = 0
+AT_DN_RAW = AT_X1 + 4 * T - 2048
+AT_DN_SCALES = AT_DN_RAW - R // 2
+AT_WORDS1 = AT_DN_RAW + 4 * PASSES * R - 2 * HALF
+AT_WORDS0 = AT_WORDS1 + 2 * HALF
+AT_BIAS = AT_WORDS1
+AT_W8 = AT_BIAS + 64
+AT_X0 = AT_WORDS0 + 4 * HALF
+AT_UP = AT_X0 + 4 * T
+AT_TAB_SCALES = AT_UP - T // 2
 
 
 def tile_list_xcross_res_none_kernel(
@@ -32,179 +47,200 @@ def tile_list_xcross_res_none_kernel(
         held = ctx.enter_context(tc.tile_pool(name="held", bufs=1))
         reused = ctx.enter_context(tc.tile_pool(name="reused", bufs=1))
         ybanks = ctx.enter_context(tc.psum_pool(name="ybanks", bufs=1))
-        hbanks = ctx.enter_context(tc.psum_pool(name="hbanks", bufs=4))
+        hbanks = ctx.enter_context(tc.psum_pool(name="hbanks", bufs=H_BANKS))
 
-        def sb(shape, dtype, name, tag=None):
-            return held.tile(shape, dtype, name=name, tag=tag or name, align_bytes=64)
-
-        def scale_rows(scales):
-            return scales.bitcast(I32).rearrange("a q n -> q a n")
+        def own(shape, dtype, name):
+            return held.tile(shape, dtype, name=name, align_bytes=64)
 
         def shared(shape, dtype, name, offset):
             return reused.tile(shape, dtype, name=name, offset=offset, align_bytes=64)
 
-        stage = sb([P, WW], U8, "stage")
-        nc.sync.dma_start(stage[S0:P, OFF_W4 : OFF_W4 + N].bitcast(I32), scale_rows(wb4_scales))
-        nc.sync.dma_start(stage[S0:P, OFF_W8 : OFF_W8 + N].bitcast(I32), scale_rows(wb8_scales))
-        dn_sraw = shared([P, R], U8, "dn_sraw", 2048 - 256)
-        nc.sync.dma_start(dn_sraw[S0:P, :].bitcast(I32), scale_rows(dn_scales))
-        lst = held.tile([P, J // 16], U16, name="lst")
-        nc.sync.dma_start(lst[:], offs)
-        tscale = shared([P, T], U8, "tscale", 16384 - 1024)
-        nc.sync.dma_start(tscale[S0:P, :].bitcast(I32), scale_rows(tab_scales))
-        twords = sb([P, T], U32, "twords")
-        nc.sync.dma_start(twords[:].bitcast(I32), tab_words[0].rearrange("p t c -> p (t c)").bitcast(I32))
-        w4 = sb([P, PASSES * 2 * N], U8, "w4")
+        def load_scale_rows(dst, scales):
+            nc.sync.dma_start(dst.bitcast(I32), scales.bitcast(I32).rearrange("a q n -> q a n"))
+
+        def spread(plane, rows):
+            for quad in (0, 2, 1, 3):
+                nc.sync.dma_start(
+                    plane[32 * quad : 32 * quad + 4, :].bitcast(I32),
+                    rows[ROW0 + 8 * quad : ROW0 + 8 * quad + 8, :].bitcast(I32),
+                )
+
+        w_rows = own([P, W_COLS], U8, "w_rows")
+        load_scale_rows(w_rows[ROW0:P, W4_COL : W4_COL + N], wb4_scales)
+        load_scale_rows(w_rows[ROW0:P, W8_COL : W8_COL + N], wb8_scales)
+        dn_rows = shared([P, R], U8, "dn_rows", AT_DN_SCALES)
+        load_scale_rows(dn_rows[ROW0:P, :], dn_scales)
+        entries = held.tile([P, J // 16], U16, name="entries")
+        nc.sync.dma_start(entries[:], offs)
+        tab_rows = shared([P, T], U8, "tab_rows", AT_TAB_SCALES)
+        load_scale_rows(tab_rows[ROW0:P, :], tab_scales)
+        tab = own([P, T], U32, "tab")
+        nc.sync.dma_start(tab[:].bitcast(I32), tab_words[0].rearrange("p t c -> p (t c)").bitcast(I32))
+        w4 = own([P, PASSES * 2 * N], U8, "w4")
         nc.sync.dma_start(
             w4[:].bitcast(I32).rearrange("p (a c) -> p a c", a=PASSES),
             wb4_words.bitcast(I32).rearrange("a p c -> p a c"),
         )
 
-        nc.vector.memset(tscale[0:S0, :].bitcast(I32), 0)
-        plane_w = sb([P, PASSES * WW], U8, "plane_w")
-        nc.vector.memset(plane_w[:].bitcast(I32), 0)
-        plane_t = sb([P, PASSES * J], U8, "plane_t")
-        nc.vector.memset(plane_t[:].bitcast(I32), 0)
+        nc.vector.memset(tab_rows[0:ROW0, :].bitcast(I32), 0)
+        w_plane = own([P, PASSES * W_COLS], U8, "w_plane")
+        nc.vector.memset(w_plane[:].bitcast(I32), 0)
+        tab_plane = own([P, PASSES * J], U8, "tab_plane")
+        nc.vector.memset(tab_plane[:].bitcast(I32), 0)
+
+        nc.vector.tensor_copy(
+            w_rows[ROW0:P, DN_COL : DN_COL + R].bitcast(I32).rearrange("p (t g i) -> p t g i", t=PACK, i=2),
+            dn_rows[ROW0:P, :].bitcast(I32).rearrange("p (g t i) -> p t g i", t=PACK, i=2),
+        )
+        spread(w_plane, w_rows)
+        dn_raw = shared([P, PASSES, R], I32, "dn_raw", AT_DN_RAW)
+        nc.sync.dma_start(dn_raw[:], dn_words.rearrange("a p n c -> p a (n c)").bitcast(I32))
+
+        picked_rows = own([P, J], U8, "picked_rows")
+        nc.vector.tensor_copy(picked_rows[:], tab_rows[:].indirect(entries[:]))
+        spread(tab_plane, picked_rows)
+
+        x0_first = shared([P, T], F32, "x0_first", AT_X0)
+        nc.sync.dma_start(x0_first[:], x0T[0:P, :])
+        up_raw = shared([P, PACK, N], F32, "up_raw", AT_UP)
+        up_rows = upw.rearrange("(g t i) n -> t g i n", t=PACK, i=8)
+        for t in range(PACK):
+            nc.sync.dma_start(up_raw[:, t, :], up_rows[t])
 
         def picks(h):
-            return lst[:, h * (HALF // 16) : (h + 1) * (HALF // 16)]
+            return entries[:, h * (HALF // 16) : (h + 1) * (HALF // 16)]
 
-        def spread(plane, rows, queues):
-            for q in range(4):
-                queues[q].dma_start(
-                    plane[32 * q : 32 * q + 4, :].bitcast(I32), rows[S0 + 8 * q : S0 + 8 * q + 8, :].bitcast(I32)
-                )
-
-        def gather_words(h):
-            g = shared([P, HALF], U32, f"gwords{h}", 6144 - 1024 * h)
-            nc.vector.tensor_copy(g[:], twords[:].indirect(picks(h)))
-            v = sb([P, PASSES * 2 * HALF], U8, f"v{h}")
+        def gather_words(h, offset):
+            pairs = shared([P, HALF], U32, f"pairs{h}", offset)
+            nc.vector.tensor_copy(pairs[:], tab[:].indirect(picks(h)))
+            words = own([P, PASSES * 2 * HALF], U8, f"v{h}")
             nc.vector.tensor_copy(
-                v[:].bitcast(U16).rearrange("p (d j) -> p d j", d=PASSES),
-                g[:].bitcast(U16).rearrange("p (j d) -> p d j", d=PASSES),
+                words[:].bitcast(U16).rearrange("p (a j) -> p a j", a=PASSES),
+                pairs[:].bitcast(U16).rearrange("p (j a) -> p a j", a=PASSES),
             )
-            return v
+            return words
 
+        v_first = gather_words(0, AT_WORDS0)
+        dn = own([P, PASSES, R], I32, "dn")
         nc.vector.tensor_copy(
-            stage[S0:P, OFF_DN : OFF_DN + R].bitcast(I32).rearrange("p (t g i) -> p t g i", t=4, i=2),
-            dn_sraw[S0:P, :].bitcast(I32).rearrange("p (g t i) -> p t g i", t=4, i=2),
+            dn[:].rearrange("p a (t g i) -> p a t g i", t=PACK, i=8),
+            dn_raw[:].rearrange("p a (g t i) -> p a t g i", t=PACK, i=8),
         )
-        spread(plane_w, stage, [nc.sync] * 4)
-        dn_raw = shared([P, PASSES, R], I32, "dn_raw", 2048)
-        nc.sync.dma_start(dn_raw[:], dn_words.rearrange("a p n c -> p a (n c)").bitcast(I32))
-        w8 = shared([P, PASSES, N], I32, "w8", 0)
+        x0_second = shared([P, T], F32, "x0_second", AT_X1)
+        nc.sync.dma_start(x0_second[:], x0T[P : 2 * P, :])
+        v = [v_first, gather_words(1, AT_WORDS1)]
+        x0 = [x0_first, x0_second]
+        w8 = shared([P, PASSES, N], I32, "w8", AT_W8)
         nc.sync.dma_start(w8[:], wb8_words.rearrange("a p n c -> p a (n c)").bitcast(I32))
-
-        gscale = sb([P, J], U8, "gscale", "slot_x1")
-        nc.vector.tensor_copy(gscale[:], tscale[:].indirect(lst[:]))
-        spread(plane_t, gscale, [nc.sync] * 4)
-        bias = shared([P, 2], F32, "bias", 16384)
-        with nc.allow_non_contiguous_dma(reason="one bias value to a partition"):
+        bias = shared([P, N // P], F32, "bias", AT_BIAS)
+        with nc.allow_non_contiguous_dma(reason="one value of b to a partition and output tile"):
             nc.sync.dma_start(bias[:], b.rearrange("(u p) -> p u", p=P))
-        bias1 = sb([P, 2], F32, "bias1")
-        nc.scalar.activation(bias1[:], bias[:], mybir.ActivationFunctionType.Copy, bias=1.0)
+        bias1 = own([P, N // P], F32, "bias1")
+        nc.gpsimd.tensor_scalar_add(bias1[:], bias[:], 1.0)
 
-        x0 = [shared([P, T], F32, "x0_0", 8192), sb([P, T], F32, "x0_1", "slot_x1")]
-        nc.sync.dma_start(x0[0][:], x0T[0:P, :])
-        up_raw = shared([P, 4, N], F32, "up_raw", 16448)
-        up_rows = upw.rearrange("(g t i) n -> t g i n", t=4, i=8)
-        for t in range(4):
-            nc.sync.dma_start(up_raw[:, t, :], up_rows[t])
-        nc.sync.dma_start(x0[1][:], x0T[P : 2 * P, :])
+        def v_operand(h, a, first, count):
+            codes = v[h][:, 2 * (a * HALF + first) : 2 * (a * HALF + first + count)].bitcast(FP4X4)
+            col = a * J + h * HALF + first
+            return codes, tab_plane[:, col : col + count]
 
-        v0 = gather_words(0)
-        dn = sb([P, PASSES, R], I32, "dn")
-        nc.vector.tensor_copy(
-            dn[:].rearrange("p a (t g i) -> p a t g i", t=4, i=8),
-            dn_raw[:].rearrange("p a (g t i) -> p a t g i", t=4, i=8),
-        )
-        v1 = gather_words(1)
-        v = [v0, v1]
+        def w_scales(a, col):
+            return w_plane[:, a * W_COLS + col : a * W_COLS + col + P]
 
-        def tab_op(h, a, c0, n):
-            codes = v[h][:, 2 * (a * HALF + c0) : 2 * (a * HALF + c0 + n)].bitcast(FP4X4)
-            s0 = a * J + h * HALF + c0
-            return codes, plane_t[:, s0 : s0 + n]
-
-        def wscale(a, off, c0):
-            return plane_w[:, a * WW + off + c0 : a * WW + off + c0 + P]
+        def w4_codes(a, u):
+            return w4[:, 2 * (a * N + u * P) : 2 * (a * N + (u + 1) * P)].bitcast(FP4X4)
 
         y = {(u, h): ybanks.tile([P, HALF], F32, name=f"y{u}{h}") for u in range(2) for h in range(2)}
-        for i in range(3):
+
+        for repeat in range(WARM_PASSES):
             nc.tensor.matmul_mx(
-                y[1, 1][:], lhsT=w4[:, 0 : 2 * P].bitcast(FP4X4), lhsT_scale=wscale(0, OFF_W4, 0),
-                rhs=w4[:].bitcast(FP4X4), rhs_scale=plane_w[:, OFF_W4:WW], start=True, stop=True,
+                y[1, 1][:], lhsT=w4_codes(0, 0), lhsT_scale=w_scales(0, W4_COL),
+                rhs=w4[:].bitcast(FP4X4), rhs_scale=w_plane[:, W4_COL:W_COLS], start=True, stop=True,
             )
 
-        def y_base(u, h):
+        def y_wb4(u, h):
             for a in range(PASSES):
-                codes, scales = tab_op(h, a, 0, HALF)
+                codes, scales = v_operand(h, a, 0, HALF)
                 nc.tensor.matmul_mx(
-                    y[u, h][:], lhsT=w8[:, a, u * P : (u + 1) * P].bitcast(FP8X4), lhsT_scale=wscale(a, OFF_W8, u * P),
+                    y[u, h][:], lhsT=w4_codes(a, u), lhsT_scale=w_scales(a, W4_COL + u * P),
                     rhs=codes, rhs_scale=scales, start=(a == 0), stop=False,
                 )
+
+        def y_wb8(u, h):
+            for a in range(PASSES):
+                codes, scales = v_operand(h, a, 0, HALF)
                 nc.tensor.matmul_mx(
-                    y[u, h][:], lhsT=w4[:, 2 * (a * N + u * P) : 2 * (a * N + (u + 1) * P)].bitcast(FP4X4),
-                    lhsT_scale=wscale(a, OFF_W4, u * P), rhs=codes, rhs_scale=scales, start=False, stop=False,
+                    y[u, h][:], lhsT=w8[:, a, u * P : (u + 1) * P].bitcast(FP8X4), lhsT_scale=w_scales(a, W8_COL + u * P),
+                    rhs=codes, rhs_scale=scales, start=False, stop=False,
                 )
 
-        def down(h):
-            hb = shared([P, HALF * 4], BF16, f"hb{h}", 16448) if h else sb([P, HALF * 4], BF16, f"hb{h}")
-            for c in range(HALF // BLK):
-                bank = hbanks.tile([P, 4, BLK], F32, name="hbank")
-                for t in range(4):
+        def y_up(u, h, up_q, h_q):
+            cols = slice(u * P, (u + 1) * P)
+            nc.tensor.matmul_mx(
+                y[u, h][:], lhsT=up_q[0][:, cols].bitcast(FP8X4), lhsT_scale=up_q[1][:, cols],
+                rhs=h_q[0][:].bitcast(FP8X4), rhs_scale=h_q[1][:], start=False, stop=True,
+            )
+
+        def down(h, h_bf):
+            for c in range(HALF // BLOCK):
+                bank = hbanks.tile([P, PACK, BLOCK], F32, name="hbank")
+                for t in range(PACK):
                     for a in range(PASSES):
-                        codes, scales = tab_op(h, a, c * BLK, BLK)
+                        codes, scales = v_operand(h, a, c * BLOCK, BLOCK)
                         nc.tensor.matmul_mx(
                             bank[:, t, :], lhsT=dn[:, a, t * P : (t + 1) * P].bitcast(FP8X4),
-                            lhsT_scale=wscale(a, OFF_DN, t * P), rhs=codes, rhs_scale=scales,
+                            lhsT_scale=w_scales(a, DN_COL + t * P), rhs=codes, rhs_scale=scales,
                             start=(a == 0), stop=(a == PASSES - 1),
                         )
                 nc.scalar.copy(
-                    hb[:, c * 4 * BLK : (c + 1) * 4 * BLK].rearrange("p (j t) -> p j t", t=4),
+                    h_bf[:, c * PACK * BLOCK : (c + 1) * PACK * BLOCK].rearrange("p (j t) -> p j t", t=PACK),
                     bank[:].rearrange("p t j -> p j t"),
                 )
-            return hb
 
-        def quant(src, width, name, tag=None):
-            codes = sb([P, width], U32, name + "_codes", tag)
-            scales = sb([P, width], U8, name + "_scales")
+        def quantise(src, codes, name):
+            scales = own(codes.shape, U8, name)
             nc.vector.quantize_mx(codes[:].bitcast(FP8X4), scales[:], src[:])
             return codes, scales
 
-        xg = {}
+        x_picked = {}
 
         def gather_x(u, h):
-            xg[u, h] = sb([P, HALF], F32, f"xg{u}{h}")
-            nc.vector.tensor_copy(xg[u, h][:], x0[u][:].indirect(picks(h)))
+            x_picked[u, h] = own([P, HALF], F32, f"x_picked{u}{h}")
+            nc.vector.tensor_copy(x_picked[u, h][:], x0[u][:].indirect(picks(h)))
 
-        def y_up(u, h, upq, hq):
-            nc.tensor.matmul_mx(
-                y[u, h][:], lhsT=upq[0][:, u * P : (u + 1) * P].bitcast(FP8X4), lhsT_scale=upq[1][:, u * P : (u + 1) * P],
-                rhs=hq[0][:].bitcast(FP8X4), rhs_scale=hq[1][:], start=False, stop=True,
-            )
+        def finish(u, h, first, res):
+            count = res.shape[1]
+            cols = slice(first, first + count)
+            nc.vector.scalar_tensor_tensor(res[:], y[u, h][:, cols], bias1[:, u : u + 1], x_picked[u, h][:, cols], ADD, MULT)
+            nc.sync.dma_start(out[u * P : (u + 1) * P, h * HALF + first : h * HALF + first + count], res[:])
 
-        def finish(u, h, pieces=1):
-            w = HALF // pieces
-            for i in range(pieces):
-                res = sb([P, w], F32, f"res{u}{h}{i}") if h else shared([P, w], F32, f"res{u}{h}{i}", 16448 + 2048 * u)
-                cols = slice(i * w, (i + 1) * w)
-                nc.vector.scalar_tensor_tensor(res[:], y[u, h][:, cols], bias1[:, u : u + 1], xg[u, h][:, cols], ADD, MULT)
-                nc.sync.dma_start(out[u * P : (u + 1) * P, h * HALF + i * w : h * HALF + (i + 1) * w], res[:])
-
-        hb0 = down(0)
+        y_wb4(0, 0)
+        h_bf_first = own([P, HALF * PACK], BF16, "h_bf_first")
+        down(0, h_bf_first)
         gather_x(0, 0)
         gather_x(0, 1)
-        hq0 = quant(hb0, HALF, "h0")
-        up_bf = sb([P, N * 4], BF16, "up_bf")
-        nc.scalar.copy(up_bf[:].rearrange("p (n t) -> p n t", t=4), up_raw[:].rearrange("p t n -> p n t"))
-        hb1 = down(1)
+        h_q_first = quantise(h_bf_first, own([P, HALF], U32, "h_codes_first"), "h_scales_first")
+        up_bf = own([P, N * PACK], BF16, "up_bf")
+        nc.scalar.copy(up_bf[:].rearrange("p (n t) -> p n t", t=PACK), up_raw[:].rearrange("p t n -> p n t"))
+        h_bf_second = shared([P, HALF * PACK], BF16, "h_bf_second", AT_UP)
+        down(1, h_bf_second)
         gather_x(1, 0)
-        upq = quant(up_bf, N, "up")
+        up_q = quantise(up_bf, own([P, N], U32, "up_codes"), "up_scales")
         gather_x(1, 1)
-        hq1 = quant(hb1, HALF, "h1", "slot_x1")
-        for h, hq in enumerate((hq0, hq1)):
-            for u in range(2):
-                y_base(u, h)
-                y_up(u, h, upq, hq)
-                finish(u, h, 1 + u * h)
+        h_q_second = quantise(h_bf_second, shared([P, HALF], U32, "h_codes_second", AT_X1), "h_scales_second")
+
+        y_wb4(1, 0)
+        y_wb8(0, 0)
+        y_up(0, 0, up_q, h_q_first)
+        finish(0, 0, 0, shared([P, HALF], F32, "res00", AT_UP))
+        y_wb8(1, 0)
+        y_up(1, 0, up_q, h_q_first)
+        finish(1, 0, 0, shared([P, HALF], F32, "res10", AT_UP + 4 * HALF))
+        y_wb4(0, 1)
+        y_wb8(0, 1)
+        y_up(0, 1, up_q, h_q_second)
+        finish(0, 1, 0, own([P, HALF], F32, "res01"))
+        y_wb4(1, 1)
+        y_wb8(1, 1)
+        y_up(1, 1, up_q, h_q_second)
+        for piece in range(2):
+            finish(1, 1, piece * HALF // 2, own([P, HALF // 2], F32, f"res11_{piece}"))

@@ -15,28 +15,31 @@ FP8X4 = mybir.dt.float8_e4m3fn_x4
 FP4X4 = mybir.dt.float4_e2m1fn_x4
 ADD = mybir.AluOpType.add
 MULT = mybir.AluOpType.mult
+IDENTITY = mybir.ActivationFunctionType.Identity
 
 P = 128
 PACK = 4
 PASSES = K // (P * PACK)
 HALF = J // 2
+QUART = J // 4
 BLOCK = HALF // PACK
 ROW0 = P - 16 * PASSES
 H_BANKS = 4
-WARM_PASSES = 3
+WARM_PASSES = 7
 
-DN_COL, W4_COL, W8_COL, W_COLS = 0, R, R + N, R + 2 * N
+DN_COL, W4_COL, W8_COL, TAB_COL, COLS = 0, R, R + N, R + 2 * N, R + 2 * N + J
+EARLY = TAB_COL + HALF
 
-AT_X1 = 0
-AT_DN_RAW = AT_X1 + 4 * T - 2048
-AT_DN_SCALES = AT_DN_RAW - R // 2
-AT_WORDS1 = AT_DN_RAW + 4 * PASSES * R - 2 * HALF
-AT_WORDS0 = AT_WORDS1 + 2 * HALF
-AT_BIAS = AT_WORDS1
-AT_W8 = AT_BIAS + 64
-AT_X0 = AT_WORDS0 + 4 * HALF
-AT_UP = AT_X0 + 4 * T
-AT_TAB_SCALES = AT_UP - T // 2
+AT_V0 = 0
+AT_DN0 = AT_V0 + 2 * HALF
+AT_PAIRS1 = AT_V0 + 4 * HALF
+AT_W8 = AT_DN0 + 4 * R
+AT_X0 = AT_W8 + 4 * PASSES * N
+AT_TAB_SCALES = AT_X0 + 4 * T
+AT_BIAS = AT_TAB_SCALES
+AT_X1 = AT_BIAS + 64
+AT_DN1 = AT_X1 + 4 * T
+AT_H = AT_DN1 + 2 * 4 * R
 
 
 def tile_list_xcross_res_none_kernel(
@@ -55,96 +58,108 @@ def tile_list_xcross_res_none_kernel(
         def shared(shape, dtype, name, offset):
             return reused.tile(shape, dtype, name=name, offset=offset, align_bytes=64)
 
-        def load_scale_rows(dst, scales):
-            nc.sync.dma_start(dst.bitcast(I32), scales.bitcast(I32).rearrange("a q n -> q a n"))
+        def load_scale_rows(queue, dst, scales):
+            queue.dma_start(dst.bitcast(I32), scales.bitcast(I32).rearrange("a q n -> q a n"))
 
-        def spread(plane, rows):
+        def spread(queue, rows, first, count):
             for quad in (0, 2, 1, 3):
-                nc.sync.dma_start(
-                    plane[32 * quad : 32 * quad + 4, :].bitcast(I32),
+                queue.dma_start(
+                    plane[32 * quad : 32 * quad + 4, :].bitcast(I32).rearrange("p (a c) -> p a c", a=PASSES)[
+                        :, :, first // 4 : (first + count) // 4
+                    ],
                     rows[ROW0 + 8 * quad : ROW0 + 8 * quad + 8, :].bitcast(I32),
                 )
 
-        w_rows = own([P, W_COLS], U8, "w_rows")
-        load_scale_rows(w_rows[ROW0:P, W4_COL : W4_COL + N], wb4_scales)
-        load_scale_rows(w_rows[ROW0:P, W8_COL : W8_COL + N], wb8_scales)
-        dn_rows = shared([P, R], U8, "dn_rows", AT_DN_SCALES)
-        load_scale_rows(dn_rows[ROW0:P, :], dn_scales)
         entries = held.tile([P, J // 16], U16, name="entries")
         nc.sync.dma_start(entries[:], offs)
         tab_rows = shared([P, T], U8, "tab_rows", AT_TAB_SCALES)
-        load_scale_rows(tab_rows[ROW0:P, :], tab_scales)
-        tab = own([P, T], U32, "tab")
-        nc.sync.dma_start(tab[:].bitcast(I32), tab_words[0].rearrange("p t c -> p (t c)").bitcast(I32))
+        load_scale_rows(nc.sync, tab_rows[ROW0:P, :], tab_scales)
+        dn_rows = own([P, R], U8, "dn_rows")
+        load_scale_rows(nc.scalar, dn_rows[ROW0:P, :], dn_scales)
+        staged = own([P, EARLY], U8, "staged")
+        load_scale_rows(nc.scalar, staged[ROW0:P, W4_COL : W4_COL + N], wb4_scales)
+        load_scale_rows(nc.scalar, staged[ROW0:P, W8_COL : W8_COL + N], wb8_scales)
         w4 = own([P, PASSES * 2 * N], U8, "w4")
         nc.sync.dma_start(
             w4[:].bitcast(I32).rearrange("p (a c) -> p a c", a=PASSES),
             wb4_words.bitcast(I32).rearrange("a p c -> p a c"),
         )
+        tab = own([P, T], U32, "tab")
+        nc.sync.dma_start(tab[:].bitcast(I32), tab_words[0].rearrange("p t c -> p (t c)").bitcast(I32))
+        dn_raw = [
+            shared([P, (AT_X0 + 64 - AT_DN0) // 4], I32, "dn_raw0", AT_DN0)[:, 0:R],
+            shared([P, R], I32, "dn_raw1", AT_DN1)[:],
+        ]
+        for a in range(PASSES):
+            nc.sync.dma_start(dn_raw[a], dn_words[a].rearrange("p n c -> p (n c)").bitcast(I32))
+        up_raw = own([P, PACK, N], F32, "up_raw")
+        nc.sync.dma_start(up_raw[:], upw.rearrange("(p t) n -> p t n", t=PACK))
 
         nc.vector.memset(tab_rows[0:ROW0, :].bitcast(I32), 0)
-        w_plane = own([P, PASSES * W_COLS], U8, "w_plane")
-        nc.vector.memset(w_plane[:].bitcast(I32), 0)
-        tab_plane = own([P, PASSES * J], U8, "tab_plane")
-        nc.vector.memset(tab_plane[:].bitcast(I32), 0)
+        nc.vector.memset(dn_rows[0:ROW0, :].bitcast(I32), 0)
+        plane = own([P, PASSES * COLS], U8, "plane")
+        nc.vector.memset(plane[:].bitcast(I32), 0)
+        nc.vector.memset(staged[0:ROW0, TAB_COL : TAB_COL + QUART].bitcast(I32), 0)
 
+        def picks(first, count):
+            return entries[:, first // 16 : (first + count) // 16]
+
+        picked0 = own([P, HALF], U8, "picked0")
+        nc.vector.tensor_copy(picked0[:, 0:HALF], tab_rows[:].indirect(picks(0, HALF)))
         nc.vector.tensor_copy(
-            w_rows[ROW0:P, DN_COL : DN_COL + R].bitcast(I32).rearrange("p (t g i) -> p t g i", t=PACK, i=2),
-            dn_rows[ROW0:P, :].bitcast(I32).rearrange("p (g t i) -> p t g i", t=PACK, i=2),
+            staged[:, DN_COL : DN_COL + R].rearrange("p (t m) -> p t m", t=PACK),
+            dn_rows[:].rearrange("p (m t) -> p t m", t=PACK),
         )
-        spread(w_plane, w_rows)
-        dn_raw = shared([P, PASSES, R], I32, "dn_raw", AT_DN_RAW)
-        nc.sync.dma_start(dn_raw[:], dn_words.rearrange("a p n c -> p a (n c)").bitcast(I32))
+        nc.vector.tensor_copy(staged[ROW0:P, TAB_COL:EARLY].bitcast(I32), picked0[ROW0:P, 0:HALF].bitcast(I32))
+        spread(nc.scalar, staged, 0, EARLY)
 
-        picked_rows = own([P, J], U8, "picked_rows")
-        nc.vector.tensor_copy(picked_rows[:], tab_rows[:].indirect(entries[:]))
-        spread(tab_plane, picked_rows)
 
-        x0_first = shared([P, T], F32, "x0_first", AT_X0)
-        nc.sync.dma_start(x0_first[:], x0T[0:P, :])
-        up_raw = shared([P, PACK, N], F32, "up_raw", AT_UP)
-        up_rows = upw.rearrange("(g t i) n -> t g i n", t=PACK, i=8)
-        for t in range(PACK):
-            nc.sync.dma_start(up_raw[:, t, :], up_rows[t])
+        v = [shared([P, PASSES * 2 * HALF], U8, "v0", AT_V0), own([P, PASSES * 2 * HALF], U8, "v1")]
 
-        def picks(h):
-            return entries[:, h * (HALF // 16) : (h + 1) * (HALF // 16)]
+        def gather_words(quarter, pairs):
+            nc.vector.tensor_copy(pairs[:], tab[:].indirect(picks(quarter * QUART, QUART)))
+            return pairs
 
-        def gather_words(h, offset):
-            pairs = shared([P, HALF], U32, f"pairs{h}", offset)
-            nc.vector.tensor_copy(pairs[:], tab[:].indirect(picks(h)))
-            words = own([P, PASSES * 2 * HALF], U8, f"v{h}")
+        def part_words(quarter, pairs):
+            h, first = quarter // 2, quarter % 2 * QUART
             nc.vector.tensor_copy(
-                words[:].bitcast(U16).rearrange("p (a j) -> p a j", a=PASSES),
+                v[h][:].bitcast(U16).rearrange("p (a j) -> p a j", a=PASSES)[:, :, first : first + QUART],
                 pairs[:].bitcast(U16).rearrange("p (j a) -> p a j", a=PASSES),
             )
-            return words
 
-        v_first = gather_words(0, AT_WORDS0)
+        pairs_first = gather_words(0, own([P, QUART], U32, "pairs0"))
         dn = own([P, PASSES, R], I32, "dn")
-        nc.vector.tensor_copy(
-            dn[:].rearrange("p a (t g i) -> p a t g i", t=PACK, i=8),
-            dn_raw[:].rearrange("p a (g t i) -> p a t g i", t=PACK, i=8),
-        )
-        x0_second = shared([P, T], F32, "x0_second", AT_X1)
-        nc.sync.dma_start(x0_second[:], x0T[P : 2 * P, :])
-        v = [v_first, gather_words(1, AT_WORDS1)]
-        x0 = [x0_first, x0_second]
+        for a in range(PASSES):
+            nc.vector.tensor_copy(
+                dn[:, a, :].rearrange("p (t m i) -> p m t i", t=PACK, i=4),
+                dn_raw[a].rearrange("p (m i t) -> p m t i", t=PACK, i=4),
+            )
+        x0 = [shared([P, T], F32, "x0_first", AT_X0), shared([P, T], F32, "x0_second", AT_X1)]
+        nc.sync.dma_start(x0[0][:], x0T[0:P, :])
         w8 = shared([P, PASSES, N], I32, "w8", AT_W8)
         nc.sync.dma_start(w8[:], wb8_words.rearrange("a p n c -> p a (n c)").bitcast(I32))
+        part_words(0, pairs_first)
+        part_words(1, gather_words(1, shared([P, QUART], U32, "pairs1", AT_PAIRS1)))
+        picked1 = shared([P, HALF], U8, "picked1", AT_DN1)
+        nc.vector.tensor_copy(picked1[:], tab_rows[:].indirect(picks(HALF, HALF)))
+        spread(nc.sync, picked1, EARLY, HALF)
         bias = shared([P, N // P], F32, "bias", AT_BIAS)
         with nc.allow_non_contiguous_dma(reason="one value of b to a partition and output tile"):
             nc.sync.dma_start(bias[:], b.rearrange("(u p) -> p u", p=P))
+        nc.sync.dma_start(x0[1][:], x0T[P : 2 * P, :])
         bias1 = own([P, N // P], F32, "bias1")
         nc.gpsimd.tensor_scalar_add(bias1[:], bias[:], 1.0)
+        for quarter in range(2, 4):
+            pairs = shared([P, QUART], U32, f"pairs{quarter}", AT_DN1 + HALF + 4 * QUART * (quarter - 2))
+            part_words(quarter, gather_words(quarter, pairs))
 
         def v_operand(h, a, first, count):
             codes = v[h][:, 2 * (a * HALF + first) : 2 * (a * HALF + first + count)].bitcast(FP4X4)
-            col = a * J + h * HALF + first
-            return codes, tab_plane[:, col : col + count]
+            col = a * COLS + TAB_COL + h * HALF + first
+            return codes, plane[:, col : col + count]
 
         def w_scales(a, col):
-            return w_plane[:, a * W_COLS + col : a * W_COLS + col + P]
+            return plane[:, a * COLS + col : a * COLS + col + P]
 
         def w4_codes(a, u):
             return w4[:, 2 * (a * N + u * P) : 2 * (a * N + (u + 1) * P)].bitcast(FP4X4)
@@ -153,16 +168,17 @@ def tile_list_xcross_res_none_kernel(
 
         for repeat in range(WARM_PASSES):
             nc.tensor.matmul_mx(
-                y[1, 1][:], lhsT=w4_codes(0, 0), lhsT_scale=w_scales(0, W4_COL),
-                rhs=w4[:].bitcast(FP4X4), rhs_scale=w_plane[:, W4_COL:W_COLS], start=True, stop=True,
+                y[1, 1][:, 0:QUART], lhsT=w4_codes(0, 0), lhsT_scale=staged[:, 0:P],
+                rhs=w4[:, 0 : 2 * QUART].bitcast(FP4X4), rhs_scale=staged[:, TAB_COL : TAB_COL + QUART],
+                start=(repeat == 0), stop=(repeat == WARM_PASSES - 1),
             )
 
-        def y_wb4(u, h):
+        def y_wb4(u, h, first, count):
             for a in range(PASSES):
-                codes, scales = v_operand(h, a, 0, HALF)
+                codes, scales = v_operand(h, a, first, count)
                 nc.tensor.matmul_mx(
-                    y[u, h][:], lhsT=w4_codes(a, u), lhsT_scale=w_scales(a, W4_COL + u * P),
-                    rhs=codes, rhs_scale=scales, start=(a == 0), stop=False,
+                    y[u, h][:, first : first + count], lhsT=w4_codes(a, u), lhsT_scale=w_scales(a, W4_COL + u * P),
+                    rhs=codes, rhs_scale=scales, start=(a == 0 and first == 0), stop=False,
                 )
 
         def y_wb8(u, h):
@@ -180,8 +196,8 @@ def tile_list_xcross_res_none_kernel(
                 rhs=h_q[0][:].bitcast(FP8X4), rhs_scale=h_q[1][:], start=False, stop=True,
             )
 
-        def down(h, h_bf):
-            for c in range(HALF // BLOCK):
+        def down(h, h_bf, blocks):
+            for c in blocks:
                 bank = hbanks.tile([P, PACK, BLOCK], F32, name="hbank")
                 for t in range(PACK):
                     for a in range(PASSES):
@@ -196,51 +212,59 @@ def tile_list_xcross_res_none_kernel(
                     bank[:].rearrange("p t j -> p j t"),
                 )
 
-        def quantise(src, codes, name):
-            scales = own(codes.shape, U8, name)
+        def quantise(src, name):
+            width = src.shape[1] // PACK
+            codes, scales = own([P, width], U32, name + "_codes"), own([P, width], U8, name + "_scales")
             nc.vector.quantize_mx(codes[:].bitcast(FP8X4), scales[:], src[:])
             return codes, scales
 
         x_picked = {}
 
         def gather_x(u, h):
-            x_picked[u, h] = own([P, HALF], F32, f"x_picked{u}{h}")
-            nc.vector.tensor_copy(x_picked[u, h][:], x0[u][:].indirect(picks(h)))
+            x_picked[u, h] = shared([P, HALF], F32, f"x_picked{u}{h}", AT_H + 2 * 2 * PACK * HALF * u)
+            nc.vector.tensor_copy(x_picked[u, h][:], x0[u][:].indirect(picks(h * HALF, HALF)))
 
-        def finish(u, h, first, res):
-            count = res.shape[1]
+        def store(u, h, first, res):
+            nc.sync.dma_start(out[u * P : (u + 1) * P, h * HALF + first : h * HALF + first + res.shape[1]], res[:])
+
+        def finish(u, h, first, count):
+            res = own([P, count], F32, f"res{u}{h}_{first}")
             cols = slice(first, first + count)
             nc.vector.scalar_tensor_tensor(res[:], y[u, h][:, cols], bias1[:, u : u + 1], x_picked[u, h][:, cols], ADD, MULT)
-            nc.sync.dma_start(out[u * P : (u + 1) * P, h * HALF + first : h * HALF + first + count], res[:])
+            store(u, h, first, res)
 
-        y_wb4(0, 0)
-        h_bf_first = own([P, HALF * PACK], BF16, "h_bf_first")
-        down(0, h_bf_first)
-        gather_x(0, 0)
-        gather_x(0, 1)
-        h_q_first = quantise(h_bf_first, own([P, HALF], U32, "h_codes_first"), "h_scales_first")
+        def finish_fused(u, h):
+            factor = own([P, HALF], F32, f"factor{u}{h}")
+            nc.scalar.activation(factor[:], y[u, h][:], IDENTITY, bias=bias1[:, u : u + 1])
+            res = own([P, HALF], F32, f"res{u}{h}")
+            nc.vector.tensor_tensor(res[:], x0[u][:].indirect(picks(h * HALF, HALF)), factor[:], MULT)
+            store(u, h, 0, res)
+
         up_bf = own([P, N * PACK], BF16, "up_bf")
         nc.scalar.copy(up_bf[:].rearrange("p (n t) -> p n t", t=PACK), up_raw[:].rearrange("p t n -> p n t"))
-        h_bf_second = shared([P, HALF * PACK], BF16, "h_bf_second", AT_UP)
-        down(1, h_bf_second)
-        gather_x(1, 0)
-        up_q = quantise(up_bf, own([P, N], U32, "up_codes"), "up_scales")
-        gather_x(1, 1)
-        h_q_second = quantise(h_bf_second, shared([P, HALF], U32, "h_codes_second", AT_X1), "h_scales_second")
-
-        y_wb4(1, 0)
+        for u in range(2):
+            y_wb4(u, 0, 0, QUART)
+        h_bf = [shared([P, HALF * PACK], BF16, f"h_bf{h}", AT_H + 2 * PACK * HALF * h) for h in range(2)]
+        down(0, h_bf[0], range(4))
+        up_q = quantise(up_bf, "up")
+        h_q_first = quantise(h_bf[0], "h_first")
+        gather_x(0, 1)
+        y_wb4(0, 0, QUART, QUART)
         y_wb8(0, 0)
+        down(1, h_bf[1], range(1))
         y_up(0, 0, up_q, h_q_first)
-        finish(0, 0, 0, shared([P, HALF], F32, "res00", AT_UP))
+        finish_fused(0, 0)
+        down(1, h_bf[1], range(1, 4))
+        gather_x(1, 1)
+        h_q_second = quantise(h_bf[1], "h_second")
+        y_wb4(1, 0, QUART, QUART)
         y_wb8(1, 0)
         y_up(1, 0, up_q, h_q_first)
-        finish(1, 0, 0, shared([P, HALF], F32, "res10", AT_UP + 4 * HALF))
-        y_wb4(0, 1)
-        y_wb8(0, 1)
-        y_up(0, 1, up_q, h_q_second)
-        finish(0, 1, 0, own([P, HALF], F32, "res01"))
-        y_wb4(1, 1)
-        y_wb8(1, 1)
-        y_up(1, 1, up_q, h_q_second)
+        finish_fused(1, 0)
+        for u in (1, 0):
+            y_wb4(u, 1, 0, HALF)
+            y_wb8(u, 1)
+            y_up(u, 1, up_q, h_q_second)
+        finish(1, 1, 0, HALF)
         for piece in range(2):
-            finish(1, 1, piece * HALF // 2, own([P, HALF // 2], F32, f"res11_{piece}"))
+            finish(0, 1, piece * QUART, QUART)

@@ -24,22 +24,18 @@ HALF = J // 2
 QUART = J // 4
 BLOCK = HALF // PACK
 ROW0 = P - 16 * PASSES
-H_BANKS = 4
-WARM_PASSES = 7
+H_BANKS = 5
+WARM_PASSES = 3
 
-DN_COL, W4_COL, W8_COL, TAB_COL, COLS = 0, R, R + N, R + 2 * N, R + 2 * N + J
-EARLY = TAB_COL + HALF
+DN_COL, W4_COL, W8_COL, W_COLS = 0, R, R + N, R + 2 * N
 
-AT_V0 = 0
-AT_DN0 = AT_V0 + 2 * HALF
-AT_PAIRS1 = AT_V0 + 4 * HALF
-AT_W8 = AT_DN0 + 4 * R
+AT_TAB_SCALES = 0
+AT_UP = 0
+AT_W8 = AT_UP + 4 * PACK * N
 AT_X0 = AT_W8 + 4 * PASSES * N
-AT_TAB_SCALES = AT_X0 + 4 * T
-AT_BIAS = AT_TAB_SCALES
+AT_BIAS = AT_X0 + 4 * T
 AT_X1 = AT_BIAS + 64
-AT_DN1 = AT_X1 + 4 * T
-AT_H = AT_DN1 + 2 * 4 * R
+AT_DN = AT_X1 + 4 * T
 
 
 def tile_list_xcross_res_none_kernel(
@@ -61,24 +57,22 @@ def tile_list_xcross_res_none_kernel(
         def load_scale_rows(queue, dst, scales):
             queue.dma_start(dst.bitcast(I32), scales.bitcast(I32).rearrange("a q n -> q a n"))
 
-        def spread(queue, rows, first, count):
+        def spread(plane, rows):
             for quad in (0, 2, 1, 3):
-                queue.dma_start(
-                    plane[32 * quad : 32 * quad + 4, :].bitcast(I32).rearrange("p (a c) -> p a c", a=PASSES)[
-                        :, :, first // 4 : (first + count) // 4
-                    ],
+                nc.sync.dma_start(
+                    plane[32 * quad : 32 * quad + 4, :].bitcast(I32),
                     rows[ROW0 + 8 * quad : ROW0 + 8 * quad + 8, :].bitcast(I32),
                 )
 
         entries = held.tile([P, J // 16], U16, name="entries")
         nc.sync.dma_start(entries[:], offs)
-        tab_rows = shared([P, T], U8, "tab_rows", AT_TAB_SCALES)
+        tab_rows = shared([P, AT_X1 + 64], U8, "tab_rows", AT_TAB_SCALES)[:, 0:T]
         load_scale_rows(nc.sync, tab_rows[ROW0:P, :], tab_scales)
-        dn_rows = own([P, R], U8, "dn_rows")
+        dn_rows = shared([P, R], U8, "dn_rows", AT_DN)
         load_scale_rows(nc.scalar, dn_rows[ROW0:P, :], dn_scales)
-        staged = own([P, EARLY], U8, "staged")
-        load_scale_rows(nc.scalar, staged[ROW0:P, W4_COL : W4_COL + N], wb4_scales)
-        load_scale_rows(nc.scalar, staged[ROW0:P, W8_COL : W8_COL + N], wb8_scales)
+        w_rows = own([P, W_COLS], U8, "w_rows")
+        load_scale_rows(nc.scalar, w_rows[ROW0:P, W4_COL : W4_COL + N], wb4_scales)
+        load_scale_rows(nc.scalar, w_rows[ROW0:P, W8_COL : W8_COL + N], wb8_scales)
         w4 = own([P, PASSES * 2 * N], U8, "w4")
         nc.sync.dma_start(
             w4[:].bitcast(I32).rearrange("p (a c) -> p a c", a=PASSES),
@@ -86,91 +80,78 @@ def tile_list_xcross_res_none_kernel(
         )
         tab = own([P, T], U32, "tab")
         nc.sync.dma_start(tab[:].bitcast(I32), tab_words[0].rearrange("p t c -> p (t c)").bitcast(I32))
-        dn_raw = [
-            shared([P, (AT_X0 + 64 - AT_DN0) // 4], I32, "dn_raw0", AT_DN0)[:, 0:R],
-            shared([P, R], I32, "dn_raw1", AT_DN1)[:],
-        ]
-        for a in range(PASSES):
-            nc.sync.dma_start(dn_raw[a], dn_words[a].rearrange("p n c -> p (n c)").bitcast(I32))
-        up_raw = own([P, PACK, N], F32, "up_raw")
-        nc.sync.dma_start(up_raw[:], upw.rearrange("(p t) n -> p t n", t=PACK))
 
         nc.vector.memset(tab_rows[0:ROW0, :].bitcast(I32), 0)
         nc.vector.memset(dn_rows[0:ROW0, :].bitcast(I32), 0)
-        plane = own([P, PASSES * COLS], U8, "plane")
-        nc.vector.memset(plane[:].bitcast(I32), 0)
-        nc.vector.memset(staged[0:ROW0, TAB_COL : TAB_COL + QUART].bitcast(I32), 0)
+        w_plane = own([P, PASSES * W_COLS], U8, "w_plane")
+        nc.vector.memset(w_plane[:].bitcast(I32), 0)
+        tab_plane = own([P, PASSES * J], U8, "tab_plane")
+        nc.vector.memset(tab_plane[:].bitcast(I32), 0)
 
         def picks(first, count):
             return entries[:, first // 16 : (first + count) // 16]
 
-        picked0 = own([P, HALF], U8, "picked0")
-        nc.vector.tensor_copy(picked0[:, 0:HALF], tab_rows[:].indirect(picks(0, HALF)))
         nc.vector.tensor_copy(
-            staged[:, DN_COL : DN_COL + R].rearrange("p (t m) -> p t m", t=PACK),
+            w_rows[:, DN_COL : DN_COL + R].rearrange("p (t m) -> p t m", t=PACK),
             dn_rows[:].rearrange("p (m t) -> p t m", t=PACK),
         )
-        nc.vector.tensor_copy(staged[ROW0:P, TAB_COL:EARLY].bitcast(I32), picked0[ROW0:P, 0:HALF].bitcast(I32))
-        spread(nc.scalar, staged, 0, EARLY)
+        spread(w_plane, w_rows)
+        dn_raw = shared([P, PASSES, R], I32, "dn_raw", AT_DN)
+        nc.sync.dma_start(dn_raw[:], dn_words.rearrange("a p n c -> p a (n c)").bitcast(I32))
+        picked = own([P, J], U8, "picked")
+        nc.vector.tensor_copy(picked[:], tab_rows.indirect(entries[:]))
+        spread(tab_plane, picked)
 
-
-        v = [shared([P, PASSES * 2 * HALF], U8, "v0", AT_V0), own([P, PASSES * 2 * HALF], U8, "v1")]
-
-        def gather_words(quarter, pairs):
-            nc.vector.tensor_copy(pairs[:], tab[:].indirect(picks(quarter * QUART, QUART)))
-            return pairs
-
-        def part_words(quarter, pairs):
-            h, first = quarter // 2, quarter % 2 * QUART
-            nc.vector.tensor_copy(
-                v[h][:].bitcast(U16).rearrange("p (a j) -> p a j", a=PASSES)[:, :, first : first + QUART],
-                pairs[:].bitcast(U16).rearrange("p (j a) -> p a j", a=PASSES),
-            )
-
-        pairs_first = gather_words(0, own([P, QUART], U32, "pairs0"))
-        dn = own([P, PASSES, R], I32, "dn")
-        for a in range(PASSES):
-            nc.vector.tensor_copy(
-                dn[:, a, :].rearrange("p (t m i) -> p m t i", t=PACK, i=4),
-                dn_raw[a].rearrange("p (m i t) -> p m t i", t=PACK, i=4),
-            )
-        x0 = [shared([P, T], F32, "x0_first", AT_X0), shared([P, T], F32, "x0_second", AT_X1)]
-        nc.sync.dma_start(x0[0][:], x0T[0:P, :])
+        up_raw = shared([P, PACK, N], F32, "up_raw", AT_UP)
+        nc.sync.dma_start(up_raw[:], upw.rearrange("(p t) n -> p t n", t=PACK))
         w8 = shared([P, PASSES, N], I32, "w8", AT_W8)
         nc.sync.dma_start(w8[:], wb8_words.rearrange("a p n c -> p a (n c)").bitcast(I32))
-        part_words(0, pairs_first)
-        part_words(1, gather_words(1, shared([P, QUART], U32, "pairs1", AT_PAIRS1)))
-        picked1 = shared([P, HALF], U8, "picked1", AT_DN1)
-        nc.vector.tensor_copy(picked1[:], tab_rows[:].indirect(picks(HALF, HALF)))
-        spread(nc.sync, picked1, EARLY, HALF)
+        x0 = [shared([P, T], F32, "x0_first", AT_X0), shared([P, T], F32, "x0_second", AT_X1)]
+        nc.sync.dma_start(x0[0][:], x0T[0:P, :])
         bias = shared([P, N // P], F32, "bias", AT_BIAS)
         with nc.allow_non_contiguous_dma(reason="one value of b to a partition and output tile"):
             nc.sync.dma_start(bias[:], b.rearrange("(u p) -> p u", p=P))
         nc.sync.dma_start(x0[1][:], x0T[P : 2 * P, :])
         bias1 = own([P, N // P], F32, "bias1")
         nc.gpsimd.tensor_scalar_add(bias1[:], bias[:], 1.0)
+
+        v = [own([P, PASSES * 2 * HALF], U8, f"v{h}") for h in range(2)]
+
+        def gather_words(quarter, pairs):
+            h, first = quarter // 2, quarter % 2 * QUART
+            nc.vector.tensor_copy(pairs[:], tab[:].indirect(picks(quarter * QUART, QUART)))
+            nc.vector.tensor_copy(
+                v[h][:].bitcast(U16).rearrange("p (a j) -> p a j", a=PASSES)[:, :, first : first + QUART],
+                pairs[:].bitcast(U16).rearrange("p (j a) -> p a j", a=PASSES),
+            )
+
+        for quarter in range(2):
+            gather_words(quarter, own([P, QUART], U32, f"pairs{quarter}"))
+        dn = own([P, PASSES, R], I32, "dn")
+        nc.vector.tensor_copy(
+            dn[:].rearrange("p a (t m i) -> p a m t i", t=PACK, i=4),
+            dn_raw[:].rearrange("p a (m i t) -> p a m t i", t=PACK, i=4),
+        )
         for quarter in range(2, 4):
-            pairs = shared([P, QUART], U32, f"pairs{quarter}", AT_DN1 + HALF + 4 * QUART * (quarter - 2))
-            part_words(quarter, gather_words(quarter, pairs))
+            gather_words(quarter, shared([P, QUART], U32, f"pairs{quarter}", AT_DN + 4 * QUART * quarter))
 
         def v_operand(h, a, first, count):
             codes = v[h][:, 2 * (a * HALF + first) : 2 * (a * HALF + first + count)].bitcast(FP4X4)
-            col = a * COLS + TAB_COL + h * HALF + first
-            return codes, plane[:, col : col + count]
+            col = a * J + h * HALF + first
+            return codes, tab_plane[:, col : col + count]
 
         def w_scales(a, col):
-            return plane[:, a * COLS + col : a * COLS + col + P]
+            return w_plane[:, a * W_COLS + col : a * W_COLS + col + P]
 
         def w4_codes(a, u):
             return w4[:, 2 * (a * N + u * P) : 2 * (a * N + (u + 1) * P)].bitcast(FP4X4)
 
-        y = {(u, h): ybanks.tile([P, HALF], F32, name=f"y{u}{h}") for u in range(2) for h in range(2)}
+        y = {(u, h): ybanks.tile([P, HALF], F32, name=f"y{u}{h}") for u, h in ((0, 0), (1, 0), (1, 1))}
 
         for repeat in range(WARM_PASSES):
             nc.tensor.matmul_mx(
-                y[1, 1][:, 0:QUART], lhsT=w4_codes(0, 0), lhsT_scale=staged[:, 0:P],
-                rhs=w4[:, 0 : 2 * QUART].bitcast(FP4X4), rhs_scale=staged[:, TAB_COL : TAB_COL + QUART],
-                start=(repeat == 0), stop=(repeat == WARM_PASSES - 1),
+                y[1, 1][:], lhsT=w4_codes(0, 0), lhsT_scale=picked[:, 0:P],
+                rhs=w4[:].bitcast(FP4X4), rhs_scale=picked[:, 0:HALF], start=True, stop=True,
             )
 
         def y_wb4(u, h, first, count):
@@ -221,7 +202,7 @@ def tile_list_xcross_res_none_kernel(
         x_picked = {}
 
         def gather_x(u, h):
-            x_picked[u, h] = shared([P, HALF], F32, f"x_picked{u}{h}", AT_H + 2 * 2 * PACK * HALF * u)
+            x_picked[u, h] = own([P, HALF], F32, f"x_picked{u}{h}")
             nc.vector.tensor_copy(x_picked[u, h][:], x0[u][:].indirect(picks(h * HALF, HALF)))
 
         def store(u, h, first, res):
@@ -241,15 +222,13 @@ def tile_list_xcross_res_none_kernel(
             store(u, h, 0, res)
 
         up_bf = own([P, N * PACK], BF16, "up_bf")
-        nc.scalar.copy(up_bf[:].rearrange("p (n t) -> p n t", t=PACK), up_raw[:].rearrange("p t n -> p n t"))
-        for u in range(2):
-            y_wb4(u, 0, 0, QUART)
-        h_bf = [shared([P, HALF * PACK], BF16, f"h_bf{h}", AT_H + 2 * PACK * HALF * h) for h in range(2)]
+        nc.vector.tensor_copy(up_bf[:].rearrange("p (n t) -> p n t", t=PACK), up_raw[:].rearrange("p t n -> p n t"))
+        h_bf = [own([P, HALF * PACK], BF16, f"h_bf{h}") for h in range(2)]
+        y_wb4(0, 0, 0, HALF)
         down(0, h_bf[0], range(4))
         up_q = quantise(up_bf, "up")
         h_q_first = quantise(h_bf[0], "h_first")
         gather_x(0, 1)
-        y_wb4(0, 0, QUART, QUART)
         y_wb8(0, 0)
         down(1, h_bf[1], range(1))
         y_up(0, 0, up_q, h_q_first)
@@ -257,14 +236,34 @@ def tile_list_xcross_res_none_kernel(
         down(1, h_bf[1], range(1, 4))
         gather_x(1, 1)
         h_q_second = quantise(h_bf[1], "h_second")
-        y_wb4(1, 0, QUART, QUART)
+        y_wb4(1, 0, 0, HALF)
         y_wb8(1, 0)
         y_up(1, 0, up_q, h_q_first)
         finish_fused(1, 0)
-        for u in (1, 0):
-            y_wb4(u, 1, 0, HALF)
-            y_wb8(u, 1)
-            y_up(u, 1, up_q, h_q_second)
+        y_wb4(1, 1, 0, HALF)
+        y_wb8(1, 1)
+        y_up(1, 1, up_q, h_q_second)
         finish(1, 1, 0, HALF)
-        for piece in range(2):
-            finish(0, 1, piece * QUART, QUART)
+        for first in range(0, HALF, QUART):
+            piece = hbanks.tile([P, QUART], F32, name="hbank")
+            for a in range(PASSES):
+                codes, scales = v_operand(1, a, first, QUART)
+                nc.tensor.matmul_mx(
+                    piece[:], lhsT=w4_codes(a, 0), lhsT_scale=w_scales(a, W4_COL),
+                    rhs=codes, rhs_scale=scales, start=(a == 0), stop=False,
+                )
+            for a in range(PASSES):
+                for c in range(0, QUART, BLOCK):
+                    codes, scales = v_operand(1, a, first + c, BLOCK)
+                    nc.tensor.matmul_mx(
+                        piece[:, c : c + BLOCK], lhsT=w8[:, a, 0:P].bitcast(FP8X4), lhsT_scale=w_scales(a, W8_COL),
+                        rhs=codes, rhs_scale=scales, start=False, stop=False,
+                    )
+            cols = slice(first, first + QUART)
+            nc.tensor.matmul_mx(
+                piece[:], lhsT=up_q[0][:, 0:P].bitcast(FP8X4), lhsT_scale=up_q[1][:, 0:P],
+                rhs=h_q_second[0][:, cols].bitcast(FP8X4), rhs_scale=h_q_second[1][:, cols], start=False, stop=True,
+            )
+            res = own([P, QUART], F32, f"res01_{first}")
+            nc.vector.scalar_tensor_tensor(res[:], piece[:], bias1[:, 0:1], x_picked[0, 1][:, cols], ADD, MULT)
+            store(0, 1, first, res)

@@ -36,6 +36,7 @@ AT_X0 = AT_W8 + 4 * PASSES * N
 AT_BIAS = AT_X0 + 4 * T
 AT_X1 = AT_BIAS + 64
 AT_DN = AT_X1 + 4 * T
+AT_H0 = AT_DN + 4 * PASSES * R
 
 
 def tile_list_xcross_res_none_kernel(
@@ -57,10 +58,12 @@ def tile_list_xcross_res_none_kernel(
         def load_scale_rows(queue, dst, scales):
             queue.dma_start(dst.bitcast(I32), scales.bitcast(I32).rearrange("a q n -> q a n"))
 
-        def spread(plane, rows):
+        def spread(plane, rows, first, count):
             for quad in (0, 2, 1, 3):
                 nc.sync.dma_start(
-                    plane[32 * quad : 32 * quad + 4, :].bitcast(I32),
+                    plane[32 * quad : 32 * quad + 4, :].bitcast(I32).rearrange("p (a c) -> p a c", a=PASSES)[
+                        :, :, first // 4 : (first + count) // 4
+                    ],
                     rows[ROW0 + 8 * quad : ROW0 + 8 * quad + 8, :].bitcast(I32),
                 )
 
@@ -95,19 +98,21 @@ def tile_list_xcross_res_none_kernel(
             w_rows[:, DN_COL : DN_COL + R].rearrange("p (t m) -> p t m", t=PACK),
             dn_rows[:].rearrange("p (m t) -> p t m", t=PACK),
         )
-        spread(w_plane, w_rows)
+        spread(w_plane, w_rows, 0, W_COLS)
         dn_raw = shared([P, PASSES, R], I32, "dn_raw", AT_DN)
         nc.sync.dma_start(dn_raw[:], dn_words.rearrange("a p n c -> p a (n c)").bitcast(I32))
-        picked = own([P, J], U8, "picked")
-        nc.vector.tensor_copy(picked[:], tab_rows.indirect(entries[:]))
-        spread(tab_plane, picked)
+        picked = [own([P, HALF], U8, f"picked{h}") for h in range(2)]
+        for h in range(2):
+            nc.vector.tensor_copy(picked[h][:], tab_rows.indirect(picks(h * HALF, HALF)))
+        spread(tab_plane, picked[0], 0, HALF)
 
         up_raw = shared([P, PACK, N], F32, "up_raw", AT_UP)
         nc.sync.dma_start(up_raw[:], upw.rearrange("(p t) n -> p t n", t=PACK))
-        w8 = shared([P, PASSES, N], I32, "w8", AT_W8)
-        nc.sync.dma_start(w8[:], wb8_words.rearrange("a p n c -> p a (n c)").bitcast(I32))
         x0 = [shared([P, T], F32, "x0_first", AT_X0), shared([P, T], F32, "x0_second", AT_X1)]
         nc.sync.dma_start(x0[0][:], x0T[0:P, :])
+        spread(tab_plane, picked[1], HALF, HALF)
+        w8 = shared([P, PASSES, N], I32, "w8", AT_W8)
+        nc.sync.dma_start(w8[:], wb8_words.rearrange("a p n c -> p a (n c)").bitcast(I32))
         bias = shared([P, N // P], F32, "bias", AT_BIAS)
         with nc.allow_non_contiguous_dma(reason="one value of b to a partition and output tile"):
             nc.sync.dma_start(bias[:], b.rearrange("(u p) -> p u", p=P))
@@ -150,8 +155,8 @@ def tile_list_xcross_res_none_kernel(
 
         for repeat in range(WARM_PASSES):
             nc.tensor.matmul_mx(
-                y[1, 1][:], lhsT=w4_codes(0, 0), lhsT_scale=picked[:, 0:P],
-                rhs=w4[:].bitcast(FP4X4), rhs_scale=picked[:, 0:HALF], start=True, stop=True,
+                y[1, 1][:], lhsT=w4_codes(0, 0), lhsT_scale=picked[1][:, 0:P],
+                rhs=w4[:].bitcast(FP4X4), rhs_scale=picked[1][:], start=True, stop=True,
             )
 
         def y_wb4(u, h, first, count):
@@ -202,7 +207,7 @@ def tile_list_xcross_res_none_kernel(
         x_picked = {}
 
         def gather_x(u, h):
-            x_picked[u, h] = own([P, HALF], F32, f"x_picked{u}{h}")
+            x_picked[u, h] = shared([P, HALF], F32, f"x_picked{u}{h}", AT_H0 + 4 * HALF * h * (2 + u))
             nc.vector.tensor_copy(x_picked[u, h][:], x0[u][:].indirect(picks(h * HALF, HALF)))
 
         def store(u, h, first, res):
@@ -222,21 +227,25 @@ def tile_list_xcross_res_none_kernel(
             store(u, h, 0, res)
 
         up_bf = own([P, N * PACK], BF16, "up_bf")
-        nc.vector.tensor_copy(up_bf[:].rearrange("p (n t) -> p n t", t=PACK), up_raw[:].rearrange("p t n -> p n t"))
-        h_bf = [own([P, HALF * PACK], BF16, f"h_bf{h}") for h in range(2)]
-        y_wb4(0, 0, 0, HALF)
+        nc.scalar.copy(up_bf[:].rearrange("p (n t) -> p n t", t=PACK), up_raw[:].rearrange("p t n -> p n t"))
+        h_bf = [shared([P, HALF * PACK], BF16, "h_bf0", AT_H0), own([P, HALF * PACK], BF16, "h_bf1")]
+        for u in range(2):
+            y_wb4(u, 0, 0, QUART)
+        y_wb4(0, 0, QUART, QUART)
         down(0, h_bf[0], range(4))
         up_q = quantise(up_bf, "up")
         h_q_first = quantise(h_bf[0], "h_first")
         gather_x(0, 1)
-        y_wb8(0, 0)
         down(1, h_bf[1], range(1))
+        y_wb8(0, 0)
+        down(1, h_bf[1], range(1, 2))
         y_up(0, 0, up_q, h_q_first)
-        finish_fused(0, 0)
-        down(1, h_bf[1], range(1, 4))
+        gather_x(0, 0)
+        finish(0, 0, 0, HALF)
+        down(1, h_bf[1], range(2, 4))
         gather_x(1, 1)
         h_q_second = quantise(h_bf[1], "h_second")
-        y_wb4(1, 0, 0, HALF)
+        y_wb4(1, 0, QUART, QUART)
         y_wb8(1, 0)
         y_up(1, 0, up_q, h_q_first)
         finish_fused(1, 0)

@@ -67,20 +67,20 @@ def tile_list_xcross_res_none_kernel(
                     rows[ROW0 + 8 * quad : ROW0 + 8 * quad + 8, :].bitcast(I32),
                 )
 
+        dn_rows = shared([P, R], U8, "dn_rows", AT_DN)
+        load_scale_rows(nc.sync, dn_rows[ROW0:P, :], dn_scales)
         entries = held.tile([P, J // 16], U16, name="entries")
         nc.sync.dma_start(entries[:], offs)
         tab_rows = shared([P, AT_X1 + 64], U8, "tab_rows", AT_TAB_SCALES)[:, 0:T]
         load_scale_rows(nc.sync, tab_rows[ROW0:P, :], tab_scales)
-        dn_rows = shared([P, R], U8, "dn_rows", AT_DN)
-        load_scale_rows(nc.scalar, dn_rows[ROW0:P, :], dn_scales)
-        w_rows = own([P, W_COLS], U8, "w_rows")
-        load_scale_rows(nc.scalar, w_rows[ROW0:P, W4_COL : W4_COL + N], wb4_scales)
-        load_scale_rows(nc.scalar, w_rows[ROW0:P, W8_COL : W8_COL + N], wb8_scales)
         w4 = own([P, PASSES * 2 * N], U8, "w4")
         nc.sync.dma_start(
             w4[:].bitcast(I32).rearrange("p (a c) -> p a c", a=PASSES),
             wb4_words.bitcast(I32).rearrange("a p c -> p a c"),
         )
+        w_rows = own([P, W_COLS], U8, "w_rows")
+        load_scale_rows(nc.sync, w_rows[ROW0:P, W4_COL : W4_COL + N], wb4_scales)
+        load_scale_rows(nc.sync, w_rows[ROW0:P, W8_COL : W8_COL + N], wb8_scales)
         tab = own([P, T], U32, "tab")
         nc.sync.dma_start(tab[:].bitcast(I32), tab_words[0].rearrange("p t c -> p (t c)").bitcast(I32))
 

@@ -69,10 +69,10 @@ def tile_list_xcross_res_none_kernel(
 
         dn_rows = shared([P, R], U8, "dn_rows", AT_DN)
         load_scale_rows(nc.sync, dn_rows[ROW0:P, :], dn_scales)
-        entries = held.tile([P, J // 16], U16, name="entries")
-        nc.sync.dma_start(entries[:], offs)
         tab_rows = shared([P, AT_X1 + 64], U8, "tab_rows", AT_TAB_SCALES)[:, 0:T]
         load_scale_rows(nc.sync, tab_rows[ROW0:P, :], tab_scales)
+        entries = held.tile([P, J // 16], U16, name="entries")
+        nc.sync.dma_start(entries[:], offs)
         w4 = own([P, PASSES * 2 * N], U8, "w4")
         nc.sync.dma_start(
             w4[:].bitcast(I32).rearrange("p (a c) -> p a c", a=PASSES),
@@ -207,7 +207,7 @@ def tile_list_xcross_res_none_kernel(
         x_picked = {}
 
         def gather_x(u, h):
-            x_picked[u, h] = shared([P, HALF], F32, f"x_picked{u}{h}", AT_H0 + 4 * HALF * h * (2 + u))
+            x_picked[u, h] = shared([P, HALF], F32, f"x_picked{u}{h}", AT_H0 + 4 * HALF * (2 - 2 * h + 3 * u))
             nc.vector.tensor_copy(x_picked[u, h][:], x0[u][:].indirect(picks(h * HALF, HALF)))
 
         def store(u, h, first, res):
@@ -234,13 +234,13 @@ def tile_list_xcross_res_none_kernel(
         y_wb4(0, 0, QUART, QUART)
         down(0, h_bf[0], range(4))
         up_q = quantise(up_bf, "up")
+        gather_x(0, 0)
         h_q_first = quantise(h_bf[0], "h_first")
         gather_x(0, 1)
         down(1, h_bf[1], range(1))
         y_wb8(0, 0)
         down(1, h_bf[1], range(1, 2))
         y_up(0, 0, up_q, h_q_first)
-        gather_x(0, 0)
         finish(0, 0, 0, HALF)
         down(1, h_bf[1], range(2, 4))
         gather_x(1, 1)

@@ -220,11 +220,12 @@ def tile_list_xcross_res_none_kernel(
             store(u, h, first, res)
 
         def finish_fused(u, h):
-            factor = own([P, HALF], F32, f"factor{u}{h}")
-            nc.scalar.activation(factor[:], y[u, h][:], IDENTITY, bias=bias1[:, u : u + 1])
-            res = own([P, HALF], F32, f"res{u}{h}")
-            nc.vector.tensor_tensor(res[:], x0[u][:].indirect(picks(h * HALF, HALF)), factor[:], MULT)
-            store(u, h, 0, res)
+            for first in range(0, HALF, QUART):
+                factor = own([P, QUART], F32, f"factor{u}{h}_{first}")
+                nc.scalar.activation(factor[:], y[u, h][:, first : first + QUART], IDENTITY, bias=bias1[:, u : u + 1])
+                res = own([P, QUART], F32, f"res{u}{h}_{first}")
+                nc.vector.tensor_tensor(res[:], x0[u][:].indirect(picks(h * HALF + first, QUART)), factor[:], MULT)
+                store(u, h, first, res)
 
         up_bf = own([P, N * PACK], BF16, "up_bf")
         nc.scalar.copy(up_bf[:].rearrange("p (n t) -> p n t", t=PACK), up_raw[:].rearrange("p t n -> p n t"))
@@ -252,7 +253,8 @@ def tile_list_xcross_res_none_kernel(
         y_wb4(1, 1, 0, HALF)
         y_wb8(1, 1)
         y_up(1, 1, up_q, h_q_second)
-        finish(1, 1, 0, HALF)
+        for first in range(0, HALF, QUART):
+            finish(1, 1, first, QUART)
         for first in range(0, HALF, QUART):
             piece = hbanks.tile([P, QUART], F32, name="hbank")
             for a in range(PASSES):

@@ -24,7 +24,7 @@ HALF = J // 2
 QUART = J // 4
 BLOCK = HALF // PACK
 ROW0 = P - 16 * PASSES
-H_BANKS = 5
+H_BANKS = 6
 WARM_PASSES = 3
 
 DN_COL, W4_COL, W8_COL, W_COLS = 0, R, R + N, R + 2 * N
@@ -34,9 +34,10 @@ AT_UP = 0
 AT_W8 = AT_UP + 4 * PACK * N
 AT_X0 = AT_W8 + 4 * PASSES * N
 AT_BIAS = AT_X0 + 4 * T
-AT_X1 = AT_BIAS + 64
+AT_X1 = AT_BIAS + 256
 AT_DN = AT_X1 + 4 * T
 AT_H0 = AT_DN + 4 * PASSES * R
+AT_H3 = AT_H0 + 16 * HALF
 
 
 def tile_list_xcross_res_none_kernel(
@@ -50,10 +51,10 @@ def tile_list_xcross_res_none_kernel(
         hbanks = ctx.enter_context(tc.psum_pool(name="hbanks", bufs=H_BANKS))
 
         def own(shape, dtype, name):
-            return held.tile(shape, dtype, name=name, align_bytes=64)
+            return held.tile(shape, dtype, name=name, align_bytes=256)
 
         def shared(shape, dtype, name, offset):
-            return reused.tile(shape, dtype, name=name, offset=offset, align_bytes=64)
+            return reused.tile(shape, dtype, name=name, offset=offset, align_bytes=256)
 
         def load_scale_rows(queue, dst, scales):
             queue.dma_start(dst.bitcast(I32), scales.bitcast(I32).rearrange("a q n -> q a n"))
@@ -151,11 +152,11 @@ def tile_list_xcross_res_none_kernel(
         def w4_codes(a, u):
             return w4[:, 2 * (a * N + u * P) : 2 * (a * N + (u + 1) * P)].bitcast(FP4X4)
 
-        y = {(u, h): ybanks.tile([P, HALF], F32, name=f"y{u}{h}") for u, h in ((0, 0), (1, 0), (1, 1))}
+        y = {(u, h): ybanks.tile([P, HALF], F32, name=f"y{u}{h}") for u, h in ((0, 0), (1, 0))}
 
         for repeat in range(WARM_PASSES):
             nc.tensor.matmul_mx(
-                y[1, 1][:], lhsT=w4_codes(0, 0), lhsT_scale=picked[1][:, 0:P],
+                y[1, 0][:], lhsT=w4_codes(0, 0), lhsT_scale=picked[1][:, 0:P],
                 rhs=w4[:].bitcast(FP4X4), rhs_scale=picked[1][:], start=True, stop=True,
             )
 
@@ -182,7 +183,7 @@ def tile_list_xcross_res_none_kernel(
                 rhs=h_q[0][:].bitcast(FP8X4), rhs_scale=h_q[1][:], start=False, stop=True,
             )
 
-        def down(h, h_bf, blocks):
+        def down(h, h_bf, blocks, base=0):
             for c in blocks:
                 bank = hbanks.tile([P, PACK, BLOCK], F32, name="hbank")
                 for t in range(PACK):
@@ -194,7 +195,7 @@ def tile_list_xcross_res_none_kernel(
                             start=(a == 0), stop=(a == PASSES - 1),
                         )
                 nc.scalar.copy(
-                    h_bf[:, c * PACK * BLOCK : (c + 1) * PACK * BLOCK].rearrange("p (j t) -> p j t", t=PACK),
+                    h_bf[:, (c - base) * PACK * BLOCK : (c - base + 1) * PACK * BLOCK].rearrange("p (j t) -> p j t", t=PACK),
                     bank[:].rearrange("p t j -> p j t"),
                 )
 
@@ -228,53 +229,68 @@ def tile_list_xcross_res_none_kernel(
                 store(u, h, first, res)
 
         up_bf = own([P, N * PACK], BF16, "up_bf")
-        nc.scalar.copy(up_bf[:].rearrange("p (n t) -> p n t", t=PACK), up_raw[:].rearrange("p t n -> p n t"))
-        h_bf = [shared([P, HALF * PACK], BF16, "h_bf0", AT_H0), own([P, HALF * PACK], BF16, "h_bf1")]
-        for u in range(2):
-            y_wb4(u, 0, 0, QUART)
-        y_wb4(0, 0, QUART, QUART)
-        down(0, h_bf[0], range(4))
-        up_q = quantise(up_bf, "up")
-        gather_x(0, 0)
-        h_q_first = quantise(h_bf[0], "h_first")
-        gather_x(0, 1)
-        down(1, h_bf[1], range(1))
-        y_wb8(0, 0)
-        down(1, h_bf[1], range(1, 2))
-        y_up(0, 0, up_q, h_q_first)
-        finish(0, 0, 0, HALF)
-        down(1, h_bf[1], range(2, 4))
-        gather_x(1, 1)
-        h_q_second = quantise(h_bf[1], "h_second")
-        y_wb4(1, 0, QUART, QUART)
-        y_wb8(1, 0)
-        y_up(1, 0, up_q, h_q_first)
-        finish_fused(1, 0)
-        y_wb4(1, 1, 0, HALF)
-        y_wb8(1, 1)
-        y_up(1, 1, up_q, h_q_second)
-        for first in range(0, HALF, QUART):
-            finish(1, 1, first, QUART)
-        for first in range(0, HALF, QUART):
-            piece = hbanks.tile([P, QUART], F32, name="hbank")
+        nc.scalar.copy(
+            up_bf[:].rearrange("p (c i t) -> p c t i", t=PACK, i=4),
+            up_raw[:].rearrange("p t (c i) -> p c t i", i=4),
+        )
+        def piece(u, first, h_q):
+            bank = hbanks.tile([P, QUART], F32, name="hbank")
             for a in range(PASSES):
                 codes, scales = v_operand(1, a, first, QUART)
                 nc.tensor.matmul_mx(
-                    piece[:], lhsT=w4_codes(a, 0), lhsT_scale=w_scales(a, W4_COL),
+                    bank[:], lhsT=w4_codes(a, u), lhsT_scale=w_scales(a, W4_COL + u * P),
                     rhs=codes, rhs_scale=scales, start=(a == 0), stop=False,
                 )
             for a in range(PASSES):
                 for c in range(0, QUART, BLOCK):
                     codes, scales = v_operand(1, a, first + c, BLOCK)
                     nc.tensor.matmul_mx(
-                        piece[:, c : c + BLOCK], lhsT=w8[:, a, 0:P].bitcast(FP8X4), lhsT_scale=w_scales(a, W8_COL),
-                        rhs=codes, rhs_scale=scales, start=False, stop=False,
+                        bank[:, c : c + BLOCK], lhsT=w8[:, a, u * P : (u + 1) * P].bitcast(FP8X4),
+                        lhsT_scale=w_scales(a, W8_COL + u * P), rhs=codes, rhs_scale=scales, start=False, stop=False,
                     )
-            cols = slice(first, first + QUART)
+            cols = slice(u * P, (u + 1) * P)
             nc.tensor.matmul_mx(
-                piece[:], lhsT=up_q[0][:, 0:P].bitcast(FP8X4), lhsT_scale=up_q[1][:, 0:P],
-                rhs=h_q_second[0][:, cols].bitcast(FP8X4), rhs_scale=h_q_second[1][:, cols], start=False, stop=True,
+                bank[:], lhsT=up_q[0][:, cols].bitcast(FP8X4), lhsT_scale=up_q[1][:, cols],
+                rhs=h_q[0][:].bitcast(FP8X4), rhs_scale=h_q[1][:], start=False, stop=True,
             )
-            res = own([P, QUART], F32, f"res01_{first}")
-            nc.vector.scalar_tensor_tensor(res[:], piece[:], bias1[:, 0:1], x_picked[0, 1][:, cols], ADD, MULT)
-            store(0, 1, first, res)
+            return bank
+
+        def piece_fused(u, bank, res):
+            factor = own([P, QUART], F32, f"factor{u}_third")
+            nc.scalar.activation(factor[:], bank[:], IDENTITY, bias=bias1[:, u : u + 1])
+            nc.vector.tensor_tensor(res[:], x0[u][:].indirect(picks(HALF, QUART)), factor[:], MULT)
+            store(u, 1, 0, res)
+
+        def piece_plain(u, bank, x_last):
+            res = own([P, QUART], F32, f"res{u}_last")
+            nc.vector.scalar_tensor_tensor(res[:], bank[:], bias1[:, u : u + 1], x_last[:], ADD, MULT)
+            store(u, 1, QUART, res)
+
+        h_bf0 = shared([P, HALF * PACK], BF16, "h_bf0", AT_H0)
+        h_bf2 = own([P, QUART * PACK], BF16, "h_bf2")
+        h_bf3 = shared([P, QUART * PACK], BF16, "h_bf3", AT_H3)
+        for u in range(2):
+            y_wb4(u, 0, 0, QUART)
+        for u in range(2):
+            y_wb4(u, 0, QUART, QUART)
+        down(0, h_bf0, range(4))
+        up_q = quantise(up_bf, "up")
+        gather_x(0, 0)
+        h_q_first = quantise(h_bf0, "h_first")
+        x_last = [shared([P, QUART], F32, "x_last0", AT_H0), own([P, QUART], F32, "x_last1")]
+        nc.vector.tensor_copy(x_last[0][:], x0[0][:].indirect(picks(HALF + QUART, QUART)))
+        down(1, h_bf2, range(2))
+        h_q_third = quantise(h_bf2, "h_third")
+        y_wb8(0, 0)
+        y_up(0, 0, up_q, h_q_first)
+        finish(0, 0, 0, HALF)
+        nc.vector.tensor_copy(x_last[1][:], x0[1][:].indirect(picks(HALF + QUART, QUART)))
+        y_wb8(1, 0)
+        y_up(1, 0, up_q, h_q_first)
+        finish_fused(1, 0)
+        down(1, h_bf3, range(2, 4), 2)
+        h_q_last = quantise(h_bf3, "h_last")
+        piece_fused(1, piece(1, 0, h_q_third), own([P, QUART], F32, "res1_third"))
+        piece_fused(0, piece(0, 0, h_q_third), shared([P, QUART], F32, "res0_third", AT_H3))
+        for u in (1, 0):
+            piece_plain(u, piece(u, QUART, h_q_last), x_last[u])

@@ -24,20 +24,15 @@ HALF = J // 2
 QUART = J // 4
 BLOCK = HALF // PACK
 ROW0 = P - 16 * PASSES
-H_BANKS = 6
+BANK_BYTES = 2048
 WARM_PASSES = 3
 
-DN_COL, W4_COL, W8_COL, W_COLS = 0, R, R + N, R + 2 * N
+DN_COL, W4_COL, W8_COL, TAB_COL, STAGE_COLS = 0, R, R + N, R + 2 * N, R + 2 * N + HALF
 
-AT_TAB_SCALES = 0
-AT_UP = 0
-AT_W8 = AT_UP + 4 * PACK * N
-AT_X0 = AT_W8 + 4 * PASSES * N
-AT_BIAS = AT_X0 + 4 * T
-AT_X1 = AT_BIAS + 256
-AT_DN = AT_X1 + 4 * T
-AT_H0 = AT_DN + 4 * PASSES * R
-AT_H3 = AT_H0 + 16 * HALF
+AT_PICKED = 0
+AT_PAIRS = AT_PICKED + HALF
+AT_UP_BF = AT_PAIRS + 4 * HALF
+AT_H2 = AT_UP_BF + 2 * PACK * N
 
 
 def tile_list_xcross_res_none_kernel(
@@ -47,250 +42,259 @@ def tile_list_xcross_res_none_kernel(
     with ExitStack() as ctx:
         held = ctx.enter_context(tc.tile_pool(name="held", bufs=1))
         reused = ctx.enter_context(tc.tile_pool(name="reused", bufs=1))
-        ybanks = ctx.enter_context(tc.psum_pool(name="ybanks", bufs=1))
-        hbanks = ctx.enter_context(tc.psum_pool(name="hbanks", bufs=H_BANKS))
+        psum = ctx.enter_context(tc.psum_pool(name="psum", bufs=1))
 
         def own(shape, dtype, name):
             return held.tile(shape, dtype, name=name, align_bytes=256)
 
-        def shared(shape, dtype, name, offset):
-            return reused.tile(shape, dtype, name=name, offset=offset, align_bytes=256)
+        def shared(shape, dtype, name, offset, align=256):
+            return reused.tile(shape, dtype, name=name, offset=offset, align_bytes=align)
+
+        def in_bank(shape, name, bank):
+            return psum.tile(shape, F32, name=name, offset=bank * BANK_BYTES)
 
         def load_scale_rows(queue, dst, scales):
             queue.dma_start(dst.bitcast(I32), scales.bitcast(I32).rearrange("a q n -> q a n"))
 
-        def spread(plane, rows, first, count):
+        def spread(plane, rows):
             for quad in (0, 2, 1, 3):
                 nc.sync.dma_start(
-                    plane[32 * quad : 32 * quad + 4, :].bitcast(I32).rearrange("p (a c) -> p a c", a=PASSES)[
-                        :, :, first // 4 : (first + count) // 4
-                    ],
+                    plane[32 * quad : 32 * quad + 4, :].bitcast(I32).rearrange("p (a c) -> p a c", a=PASSES),
                     rows[ROW0 + 8 * quad : ROW0 + 8 * quad + 8, :].bitcast(I32),
                 )
 
-        dn_rows = shared([P, R], U8, "dn_rows", AT_DN)
-        load_scale_rows(nc.sync, dn_rows[ROW0:P, :], dn_scales)
-        tab_rows = shared([P, AT_X1 + 64], U8, "tab_rows", AT_TAB_SCALES)[:, 0:T]
+        def load_words(dst, words):
+            nc.sync.dma_start(dst[:].bitcast(I32), words.rearrange("p n c -> p (n c)").bitcast(I32))
+
+        bias = own([P, N // P], F32, "bias")
+        with nc.allow_non_contiguous_dma(reason="one value of b to a partition and output tile"):
+            nc.gpsimd.dma_start(bias[:], b.rearrange("(u p) -> p u", p=P))
+        bias1 = own([P, N // P], F32, "bias1")
+        nc.scalar.activation(bias1[:], bias[:], IDENTITY, bias=1.0)
+
+        dn_rows = own([P, R], U8, "dn_rows")
+        load_scale_rows(nc.scalar, dn_rows[ROW0:P, :], dn_scales)
+        tab_rows = own([P, T], U8, "tab_rows")
         load_scale_rows(nc.sync, tab_rows[ROW0:P, :], tab_scales)
         entries = held.tile([P, J // 16], U16, name="entries")
         nc.sync.dma_start(entries[:], offs)
+        stage = own([P, STAGE_COLS], U8, "stage")
+        load_scale_rows(nc.scalar, stage[ROW0:P, W4_COL : W4_COL + N], wb4_scales)
+        load_scale_rows(nc.sync, stage[ROW0:P, W8_COL : W8_COL + N], wb8_scales)
+        tab = own([P, T], U32, "tab")
+        load_words(tab, tab_words[0])
         w4 = own([P, PASSES * 2 * N], U8, "w4")
         nc.sync.dma_start(
             w4[:].bitcast(I32).rearrange("p (a c) -> p a c", a=PASSES),
             wb4_words.bitcast(I32).rearrange("a p c -> p a c"),
         )
-        w_rows = own([P, W_COLS], U8, "w_rows")
-        load_scale_rows(nc.sync, w_rows[ROW0:P, W4_COL : W4_COL + N], wb4_scales)
-        load_scale_rows(nc.sync, w_rows[ROW0:P, W8_COL : W8_COL + N], wb8_scales)
-        tab = own([P, T], U32, "tab")
-        nc.sync.dma_start(tab[:].bitcast(I32), tab_words[0].rearrange("p t c -> p (t c)").bitcast(I32))
+        dn_raw = [own([P, R], U32, f"dn_raw{a}") for a in range(PASSES)]
+        load_words(dn_raw[0], dn_words[0])
 
-        nc.vector.memset(tab_rows[0:ROW0, :].bitcast(I32), 0)
         nc.vector.memset(dn_rows[0:ROW0, :].bitcast(I32), 0)
-        w_plane = own([P, PASSES * W_COLS], U8, "w_plane")
-        nc.vector.memset(w_plane[:].bitcast(I32), 0)
-        tab_plane = own([P, PASSES * J], U8, "tab_plane")
-        nc.vector.memset(tab_plane[:].bitcast(I32), 0)
+        nc.vector.memset(tab_rows[0:ROW0, :].bitcast(I32), 0)
+        planes = [own([P, PASSES * STAGE_COLS], U8, "plane0"), own([P, PASSES * HALF], U8, "plane1")]
+        for plane in planes:
+            nc.vector.memset(plane[:].bitcast(I32), 0)
 
         def picks(first, count):
             return entries[:, first // 16 : (first + count) // 16]
 
         nc.vector.tensor_copy(
-            w_rows[:, DN_COL : DN_COL + R].rearrange("p (t m) -> p t m", t=PACK),
+            stage[:, DN_COL : DN_COL + R].rearrange("p (t m) -> p t m", t=PACK),
             dn_rows[:].rearrange("p (m t) -> p t m", t=PACK),
         )
-        spread(w_plane, w_rows, 0, W_COLS)
-        dn_raw = shared([P, PASSES, R], I32, "dn_raw", AT_DN)
-        nc.sync.dma_start(dn_raw[:], dn_words.rearrange("a p n c -> p a (n c)").bitcast(I32))
-        picked = [own([P, HALF], U8, f"picked{h}") for h in range(2)]
-        for h in range(2):
-            nc.vector.tensor_copy(picked[h][:], tab_rows.indirect(picks(h * HALF, HALF)))
-        spread(tab_plane, picked[0], 0, HALF)
-
-        up_raw = shared([P, PACK, N], F32, "up_raw", AT_UP)
-        nc.sync.dma_start(up_raw[:], upw.rearrange("(p t) n -> p t n", t=PACK))
-        x0 = [shared([P, T], F32, "x0_first", AT_X0), shared([P, T], F32, "x0_second", AT_X1)]
+        early = [shared([P, QUART], U8, "picked_a", AT_PICKED), own([P, QUART], U8, "picked_b")]
+        for c in range(2):
+            nc.vector.tensor_copy(early[c][:], tab_rows[:].indirect(picks(c * QUART, QUART)))
+        for c in range(2):
+            col = TAB_COL + c * QUART
+            nc.vector.tensor_copy(stage[ROW0:P, col : col + QUART].bitcast(I32), early[c][ROW0:P, :].bitcast(I32))
+        spread(planes[0], stage[:])
+        load_words(dn_raw[1], dn_words[1])
+        late = shared([P, HALF], U8, "picked_late", AT_PICKED)
+        nc.vector.tensor_copy(late[:], tab_rows[:].indirect(picks(HALF, HALF)))
+        x0 = [own([P, T], F32, f"x0_{u}") for u in range(2)]
         nc.sync.dma_start(x0[0][:], x0T[0:P, :])
-        spread(tab_plane, picked[1], HALF, HALF)
-        w8 = shared([P, PASSES, N], I32, "w8", AT_W8)
+        spread(planes[1], late[:])
+        up_raw = own([P, PACK, N], F32, "up_raw")
+        nc.sync.dma_start(up_raw[:], upw.rearrange("(p t) n -> p t n", t=PACK))
+        w8 = own([P, PASSES, N], I32, "w8")
         nc.sync.dma_start(w8[:], wb8_words.rearrange("a p n c -> p a (n c)").bitcast(I32))
-        bias = shared([P, N // P], F32, "bias", AT_BIAS)
-        with nc.allow_non_contiguous_dma(reason="one value of b to a partition and output tile"):
-            nc.sync.dma_start(bias[:], b.rearrange("(u p) -> p u", p=P))
         nc.sync.dma_start(x0[1][:], x0T[P : 2 * P, :])
-        bias1 = own([P, N // P], F32, "bias1")
-        nc.gpsimd.tensor_scalar_add(bias1[:], bias[:], 1.0)
 
         v = [own([P, PASSES * 2 * HALF], U8, f"v{h}") for h in range(2)]
 
-        def gather_words(quarter, pairs):
-            h, first = quarter // 2, quarter % 2 * QUART
-            nc.vector.tensor_copy(pairs[:], tab[:].indirect(picks(quarter * QUART, QUART)))
+        def gather_words(first, count, at):
+            pairs = shared([P, count], U32, f"pairs{first}", at)
+            nc.vector.tensor_copy(pairs[:], tab[:].indirect(picks(first, count)))
+            return pairs
+
+        def part(first, pairs):
+            cols = slice(first % HALF, first % HALF + pairs.shape[1])
             nc.vector.tensor_copy(
-                v[h][:].bitcast(U16).rearrange("p (a j) -> p a j", a=PASSES)[:, :, first : first + QUART],
+                v[first // HALF][:].bitcast(U16).rearrange("p (a j) -> p a j", a=PASSES)[:, :, cols],
                 pairs[:].bitcast(U16).rearrange("p (j a) -> p a j", a=PASSES),
             )
 
-        for quarter in range(2):
-            gather_words(quarter, own([P, QUART], U32, f"pairs{quarter}"))
-        dn = own([P, PASSES, R], I32, "dn")
-        nc.vector.tensor_copy(
-            dn[:].rearrange("p a (t m i) -> p a m t i", t=PACK, i=4),
-            dn_raw[:].rearrange("p a (m i t) -> p a m t i", t=PACK, i=4),
-        )
-        for quarter in range(2, 4):
-            gather_words(quarter, shared([P, QUART], U32, f"pairs{quarter}", AT_DN + 4 * QUART * quarter))
+        for first, count in ((0, BLOCK), (QUART, BLOCK), (HALF, QUART)):
+            both = [gather_words(first + c * count, count, AT_PAIRS + 4 * QUART * c) for c in range(2)]
+            for c in range(2):
+                part(first + c * count, both[c])
+
+        dn = [own([P, R], U32, f"dn{a}") for a in range(PASSES)]
+        for a in range(PASSES):
+            nc.scalar.copy(
+                dn[a][:].rearrange("p (t m i) -> p m t i", t=PACK, i=4),
+                dn_raw[a][:].rearrange("p (m i t) -> p m t i", t=PACK, i=4),
+            )
 
         def v_operand(h, a, first, count):
             codes = v[h][:, 2 * (a * HALF + first) : 2 * (a * HALF + first + count)].bitcast(FP4X4)
-            col = a * J + h * HALF + first
-            return codes, tab_plane[:, col : col + count]
+            col = a * STAGE_COLS + TAB_COL + first if h == 0 else a * HALF + first
+            return codes, planes[h][:, col : col + count]
 
         def w_scales(a, col):
-            return w_plane[:, a * W_COLS + col : a * W_COLS + col + P]
+            return planes[0][:, a * STAGE_COLS + col : a * STAGE_COLS + col + P]
 
         def w4_codes(a, u):
             return w4[:, 2 * (a * N + u * P) : 2 * (a * N + (u + 1) * P)].bitcast(FP4X4)
 
-        y = {(u, h): ybanks.tile([P, HALF], F32, name=f"y{u}{h}") for u, h in ((0, 0), (1, 0))}
+        warm = in_bank([P, HALF], "warm", 7)
 
         for repeat in range(WARM_PASSES):
             nc.tensor.matmul_mx(
-                y[1, 0][:], lhsT=w4_codes(0, 0), lhsT_scale=picked[1][:, 0:P],
-                rhs=w4[:].bitcast(FP4X4), rhs_scale=picked[1][:], start=True, stop=True,
+                warm[:], lhsT=tab_rows[:, 0 : 2 * P].bitcast(FP4X4), lhsT_scale=early[1][:, 0:P],
+                rhs=tab_rows[:, 0 : 2 * HALF].bitcast(FP4X4), rhs_scale=tab_rows[:, 0:HALF], start=True, stop=True,
             )
 
-        def y_wb4(u, h, first, count):
+        def y_wb4(dst, u, h, first, opens):
             for a in range(PASSES):
-                codes, scales = v_operand(h, a, first, count)
+                codes, scales = v_operand(h, a, first, dst.shape[1])
                 nc.tensor.matmul_mx(
-                    y[u, h][:, first : first + count], lhsT=w4_codes(a, u), lhsT_scale=w_scales(a, W4_COL + u * P),
-                    rhs=codes, rhs_scale=scales, start=(a == 0 and first == 0), stop=False,
+                    dst, lhsT=w4_codes(a, u), lhsT_scale=w_scales(a, W4_COL + u * P),
+                    rhs=codes, rhs_scale=scales, start=(opens and a == 0), stop=False,
                 )
 
-        def y_wb8(u, h):
+        def y_wb8(dst, u, h, first):
             for a in range(PASSES):
-                codes, scales = v_operand(h, a, 0, HALF)
+                codes, scales = v_operand(h, a, first, dst.shape[1])
                 nc.tensor.matmul_mx(
-                    y[u, h][:], lhsT=w8[:, a, u * P : (u + 1) * P].bitcast(FP8X4), lhsT_scale=w_scales(a, W8_COL + u * P),
+                    dst, lhsT=w8[:, a, u * P : (u + 1) * P].bitcast(FP8X4), lhsT_scale=w_scales(a, W8_COL + u * P),
                     rhs=codes, rhs_scale=scales, start=False, stop=False,
                 )
 
-        def y_up(u, h, up_q, h_q):
-            cols = slice(u * P, (u + 1) * P)
+        def y_up(dst, u, h_q):
+            rows = slice(u * P, (u + 1) * P)
             nc.tensor.matmul_mx(
-                y[u, h][:], lhsT=up_q[0][:, cols].bitcast(FP8X4), lhsT_scale=up_q[1][:, cols],
+                dst, lhsT=up_q[0][:, rows].bitcast(FP8X4), lhsT_scale=up_q[1][:, rows],
                 rhs=h_q[0][:].bitcast(FP8X4), rhs_scale=h_q[1][:], start=False, stop=True,
             )
 
-        def down(h, h_bf, blocks, base=0):
-            for c in blocks:
-                bank = hbanks.tile([P, PACK, BLOCK], F32, name="hbank")
+        def down_pass(bank, h, c, a, t, start, stop):
+            codes, scales = v_operand(h, a, c * BLOCK, BLOCK)
+            nc.tensor.matmul_mx(
+                bank[:, t, :], lhsT=dn[a][:, t * P : (t + 1) * P].bitcast(FP8X4),
+                lhsT_scale=w_scales(a, DN_COL + t * P), rhs=codes, rhs_scale=scales, start=start, stop=stop,
+            )
+
+        def copy_h(dst, bank):
+            nc.scalar.copy(dst.rearrange("p (j t) -> p j t", t=PACK), bank[:].rearrange("p t j -> p j t"))
+
+        def down(h, c, dst, at):
+            bank = in_bank([P, PACK, BLOCK], f"h{h}{c}", at)
+            for t in range(PACK):
+                for a in range(PASSES):
+                    down_pass(bank, h, c, a, t, a == 0, a == PASSES - 1)
+            copy_h(dst, bank)
+
+        def mx_pair(width, name):
+            return own([P, width], U32, name + "_codes"), own([P, width], U8, name + "_scales")
+
+        def quantise(dst, src):
+            nc.vector.quantize_mx(dst[0][:].bitcast(FP8X4), dst[1][:], src[:])
+            return dst
+
+        def gather_x(dst, u, first):
+            nc.vector.tensor_copy(dst[:], x0[u][:].indirect(picks(first, dst.shape[1])))
+            return dst
+
+        def store(u, first, res):
+            nc.sync.dma_start(out[u * P : (u + 1) * P, first : first + res.shape[1]], res[:])
+
+        def finish(u, first, sums, x_picked):
+            res = own([P, sums.shape[1]], F32, f"res{u}_{first}")
+            nc.vector.scalar_tensor_tensor(res[:], sums, bias1[:, u : u + 1], x_picked, ADD, MULT)
+            store(u, first, res)
+
+        def finish_fused(u, first, sums):
+            count = sums.shape[1]
+            factor = own([P, count], F32, f"factor{u}_{first}")
+            nc.scalar.activation(factor[:], sums, IDENTITY, bias=bias1[:, u : u + 1])
+            res = own([P, count], F32, f"res{u}_{first}")
+            nc.vector.tensor_tensor(res[:], x0[u][:].indirect(picks(first, count)), factor[:], MULT)
+            store(u, first, res)
+
+        def finish_aside(u, first, sums, x_picked):
+            count = sums.shape[1]
+            factor = own([P, count], F32, f"factor{u}_{first}")
+            nc.scalar.activation(factor[:], sums, IDENTITY, bias=bias1[:, u : u + 1])
+            res = own([P, count], F32, f"res{u}_{first}")
+            nc.gpsimd.tensor_tensor(res[:], x_picked, factor[:], MULT)
+            store(u, first, res)
+
+        WIDE = PACK * BLOCK
+        h_bf = [own([P, QUART * PACK], BF16, f"h_bf{c}") for c in range(2)]
+        h_bf += [shared([P, QUART * PACK], BF16, "h_bf2", AT_H2), own([P, QUART * PACK], BF16, "h_bf3")]
+        y = {(u, c): in_bank([P, QUART], f"y{u}{c}", 2 * (1 - u) + c) for u in range(2) for c in range(2)}
+
+        for u in range(2):
+            y_wb4(y[u, 0][:], u, 0, 0, True)
+        banks = [in_bank([P, PACK, BLOCK], f"h0{c}", 4 + c) for c in range(2)]
+        for a in range(PASSES):
+            for c in range(2):
                 for t in range(PACK):
-                    for a in range(PASSES):
-                        codes, scales = v_operand(h, a, c * BLOCK, BLOCK)
-                        nc.tensor.matmul_mx(
-                            bank[:, t, :], lhsT=dn[:, a, t * P : (t + 1) * P].bitcast(FP8X4),
-                            lhsT_scale=w_scales(a, DN_COL + t * P), rhs=codes, rhs_scale=scales,
-                            start=(a == 0), stop=(a == PASSES - 1),
-                        )
-                nc.scalar.copy(
-                    h_bf[:, (c - base) * PACK * BLOCK : (c - base + 1) * PACK * BLOCK].rearrange("p (j t) -> p j t", t=PACK),
-                    bank[:].rearrange("p t j -> p j t"),
-                )
-
-        def quantise(src, name):
-            width = src.shape[1] // PACK
-            codes, scales = own([P, width], U32, name + "_codes"), own([P, width], U8, name + "_scales")
-            nc.vector.quantize_mx(codes[:].bitcast(FP8X4), scales[:], src[:])
-            return codes, scales
-
-        x_picked = {}
-
-        def gather_x(u, h):
-            x_picked[u, h] = shared([P, HALF], F32, f"x_picked{u}{h}", AT_H0 + 4 * HALF * (2 - 2 * h + 3 * u))
-            nc.vector.tensor_copy(x_picked[u, h][:], x0[u][:].indirect(picks(h * HALF, HALF)))
-
-        def store(u, h, first, res):
-            nc.sync.dma_start(out[u * P : (u + 1) * P, h * HALF + first : h * HALF + first + res.shape[1]], res[:])
-
-        def finish(u, h, first, count):
-            res = own([P, count], F32, f"res{u}{h}_{first}")
-            cols = slice(first, first + count)
-            nc.vector.scalar_tensor_tensor(res[:], y[u, h][:, cols], bias1[:, u : u + 1], x_picked[u, h][:, cols], ADD, MULT)
-            store(u, h, first, res)
-
-        def finish_fused(u, h):
-            for first in range(0, HALF, QUART):
-                factor = own([P, QUART], F32, f"factor{u}{h}_{first}")
-                nc.scalar.activation(factor[:], y[u, h][:, first : first + QUART], IDENTITY, bias=bias1[:, u : u + 1])
-                res = own([P, QUART], F32, f"res{u}{h}_{first}")
-                nc.vector.tensor_tensor(res[:], x0[u][:].indirect(picks(h * HALF + first, QUART)), factor[:], MULT)
-                store(u, h, first, res)
-
-        up_bf = own([P, N * PACK], BF16, "up_bf")
-        nc.scalar.copy(
-            up_bf[:].rearrange("p (c i t) -> p c t i", t=PACK, i=4),
-            up_raw[:].rearrange("p t (c i) -> p c t i", i=4),
+                    down_pass(banks[c], 0, c, a, t, a == 0 and t == 0, a == PASSES - 1 and t == PACK - 1)
+        for c in range(2):
+            copy_h(h_bf[0][:, c * WIDE : (c + 1) * WIDE], banks[c])
+        h_q = [quantise(mx_pair(QUART, "h_q0"), h_bf[0])]
+        for u in range(2):
+            y_wb4(y[u, 1][:], u, 0, QUART, True)
+        for c in range(2):
+            down(0, 2 + c, h_bf[1][:, c * WIDE : (c + 1) * WIDE], 6 + c)
+        x_00 = gather_x(own([P, HALF], F32, "x_00"), 0, 0)
+        x_late = {(0, 0): gather_x(own([P, QUART], F32, "x_010"), 0, HALF)}
+        h_q.append(quantise(mx_pair(QUART, "h_q1"), h_bf[1]))
+        up_bf = shared([P, N * PACK], BF16, "up_bf", AT_UP_BF)
+        nc.gpsimd.tensor_scalar(
+            up_bf[:].rearrange("p (n t) -> p n t", t=PACK), up_raw[:].rearrange("p t n -> p n t"), 1.0, 0.0, MULT, ADD
         )
-        def piece(u, first, h_q):
-            bank = hbanks.tile([P, QUART], F32, name="hbank")
-            for a in range(PASSES):
-                codes, scales = v_operand(1, a, first, QUART)
-                nc.tensor.matmul_mx(
-                    bank[:], lhsT=w4_codes(a, u), lhsT_scale=w_scales(a, W4_COL + u * P),
-                    rhs=codes, rhs_scale=scales, start=(a == 0), stop=False,
-                )
-            for a in range(PASSES):
-                for c in range(0, QUART, BLOCK):
-                    codes, scales = v_operand(1, a, first + c, BLOCK)
-                    nc.tensor.matmul_mx(
-                        bank[:, c : c + BLOCK], lhsT=w8[:, a, u * P : (u + 1) * P].bitcast(FP8X4),
-                        lhsT_scale=w_scales(a, W8_COL + u * P), rhs=codes, rhs_scale=scales, start=False, stop=False,
-                    )
-            cols = slice(u * P, (u + 1) * P)
-            nc.tensor.matmul_mx(
-                bank[:], lhsT=up_q[0][:, cols].bitcast(FP8X4), lhsT_scale=up_q[1][:, cols],
-                rhs=h_q[0][:].bitcast(FP8X4), rhs_scale=h_q[1][:], start=False, stop=True,
-            )
-            return bank
-
-        def piece_fused(u, bank, res):
-            factor = own([P, QUART], F32, f"factor{u}_third")
-            nc.scalar.activation(factor[:], bank[:], IDENTITY, bias=bias1[:, u : u + 1])
-            nc.vector.tensor_tensor(res[:], x0[u][:].indirect(picks(HALF, QUART)), factor[:], MULT)
-            store(u, 1, 0, res)
-
-        def piece_plain(u, bank, x_last):
-            res = own([P, QUART], F32, f"res{u}_last")
-            nc.vector.scalar_tensor_tensor(res[:], bank[:], bias1[:, u : u + 1], x_last[:], ADD, MULT)
-            store(u, 1, QUART, res)
-
-        h_bf0 = shared([P, HALF * PACK], BF16, "h_bf0", AT_H0)
-        h_bf2 = own([P, QUART * PACK], BF16, "h_bf2")
-        h_bf3 = shared([P, QUART * PACK], BF16, "h_bf3", AT_H3)
-        for u in range(2):
-            y_wb4(u, 0, 0, QUART)
-        for u in range(2):
-            y_wb4(u, 0, QUART, QUART)
-        down(0, h_bf0, range(4))
-        up_q = quantise(up_bf, "up")
-        gather_x(0, 0)
-        h_q_first = quantise(h_bf0, "h_first")
-        x_last = [shared([P, QUART], F32, "x_last0", AT_H0), own([P, QUART], F32, "x_last1")]
-        nc.vector.tensor_copy(x_last[0][:], x0[0][:].indirect(picks(HALF + QUART, QUART)))
-        down(1, h_bf2, range(2))
-        h_q_third = quantise(h_bf2, "h_third")
-        y_wb8(0, 0)
-        y_up(0, 0, up_q, h_q_first)
-        finish(0, 0, 0, HALF)
-        nc.vector.tensor_copy(x_last[1][:], x0[1][:].indirect(picks(HALF + QUART, QUART)))
-        y_wb8(1, 0)
-        y_up(1, 0, up_q, h_q_first)
-        finish_fused(1, 0)
-        down(1, h_bf3, range(2, 4), 2)
-        h_q_last = quantise(h_bf3, "h_last")
-        piece_fused(1, piece(1, 0, h_q_third), own([P, QUART], F32, "res1_third"))
-        piece_fused(0, piece(0, 0, h_q_third), shared([P, QUART], F32, "res0_third", AT_H3))
+        up_q = quantise(mx_pair(N, "up_q"), up_bf)
+        x_late[0, 1] = gather_x(shared([P, QUART], F32, "x_011", AT_UP_BF), 0, HALF + QUART)
+        for c in range(2):
+            down(1, c, h_bf[2][:, c * WIDE : (c + 1) * WIDE], 4 + c)
+        third = shared([P, QUART], U32, "h_q2_codes", AT_UP_BF + 4 * QUART), own([P, QUART], U8, "h_q2_scales")
+        h_q.append(quantise(third, h_bf[2]))
         for u in (1, 0):
-            piece_plain(u, piece(u, QUART, h_q_last), x_last[u])
+            for c in range(2):
+                y_wb8(y[u, c][:], u, 0, c * QUART)
+                y_up(y[u, c][:], u, h_q[c])
+        for c in range(2):
+            finish_fused(1, c * QUART, y[1, c][:])
+        for c in range(2):
+            finish_aside(0, c * QUART, y[0, c][:], x_00[:, c * QUART : (c + 1) * QUART])
+        for c in range(2):
+            down(1, 2 + c, h_bf[3][:, c * WIDE : (c + 1) * WIDE], c)
+        x_late[1, 1] = gather_x(shared([P, QUART], F32, "x_111", AT_H2), 1, HALF + QUART)
+        h_q.append(quantise(mx_pair(QUART, "h_q3"), h_bf[3]))
+
+        for c in range(2):
+            for u in (1, 0):
+                sums = in_bank([P, QUART], f"y{u}_late{c}", 2 * (1 - c) + 1 - u)
+                y_wb4(sums[:], u, 1, c * QUART, True)
+                y_wb8(sums[:], u, 1, c * QUART)
+                y_up(sums[:], u, h_q[2 + c])
+                if (u, c) in x_late:
+                    finish(u, HALF + c * QUART, sums[:], x_late[u, c][:])
+                else:
+                    finish_fused(u, HALF + c * QUART, sums[:])

@@ -117,7 +117,7 @@ def tile_list_xcross_res_none_kernel(
         x0 = [own([P, T], F32, f"x0_{u}") for u in range(2)]
         nc.sync.dma_start(x0[0][:], x0T[0:P, :])
         spread(planes[1], late[:])
-        up_raw = own([P, PACK, N], F32, "up_raw")
+        up_raw = shared([P, PACK, N], F32, "up_raw", AT_H2)
         nc.sync.dma_start(up_raw[:], upw.rearrange("(p t) n -> p t n", t=PACK))
         w8 = own([P, PASSES, N], I32, "w8")
         nc.sync.dma_start(w8[:], wb8_words.rearrange("a p n c -> p a (n c)").bitcast(I32))
@@ -185,9 +185,8 @@ def tile_list_xcross_res_none_kernel(
                 )
 
         def y_up(dst, u, h_q):
-            rows = slice(u * P, (u + 1) * P)
             nc.tensor.matmul_mx(
-                dst, lhsT=up_q[0][:, rows].bitcast(FP8X4), lhsT_scale=up_q[1][:, rows],
+                dst, lhsT=up_q[u][0][:].bitcast(FP8X4), lhsT_scale=up_q[u][1][:],
                 rhs=h_q[0][:].bitcast(FP8X4), rhs_scale=h_q[1][:], start=False, stop=True,
             )
 
@@ -235,18 +234,10 @@ def tile_list_xcross_res_none_kernel(
             nc.vector.tensor_tensor(res[:], x0[u][:].indirect(picks(first, count)), factor[:], MULT)
             store(u, first, res)
 
-        def finish_aside(u, first, sums, x_picked):
-            count = sums.shape[1]
-            factor = own([P, count], F32, f"factor{u}_{first}")
-            nc.scalar.activation(factor[:], sums, IDENTITY, bias=bias1[:, u : u + 1])
-            res = own([P, count], F32, f"res{u}_{first}")
-            nc.gpsimd.tensor_tensor(res[:], x_picked, factor[:], MULT)
-            store(u, first, res)
-
         WIDE = PACK * BLOCK
         h_bf = [own([P, QUART * PACK], BF16, f"h_bf{c}") for c in range(2)]
         h_bf += [shared([P, QUART * PACK], BF16, "h_bf2", AT_H2), own([P, QUART * PACK], BF16, "h_bf3")]
-        y = {(u, c): in_bank([P, QUART], f"y{u}{c}", 2 * (1 - u) + c) for u in range(2) for c in range(2)}
+        y = {(u, c): in_bank([P, QUART], f"y{u}{c}", 2 * u + c) for u in range(2) for c in range(2)}
 
         for u in range(2):
             y_wb4(y[u, 0][:], u, 0, 0, True)
@@ -265,24 +256,27 @@ def tile_list_xcross_res_none_kernel(
         x_00 = gather_x(own([P, HALF], F32, "x_00"), 0, 0)
         x_late = {(0, 0): gather_x(own([P, QUART], F32, "x_010"), 0, HALF)}
         h_q.append(quantise(mx_pair(QUART, "h_q1"), h_bf[1]))
-        up_bf = shared([P, N * PACK], BF16, "up_bf", AT_UP_BF)
-        nc.gpsimd.tensor_scalar(
-            up_bf[:].rearrange("p (n t) -> p n t", t=PACK), up_raw[:].rearrange("p t n -> p n t"), 1.0, 0.0, MULT, ADD
-        )
-        up_q = quantise(mx_pair(N, "up_q"), up_bf)
+        up_q = []
+        for u in range(2):
+            up_bf = shared([P, P * PACK], BF16, f"up_bf{u}", AT_UP_BF + 2 * WIDE * u)
+            nc.scalar.copy(
+                up_bf[:].rearrange("p (c i t) -> p c t i", t=PACK, i=4),
+                up_raw[:, :, u * P : (u + 1) * P].rearrange("p t (c i) -> p c t i", i=4),
+            )
+            up_q.append(quantise(mx_pair(P, f"up_q{u}"), up_bf))
         x_late[0, 1] = gather_x(shared([P, QUART], F32, "x_011", AT_UP_BF), 0, HALF + QUART)
         for c in range(2):
             down(1, c, h_bf[2][:, c * WIDE : (c + 1) * WIDE], 4 + c)
         third = shared([P, QUART], U32, "h_q2_codes", AT_UP_BF + 4 * QUART), own([P, QUART], U8, "h_q2_scales")
         h_q.append(quantise(third, h_bf[2]))
-        for u in (1, 0):
+        for u in range(2):
             for c in range(2):
                 y_wb8(y[u, c][:], u, 0, c * QUART)
                 y_up(y[u, c][:], u, h_q[c])
         for c in range(2):
-            finish_fused(1, c * QUART, y[1, c][:])
+            finish(0, c * QUART, y[0, c][:], x_00[:, c * QUART : (c + 1) * QUART])
         for c in range(2):
-            finish_aside(0, c * QUART, y[0, c][:], x_00[:, c * QUART : (c + 1) * QUART])
+            finish_fused(1, c * QUART, y[1, c][:])
         for c in range(2):
             down(1, 2 + c, h_bf[3][:, c * WIDE : (c + 1) * WIDE], c)
         x_late[1, 1] = gather_x(shared([P, QUART], F32, "x_111", AT_H2), 1, HALF + QUART)

@@ -91,7 +91,6 @@ def tile_list_xcross_res_none_kernel(
         dn_raw = [own([P, R], U32, f"dn_raw{a}") for a in range(PASSES)]
         load_words(dn_raw[0], dn_words[0])
 
-        nc.vector.memset(dn_rows[0:ROW0, :].bitcast(I32), 0)
         nc.vector.memset(tab_rows[0:ROW0, :].bitcast(I32), 0)
         planes = [own([P, PASSES * STAGE_COLS], U8, "plane0"), own([P, PASSES * HALF], U8, "plane1")]
         for plane in planes:
@@ -100,9 +99,9 @@ def tile_list_xcross_res_none_kernel(
         def picks(first, count):
             return entries[:, first // 16 : (first + count) // 16]
 
-        nc.vector.tensor_copy(
-            stage[:, DN_COL : DN_COL + R].rearrange("p (t m) -> p t m", t=PACK),
-            dn_rows[:].rearrange("p (m t) -> p t m", t=PACK),
+        nc.scalar.copy(
+            stage[ROW0:P, DN_COL : DN_COL + R].bitcast(U16).rearrange("p (t m) -> p t m", t=PACK),
+            dn_rows[ROW0:P, :].bitcast(U16).rearrange("p (m t) -> p t m", t=PACK),
         )
         early = [shared([P, QUART], U8, "picked_a", AT_PICKED), own([P, QUART], U8, "picked_b")]
         for c in range(2):
@@ -118,7 +117,8 @@ def tile_list_xcross_res_none_kernel(
         nc.sync.dma_start(x0[0][:], x0T[0:P, :])
         spread(planes[1], late[:])
         up_raw = shared([P, PACK, N], F32, "up_raw", AT_H2)
-        nc.sync.dma_start(up_raw[:], upw.rearrange("(p t) n -> p t n", t=PACK))
+        for i in range(2):
+            nc.sync.dma_start(up_raw[i:P:2, :, :], upw.rearrange("(m t i) n -> i m t n", t=PACK, i=2)[i])
         w8 = own([P, PASSES, N], I32, "w8")
         nc.sync.dma_start(w8[:], wb8_words.rearrange("a p n c -> p a (n c)").bitcast(I32))
         nc.sync.dma_start(x0[1][:], x0T[P : 2 * P, :])
@@ -145,8 +145,8 @@ def tile_list_xcross_res_none_kernel(
         dn = [own([P, R], U32, f"dn{a}") for a in range(PASSES)]
         for a in range(PASSES):
             nc.scalar.copy(
-                dn[a][:].rearrange("p (t m i) -> p m t i", t=PACK, i=4),
-                dn_raw[a][:].rearrange("p (m i t) -> p m t i", t=PACK, i=4),
+                dn[a][:].rearrange("p (t g m i) -> p g t m i", t=PACK, m=2, i=2),
+                dn_raw[a][:].rearrange("p (g m t i) -> p g t m i", t=PACK, m=2, i=2),
             )
 
         def v_operand(h, a, first, count):
@@ -187,7 +187,7 @@ def tile_list_xcross_res_none_kernel(
         def y_up(dst, u, h_q):
             nc.tensor.matmul_mx(
                 dst, lhsT=up_q[u][0][:].bitcast(FP8X4), lhsT_scale=up_q[u][1][:],
-                rhs=h_q[0][:].bitcast(FP8X4), rhs_scale=h_q[1][:], start=False, stop=True,
+                rhs=h_q[0][:, :].bitcast(FP8X4), rhs_scale=h_q[1][:, :], start=False, stop=True,
             )
 
         def down_pass(bank, h, c, a, t, start, stop):
@@ -272,6 +272,7 @@ def tile_list_xcross_res_none_kernel(
         for u in range(2):
             for c in range(2):
                 y_wb8(y[u, c][:], u, 0, c * QUART)
+            for c in range(2):
                 y_up(y[u, c][:], u, h_q[c])
         for c in range(2):
             finish(0, c * QUART, y[0, c][:], x_00[:, c * QUART : (c + 1) * QUART])
@@ -282,13 +283,19 @@ def tile_list_xcross_res_none_kernel(
         x_late[1, 1] = gather_x(shared([P, QUART], F32, "x_111", AT_H2), 1, HALF + QUART)
         h_q.append(quantise(mx_pair(QUART, "h_q3"), h_bf[3]))
 
-        for c in range(2):
-            for u in (1, 0):
-                sums = in_bank([P, QUART], f"y{u}_late{c}", 2 * (1 - c) + 1 - u)
-                y_wb4(sums[:], u, 1, c * QUART, True)
-                y_wb8(sums[:], u, 1, c * QUART)
-                y_up(sums[:], u, h_q[2 + c])
-                if (u, c) in x_late:
-                    finish(u, HALF + c * QUART, sums[:], x_late[u, c][:])
-                else:
-                    finish_fused(u, HALF + c * QUART, sums[:])
+        def piece(u, first, count, at):
+            c, start = divmod(first, QUART)
+            sums = in_bank([P, count], f"y{u}_late{first}", at)
+            y_wb4(sums[:], u, 1, first, True)
+            y_wb8(sums[:], u, 1, first)
+            y_up(sums[:], u, [part[:, start : start + count] for part in h_q[2 + c]])
+            if (u, c) in x_late:
+                finish(u, HALF + first, sums[:], x_late[u, c][:, start : start + count])
+            else:
+                finish_fused(u, HALF + first, sums[:])
+
+        piece(1, 0, QUART, 2)
+        piece(0, 0, QUART, 3)
+        piece(1, QUART, QUART, 0)
+        piece(0, QUART, BLOCK, 1)
+        piece(0, QUART + BLOCK, BLOCK, 2)

@@ -297,5 +297,4 @@ def tile_list_xcross_res_none_kernel(
         piece(1, 0, QUART, 2)
         piece(0, 0, QUART, 3)
         piece(1, QUART, QUART, 0)
-        piece(0, QUART, BLOCK, 1)
-        piece(0, QUART + BLOCK, BLOCK, 2)
+        piece(0, QUART, QUART, 1)

@@ -137,10 +137,15 @@ def tile_list_xcross_res_none_kernel(
                 pairs[:].bitcast(U16).rearrange("p (j a) -> p a j", a=PASSES),
             )
 
-        for first, count in ((0, BLOCK), (QUART, BLOCK), (HALF, QUART)):
-            both = [gather_words(first + c * count, count, AT_PAIRS + 4 * QUART * c) for c in range(2)]
-            for c in range(2):
-                part(first + c * count, both[c])
+        both = [gather_words(0, BLOCK, AT_PAIRS), gather_words(BLOCK, BLOCK, AT_PAIRS + 4 * QUART)]
+        for c in range(2):
+            part(c * BLOCK, both[c])
+        waiting = gather_words(QUART, QUART, AT_PAIRS)
+        for q in (2, 3):
+            ahead = gather_words(q * QUART, QUART, AT_PAIRS + 4 * QUART * (3 - q))
+            part((q - 1) * QUART, waiting)
+            waiting = ahead
+        part(3 * QUART, waiting)
 
         dn = [own([P, R], U32, f"dn{a}") for a in range(PASSES)]
         for a in range(PASSES):
@@ -184,10 +189,10 @@ def tile_list_xcross_res_none_kernel(
                     rhs=codes, rhs_scale=scales, start=False, stop=False,
                 )
 
-        def y_up(dst, u, h_q):
+        def y_up(dst, u, h_q, closes):
             nc.tensor.matmul_mx(
                 dst, lhsT=up_q[u][0][:].bitcast(FP8X4), lhsT_scale=up_q[u][1][:],
-                rhs=h_q[0][:, :].bitcast(FP8X4), rhs_scale=h_q[1][:, :], start=False, stop=True,
+                rhs=h_q[0][:, :].bitcast(FP8X4), rhs_scale=h_q[1][:, :], start=False, stop=closes,
             )
 
         def down_pass(bank, h, c, a, t, start, stop):
@@ -237,10 +242,10 @@ def tile_list_xcross_res_none_kernel(
         WIDE = PACK * BLOCK
         h_bf = [own([P, QUART * PACK], BF16, f"h_bf{c}") for c in range(2)]
         h_bf += [shared([P, QUART * PACK], BF16, "h_bf2", AT_H2), own([P, QUART * PACK], BF16, "h_bf3")]
-        y = {(u, c): in_bank([P, QUART], f"y{u}{c}", 2 * u + c) for u in range(2) for c in range(2)}
+        y = [in_bank([P, HALF], f"y{u}", u) for u in range(2)]
 
         for u in range(2):
-            y_wb4(y[u, 0][:], u, 0, 0, True)
+            y_wb4(y[u][:, 0:QUART], u, 0, 0, True)
         banks = [in_bank([P, PACK, BLOCK], f"h0{c}", 4 + c) for c in range(2)]
         for a in range(PASSES):
             for c in range(2):
@@ -250,7 +255,7 @@ def tile_list_xcross_res_none_kernel(
             copy_h(h_bf[0][:, c * WIDE : (c + 1) * WIDE], banks[c])
         h_q = [quantise(mx_pair(QUART, "h_q0"), h_bf[0])]
         for u in range(2):
-            y_wb4(y[u, 1][:], u, 0, QUART, True)
+            y_wb4(y[u][:, QUART:HALF], u, 0, QUART, False)
         for c in range(2):
             down(0, 2 + c, h_bf[1][:, c * WIDE : (c + 1) * WIDE], 6 + c)
         x_00 = gather_x(own([P, HALF], F32, "x_00"), 0, 0)
@@ -269,32 +274,34 @@ def tile_list_xcross_res_none_kernel(
             down(1, c, h_bf[2][:, c * WIDE : (c + 1) * WIDE], 4 + c)
         third = shared([P, QUART], U32, "h_q2_codes", AT_UP_BF + 4 * QUART), own([P, QUART], U8, "h_q2_scales")
         h_q.append(quantise(third, h_bf[2]))
+        third = {1: in_bank([P, QUART], "y1_third", 2)}
+        y_wb4(third[1][:], 1, 1, 0, True)
         for u in range(2):
+            y_wb8(y[u][:], u, 0, 0)
             for c in range(2):
-                y_wb8(y[u, c][:], u, 0, c * QUART)
-            for c in range(2):
-                y_up(y[u, c][:], u, h_q[c])
+                y_up(y[u][:, c * QUART : (c + 1) * QUART], u, h_q[c], c == 1)
+        finish(0, 0, y[0][:], x_00[:])
+        finish_fused(1, 0, y[1][:])
         for c in range(2):
-            finish(0, c * QUART, y[0, c][:], x_00[:, c * QUART : (c + 1) * QUART])
-        for c in range(2):
-            finish_fused(1, c * QUART, y[1, c][:])
-        for c in range(2):
-            down(1, 2 + c, h_bf[3][:, c * WIDE : (c + 1) * WIDE], c)
+            down(1, 2 + c, h_bf[3][:, c * WIDE : (c + 1) * WIDE], 4 + c)
         x_late[1, 1] = gather_x(shared([P, QUART], F32, "x_111", AT_H2), 1, HALF + QUART)
         h_q.append(quantise(mx_pair(QUART, "h_q3"), h_bf[3]))
 
         def piece(u, first, count, at):
             c, start = divmod(first, QUART)
-            sums = in_bank([P, count], f"y{u}_late{first}", at)
-            y_wb4(sums[:], u, 1, first, True)
+            if at is None:
+                sums = third[u]
+            else:
+                sums = in_bank([P, count], f"y{u}_late{first}", at)
+                y_wb4(sums[:], u, 1, first, True)
             y_wb8(sums[:], u, 1, first)
-            y_up(sums[:], u, [part[:, start : start + count] for part in h_q[2 + c]])
+            y_up(sums[:], u, [part[:, start : start + count] for part in h_q[2 + c]], True)
             if (u, c) in x_late:
                 finish(u, HALF + first, sums[:], x_late[u, c][:, start : start + count])
             else:
                 finish_fused(u, HALF + first, sums[:])
 
-        piece(1, 0, QUART, 2)
-        piece(0, 0, QUART, 3)
-        piece(1, QUART, QUART, 0)
-        piece(0, QUART, QUART, 1)
+        piece(1, 0, QUART, None)
+        piece(0, 0, QUART, 0)
+        piece(1, QUART, QUART, 4)
+        piece(0, QUART, QUART, 5)

@@ -189,10 +189,10 @@ def tile_list_xcross_res_none_kernel(
                     rhs=codes, rhs_scale=scales, start=False, stop=False,
                 )
 
-        def y_up(dst, u, h_q, closes):
+        def y_up(dst, u, h_q):
             nc.tensor.matmul_mx(
                 dst, lhsT=up_q[u][0][:].bitcast(FP8X4), lhsT_scale=up_q[u][1][:],
-                rhs=h_q[0][:, :].bitcast(FP8X4), rhs_scale=h_q[1][:, :], start=False, stop=closes,
+                rhs=h_q[0][:, :].bitcast(FP8X4), rhs_scale=h_q[1][:, :], start=False, stop=True,
             )
 
         def down_pass(bank, h, c, a, t, start, stop):
@@ -216,7 +216,7 @@ def tile_list_xcross_res_none_kernel(
             return own([P, width], U32, name + "_codes"), own([P, width], U8, name + "_scales")
 
         def quantise(dst, src):
-            nc.vector.quantize_mx(dst[0][:].bitcast(FP8X4), dst[1][:], src[:])
+            nc.vector.quantize_mx(dst[0][:, :].bitcast(FP8X4), dst[1][:, :], src[:])
             return dst
 
         def gather_x(dst, u, first):
@@ -253,14 +253,15 @@ def tile_list_xcross_res_none_kernel(
                     down_pass(banks[c], 0, c, a, t, a == 0 and t == 0, a == PASSES - 1 and t == PACK - 1)
         for c in range(2):
             copy_h(h_bf[0][:, c * WIDE : (c + 1) * WIDE], banks[c])
-        h_q = [quantise(mx_pair(QUART, "h_q0"), h_bf[0])]
-        for u in range(2):
-            y_wb4(y[u][:, QUART:HALF], u, 0, QUART, False)
+        first_half = mx_pair(HALF, "h_q01")
+        h_q = [quantise([part[:, 0:QUART] for part in first_half], h_bf[0])]
         for c in range(2):
             down(0, 2 + c, h_bf[1][:, c * WIDE : (c + 1) * WIDE], 6 + c)
-        x_00 = gather_x(own([P, HALF], F32, "x_00"), 0, 0)
-        x_late = {(0, 0): gather_x(own([P, QUART], F32, "x_010"), 0, HALF)}
-        h_q.append(quantise(mx_pair(QUART, "h_q1"), h_bf[1]))
+        for u in range(2):
+            y_wb4(y[u][:, QUART:HALF], u, 0, QUART, False)
+        x_first = gather_x(own([P, HALF + QUART], F32, "x_first"), 0, 0)
+        x_late = {(0, 0): x_first[:, HALF : HALF + QUART]}
+        h_q.append(quantise([part[:, QUART:HALF] for part in first_half], h_bf[1]))
         up_q = []
         for u in range(2):
             up_bf = shared([P, P * PACK], BF16, f"up_bf{u}", AT_UP_BF + 2 * WIDE * u)
@@ -274,13 +275,13 @@ def tile_list_xcross_res_none_kernel(
             down(1, c, h_bf[2][:, c * WIDE : (c + 1) * WIDE], 4 + c)
         third = shared([P, QUART], U32, "h_q2_codes", AT_UP_BF + 4 * QUART), own([P, QUART], U8, "h_q2_scales")
         h_q.append(quantise(third, h_bf[2]))
-        third = {1: in_bank([P, QUART], "y1_third", 2)}
-        y_wb4(third[1][:], 1, 1, 0, True)
+        opened = [in_bank([P, QUART], f"y{u}_third", 3 - u) for u in range(2)]
+        for u in (1, 0):
+            y_wb4(opened[u][:], u, 1, 0, True)
         for u in range(2):
             y_wb8(y[u][:], u, 0, 0)
-            for c in range(2):
-                y_up(y[u][:, c * QUART : (c + 1) * QUART], u, h_q[c], c == 1)
-        finish(0, 0, y[0][:], x_00[:])
+            y_up(y[u][:], u, first_half)
+        finish(0, 0, y[0][:], x_first[:, 0:HALF])
         finish_fused(1, 0, y[1][:])
         for c in range(2):
             down(1, 2 + c, h_bf[3][:, c * WIDE : (c + 1) * WIDE], 4 + c)
@@ -290,18 +291,18 @@ def tile_list_xcross_res_none_kernel(
         def piece(u, first, count, at):
             c, start = divmod(first, QUART)
             if at is None:
-                sums = third[u]
+                sums = opened[u]
             else:
                 sums = in_bank([P, count], f"y{u}_late{first}", at)
                 y_wb4(sums[:], u, 1, first, True)
             y_wb8(sums[:], u, 1, first)
-            y_up(sums[:], u, [part[:, start : start + count] for part in h_q[2 + c]], True)
+            y_up(sums[:], u, [part[:, start : start + count] for part in h_q[2 + c]])
             if (u, c) in x_late:
                 finish(u, HALF + first, sums[:], x_late[u, c][:, start : start + count])
             else:
                 finish_fused(u, HALF + first, sums[:])
 
         piece(1, 0, QUART, None)
-        piece(0, 0, QUART, 0)
+        piece(0, 0, QUART, None)
         piece(1, QUART, QUART, 4)
         piece(0, QUART, QUART, 5)

@@ -288,21 +288,20 @@ def tile_list_xcross_res_none_kernel(
         x_late[1, 1] = gather_x(shared([P, QUART], F32, "x_111", AT_H2), 1, HALF + QUART)
         h_q.append(quantise(mx_pair(QUART, "h_q3"), h_bf[3]))
 
-        def piece(u, first, count, at):
-            c, start = divmod(first, QUART)
-            if at is None:
-                sums = opened[u]
+        def close(sums, u, q):
+            y_up(sums[:], u, h_q[q])
+            if (u, q - 2) in x_late:
+                finish(u, q * QUART, sums[:], x_late[u, q - 2][:, :])
             else:
-                sums = in_bank([P, count], f"y{u}_late{first}", at)
-                y_wb4(sums[:], u, 1, first, True)
-            y_wb8(sums[:], u, 1, first)
-            y_up(sums[:], u, [part[:, start : start + count] for part in h_q[2 + c]])
-            if (u, c) in x_late:
-                finish(u, HALF + first, sums[:], x_late[u, c][:, start : start + count])
-            else:
-                finish_fused(u, HALF + first, sums[:])
+                finish_fused(u, q * QUART, sums[:])
 
-        piece(1, 0, QUART, None)
-        piece(0, 0, QUART, None)
-        piece(1, QUART, QUART, 4)
-        piece(0, QUART, QUART, 5)
+        for u in (1, 0):
+            y_wb8(opened[u][:], u, 1, 0)
+            close(opened[u], u, 2)
+        last = [in_bank([P, QUART], f"y{u}_last", 5 - u) for u in range(2)]
+        y_wb4(last[1][:], 1, 1, QUART, True)
+        y_wb8(last[1][:], 1, 1, QUART)
+        y_wb4(last[0][:], 0, 1, QUART, True)
+        close(last[1], 1, 3)
+        y_wb8(last[0][:], 0, 1, QUART)
+        close(last[0], 0, 3)

@@ -1,6 +1,7 @@
 from contextlib import ExitStack
 
 import concourse.mybir as mybir
+from concourse.masks import make_identity
 
 K, R, N, T, J = 1024, 512, 256, 2048, 1024
 FLOPS = 2 * J * (K * R + 2 * K * N + R * N)
@@ -66,11 +67,10 @@ def tile_list_xcross_res_none_kernel(
         def load_words(dst, words):
             nc.sync.dma_start(dst[:].bitcast(I32), words.rearrange("p n c -> p (n c)").bitcast(I32))
 
-        bias = own([P, N // P], F32, "bias")
-        with nc.allow_non_contiguous_dma(reason="one value of b to a partition and output tile"):
-            nc.gpsimd.dma_start(bias[:], b.rearrange("(u p) -> p u", p=P))
-        bias1 = own([P, N // P], F32, "bias1")
-        nc.scalar.activation(bias1[:], bias[:], IDENTITY, bias=1.0)
+        b_rows = own([P, P], F32, "b_rows")
+        nc.vector.memset(b_rows[:], 0.0)
+        identity = own([P, P], F32, "identity")
+        make_identity(nc, identity[:])
 
         dn_rows = own([P, R], U8, "dn_rows")
         load_scale_rows(nc.scalar, dn_rows[ROW0:P, :], dn_scales)
@@ -81,6 +81,7 @@ def tile_list_xcross_res_none_kernel(
         stage = own([P, STAGE_COLS], U8, "stage")
         load_scale_rows(nc.scalar, stage[ROW0:P, W4_COL : W4_COL + N], wb4_scales)
         load_scale_rows(nc.sync, stage[ROW0:P, W8_COL : W8_COL + N], wb8_scales)
+        nc.scalar.dma_start(b_rows[0 : N // P, :], b.rearrange("(u p) -> u p", p=P))
         tab = own([P, T], U32, "tab")
         load_words(tab, tab_words[0])
         w4 = own([P, PASSES * 2 * N], U8, "w4")
@@ -164,6 +165,11 @@ def tile_list_xcross_res_none_kernel(
 
         def w4_codes(a, u):
             return w4[:, 2 * (a * N + u * P) : 2 * (a * N + (u + 1) * P)].bitcast(FP4X4)
+
+        b_turned = in_bank([P, P], "b_turned", 3)
+        nc.tensor.transpose(b_turned[:], b_rows[:], identity[:])
+        bias1 = own([P, N // P], F32, "bias1")
+        nc.scalar.activation(bias1[:], b_turned[:, 0 : N // P], IDENTITY, bias=1.0)
 
         warm = in_bank([P, HALF], "warm", 7)
 

@@ -84,13 +84,9 @@ def tile_list_xcross_res_none_kernel(
         nc.scalar.dma_start(b_rows[0 : N // P, :], b.rearrange("(u p) -> u p", p=P))
         tab = own([P, T], U32, "tab")
         load_words(tab, tab_words[0])
-        w4 = own([P, PASSES * 2 * N], U8, "w4")
-        nc.sync.dma_start(
-            w4[:].bitcast(I32).rearrange("p (a c) -> p a c", a=PASSES),
-            wb4_words.bitcast(I32).rearrange("a p c -> p a c"),
-        )
         dn_raw = [own([P, R], U32, f"dn_raw{a}") for a in range(PASSES)]
-        load_words(dn_raw[0], dn_words[0])
+        for a in range(PASSES):
+            load_words(dn_raw[a], dn_words[a])
 
         nc.vector.memset(tab_rows[0:ROW0, :].bitcast(I32), 0)
         planes = [own([P, PASSES * STAGE_COLS], U8, "plane0"), own([P, PASSES * HALF], U8, "plane1")]
@@ -111,7 +107,11 @@ def tile_list_xcross_res_none_kernel(
             col = TAB_COL + c * QUART
             nc.vector.tensor_copy(stage[ROW0:P, col : col + QUART].bitcast(I32), early[c][ROW0:P, :].bitcast(I32))
         spread(planes[0], stage[:])
-        load_words(dn_raw[1], dn_words[1])
+        w4 = own([P, PASSES * 2 * N], U8, "w4")
+        nc.sync.dma_start(
+            w4[:].bitcast(I32).rearrange("p (a c) -> p a c", a=PASSES),
+            wb4_words.bitcast(I32).rearrange("a p c -> p a c"),
+        )
         late = shared([P, HALF], U8, "picked_late", AT_PICKED)
         nc.vector.tensor_copy(late[:], tab_rows[:].indirect(picks(HALF, HALF)))
         x0 = [own([P, T], F32, f"x0_{u}") for u in range(2)]
@@ -124,7 +124,7 @@ def tile_list_xcross_res_none_kernel(
         nc.sync.dma_start(w8[:], wb8_words.rearrange("a p n c -> p a (n c)").bitcast(I32))
         nc.sync.dma_start(x0[1][:], x0T[P : 2 * P, :])
 
-        v = [own([P, PASSES * 2 * HALF], U8, f"v{h}") for h in range(2)]
+        v = {0: own([P, PASSES * 2 * HALF], U8, "v0"), HALF: own([P, PASSES * 2 * QUART], U8, "v2")}
 
         def gather_words(first, count, at):
             pairs = shared([P, count], U32, f"pairs{first}", at)
@@ -132,21 +132,20 @@ def tile_list_xcross_res_none_kernel(
             return pairs
 
         def part(first, pairs):
-            cols = slice(first % HALF, first % HALF + pairs.shape[1])
+            base = max(key for key in v if key <= first)
+            cols = slice(first - base, first - base + pairs.shape[1])
             nc.vector.tensor_copy(
-                v[first // HALF][:].bitcast(U16).rearrange("p (a j) -> p a j", a=PASSES)[:, :, cols],
+                v[base][:].bitcast(U16).rearrange("p (a j) -> p a j", a=PASSES)[:, :, cols],
                 pairs[:].bitcast(U16).rearrange("p (j a) -> p a j", a=PASSES),
             )
 
         both = [gather_words(0, BLOCK, AT_PAIRS), gather_words(BLOCK, BLOCK, AT_PAIRS + 4 * QUART)]
         for c in range(2):
             part(c * BLOCK, both[c])
-        waiting = gather_words(QUART, QUART, AT_PAIRS)
-        for q in (2, 3):
-            ahead = gather_words(q * QUART, QUART, AT_PAIRS + 4 * QUART * (3 - q))
-            part((q - 1) * QUART, waiting)
-            waiting = ahead
-        part(3 * QUART, waiting)
+        middle = [gather_words(q * QUART, QUART, AT_PAIRS + 4 * QUART * (q - 1)) for q in (1, 2)]
+        for q in (1, 2):
+            part(q * QUART, middle[q - 1])
+        last_pairs = gather_words(3 * QUART, QUART, AT_PAIRS)
 
         dn = [own([P, R], U32, f"dn{a}") for a in range(PASSES)]
         for a in range(PASSES):
@@ -156,7 +155,9 @@ def tile_list_xcross_res_none_kernel(
             )
 
         def v_operand(h, a, first, count):
-            codes = v[h][:, 2 * (a * HALF + first) : 2 * (a * HALF + first + count)].bitcast(FP4X4)
+            base = max(key for key in v if key <= h * HALF + first)
+            at = a * v[base].shape[1] // PASSES + 2 * (h * HALF + first - base)
+            codes = v[base][:, at : at + 2 * count].bitcast(FP4X4)
             col = a * STAGE_COLS + TAB_COL + first if h == 0 else a * HALF + first
             return codes, planes[h][:, col : col + count]
 
@@ -179,22 +180,6 @@ def tile_list_xcross_res_none_kernel(
                 rhs=tab_rows[:, 0 : 2 * HALF].bitcast(FP4X4), rhs_scale=tab_rows[:, 0:HALF], start=True, stop=True,
             )
 
-        def y_wb4(dst, u, h, first, opens):
-            for a in range(PASSES):
-                codes, scales = v_operand(h, a, first, dst.shape[1])
-                nc.tensor.matmul_mx(
-                    dst, lhsT=w4_codes(a, u), lhsT_scale=w_scales(a, W4_COL + u * P),
-                    rhs=codes, rhs_scale=scales, start=(opens and a == 0), stop=False,
-                )
-
-        def y_wb8(dst, u, h, first):
-            for a in range(PASSES):
-                codes, scales = v_operand(h, a, first, dst.shape[1])
-                nc.tensor.matmul_mx(
-                    dst, lhsT=w8[:, a, u * P : (u + 1) * P].bitcast(FP8X4), lhsT_scale=w_scales(a, W8_COL + u * P),
-                    rhs=codes, rhs_scale=scales, start=False, stop=False,
-                )
-
         def y_up(dst, u, h_q):
             nc.tensor.matmul_mx(
                 dst, lhsT=up_q[u][0][:].bitcast(FP8X4), lhsT_scale=up_q[u][1][:],
@@ -211,22 +196,11 @@ def tile_list_xcross_res_none_kernel(
         def copy_h(dst, bank):
             nc.scalar.copy(dst.rearrange("p (j t) -> p j t", t=PACK), bank[:].rearrange("p t j -> p j t"))
 
-        def down(h, c, dst, at):
-            bank = in_bank([P, PACK, BLOCK], f"h{h}{c}", at)
-            for t in range(PACK):
-                for a in range(PASSES):
-                    down_pass(bank, h, c, a, t, a == 0, a == PASSES - 1)
-            copy_h(dst, bank)
-
         def mx_pair(width, name):
             return own([P, width], U32, name + "_codes"), own([P, width], U8, name + "_scales")
 
         def quantise(dst, src):
             nc.vector.quantize_mx(dst[0][:, :].bitcast(FP8X4), dst[1][:, :], src[:])
-            return dst
-
-        def gather_x(dst, u, first):
-            nc.vector.tensor_copy(dst[:], x0[u][:].indirect(picks(first, dst.shape[1])))
             return dst
 
         def store(u, first, res):
@@ -248,26 +222,42 @@ def tile_list_xcross_res_none_kernel(
         WIDE = PACK * BLOCK
         h_bf = [own([P, QUART * PACK], BF16, f"h_bf{c}") for c in range(2)]
         h_bf += [shared([P, QUART * PACK], BF16, "h_bf2", AT_H2), own([P, QUART * PACK], BF16, "h_bf3")]
-        y = [in_bank([P, HALF], f"y{u}", u) for u in range(2)]
+        y_half = [in_bank([P, HALF], f"y_half{u}", u) for u in range(2)]
+        piece_bank = {(1, 2): 3, (0, 2): 2, (1, 3): 6, (0, 3): 7}
 
-        for u in range(2):
-            y_wb4(y[u][:, 0:QUART], u, 0, 0, True)
-        banks = [in_bank([P, PACK, BLOCK], f"h0{c}", 4 + c) for c in range(2)]
-        for a in range(PASSES):
-            for c in range(2):
+        def piece(u, q):
+            return in_bank([P, QUART], f"y{u}_{q}", piece_bank[u, q])
+
+        def y_tier(dst, u, q, tier, opens):
+            for a in range(PASSES):
+                codes, scales = v_operand(q // 2, a, (q % 2) * QUART, dst.shape[1])
+                if tier == 4:
+                    w, w_scale = w4_codes(a, u), w_scales(a, W4_COL + u * P)
+                else:
+                    w, w_scale = w8[:, a, u * P : (u + 1) * P].bitcast(FP8X4), w_scales(a, W8_COL + u * P)
+                nc.tensor.matmul_mx(
+                    dst, lhsT=w, lhsT_scale=w_scale, rhs=codes, rhs_scale=scales, start=(opens and a == 0), stop=False
+                )
+
+        def down_block(h, c, at):
+            bank = in_bank([P, PACK, BLOCK], f"h{h}{c}", at)
+            for a in range(PASSES):
                 for t in range(PACK):
-                    down_pass(banks[c], 0, c, a, t, a == 0 and t == 0, a == PASSES - 1 and t == PACK - 1)
+                    down_pass(bank, h, c, a, t, a == 0 and t == 0, a == PASSES - 1 and t == PACK - 1)
+            return bank
+
         for c in range(2):
-            copy_h(h_bf[0][:, c * WIDE : (c + 1) * WIDE], banks[c])
+            copy_h(h_bf[0][:, c * WIDE : (c + 1) * WIDE], down_block(0, c, 4 + c))
         first_half = mx_pair(HALF, "h_q01")
-        h_q = [quantise([part[:, 0:QUART] for part in first_half], h_bf[0])]
+        h_q = [quantise([side[:, 0:QUART] for side in first_half], h_bf[0])]
+        y_tier(y_half[0][:, 0:QUART], 0, 0, 4, True)
         for c in range(2):
-            down(0, 2 + c, h_bf[1][:, c * WIDE : (c + 1) * WIDE], 6 + c)
-        for u in range(2):
-            y_wb4(y[u][:, QUART:HALF], u, 0, QUART, False)
-        x_first = gather_x(own([P, HALF + QUART], F32, "x_first"), 0, 0)
-        x_late = {(0, 0): x_first[:, HALF : HALF + QUART]}
-        h_q.append(quantise([part[:, QUART:HALF] for part in first_half], h_bf[1]))
+            copy_h(h_bf[1][:, c * WIDE : (c + 1) * WIDE], down_block(0, 2 + c, 6 + c))
+        y_tier(y_half[0][:, QUART:HALF], 0, 1, 4, False)
+        y_tier(y_half[1][:], 1, 0, 4, True)
+        x_ahead = own([P, HALF + QUART], F32, "x_ahead")
+        nc.vector.tensor_copy(x_ahead[:], x0[0][:].indirect(picks(0, HALF + QUART)))
+        h_q.append(quantise([side[:, QUART:HALF] for side in first_half], h_bf[1]))
         up_q = []
         for u in range(2):
             up_bf = shared([P, P * PACK], BF16, f"up_bf{u}", AT_UP_BF + 2 * WIDE * u)
@@ -276,38 +266,38 @@ def tile_list_xcross_res_none_kernel(
                 up_raw[:, :, u * P : (u + 1) * P].rearrange("p t (c i) -> p c t i", i=4),
             )
             up_q.append(quantise(mx_pair(P, f"up_q{u}"), up_bf))
-        x_late[0, 1] = gather_x(shared([P, QUART], F32, "x_011", AT_UP_BF), 0, HALF + QUART)
+        v[HALF + QUART] = shared([P, PASSES * 2 * QUART], U8, "v3", AT_H2 + 3 * PACK * QUART)
+        part(HALF + QUART, last_pairs)
+        x_last = shared([P, QUART], F32, "x_last", AT_H2 + 2 * PACK * QUART)
+        nc.vector.tensor_copy(x_last[:], x0[0][:].indirect(picks(HALF + QUART, QUART)))
         for c in range(2):
-            down(1, c, h_bf[2][:, c * WIDE : (c + 1) * WIDE], 4 + c)
-        third = shared([P, QUART], U32, "h_q2_codes", AT_UP_BF + 4 * QUART), own([P, QUART], U8, "h_q2_scales")
-        h_q.append(quantise(third, h_bf[2]))
-        opened = [in_bank([P, QUART], f"y{u}_third", 3 - u) for u in range(2)]
-        for u in (1, 0):
-            y_wb4(opened[u][:], u, 1, 0, True)
+            copy_h(h_bf[2][:, c * WIDE : (c + 1) * WIDE], down_block(1, c, 4 + c))
+
         for u in range(2):
-            y_wb8(y[u][:], u, 0, 0)
-            y_up(y[u][:], u, first_half)
-        finish(0, 0, y[0][:], x_first[:, 0:HALF])
-        finish_fused(1, 0, y[1][:])
+            y_tier(y_half[u][:], u, 0, 8, False)
+            y_up(y_half[u][:], u, first_half)
+        finish(0, 0, y_half[0][:], x_ahead[:, 0:HALF])
+        h_q.append(quantise(mx_pair(QUART, "h_q2"), h_bf[2]))
+        finish_fused(1, 0, y_half[1][:])
         for c in range(2):
-            down(1, 2 + c, h_bf[3][:, c * WIDE : (c + 1) * WIDE], 4 + c)
-        x_late[1, 1] = gather_x(shared([P, QUART], F32, "x_111", AT_H2), 1, HALF + QUART)
+            copy_h(h_bf[3][:, c * WIDE : (c + 1) * WIDE], down_block(1, 2 + c, 4 + c))
+        x_end = shared([P, QUART], F32, "x_end", AT_H2)
+        nc.vector.tensor_copy(x_end[:], x0[1][:].indirect(picks(HALF + QUART, QUART)))
         h_q.append(quantise(mx_pair(QUART, "h_q3"), h_bf[3]))
+        gathered = {(0, 2): x_ahead[:, HALF:], (0, 3): x_last[:], (1, 3): x_end[:]}
+
+        def both_tiers(u, q):
+            sums = piece(u, q)
+            y_tier(sums[:], u, q, 8, True)
+            y_tier(sums[:], u, q, 4, False)
+            return sums
 
         def close(sums, u, q):
             y_up(sums[:], u, h_q[q])
-            if (u, q - 2) in x_late:
-                finish(u, q * QUART, sums[:], x_late[u, q - 2][:, :])
+            if (u, q) in gathered:
+                finish(u, q * QUART, sums[:], gathered[u, q])
             else:
                 finish_fused(u, q * QUART, sums[:])
 
-        for u in (1, 0):
-            y_wb8(opened[u][:], u, 1, 0)
-            close(opened[u], u, 2)
-        last = [in_bank([P, QUART], f"y{u}_last", 5 - u) for u in range(2)]
-        y_wb4(last[1][:], 1, 1, QUART, True)
-        y_wb8(last[1][:], 1, 1, QUART)
-        y_wb4(last[0][:], 0, 1, QUART, True)
-        close(last[1], 1, 3)
-        y_wb8(last[0][:], 0, 1, QUART)
-        close(last[0], 0, 3)
+        for u, q in ((1, 2), (0, 2), (1, 3), (0, 3)):
+            close(both_tiers(u, q), u, q)

@@ -176,8 +176,8 @@ def tile_list_xcross_res_none_kernel(
 
         for repeat in range(WARM_PASSES):
             nc.tensor.matmul_mx(
-                warm[:], lhsT=tab_rows[:, 0 : 2 * P].bitcast(FP4X4), lhsT_scale=early[1][:, 0:P],
-                rhs=tab_rows[:, 0 : 2 * HALF].bitcast(FP4X4), rhs_scale=tab_rows[:, 0:HALF], start=True, stop=True,
+                warm[:], lhsT=tab_rows[:, 0 : 2 * P].bitcast(FP4X4), lhsT_scale=tab_rows[:, 0:P],
+                rhs=tab[:, 0:QUART].bitcast(U8).bitcast(FP4X4), rhs_scale=tab_rows[:, 0:HALF], start=True, stop=True,
             )
 
         def y_up(dst, u, h_q):

@@ -26,7 +26,6 @@ QUART = J // 4
 BLOCK = HALF // PACK
 ROW0 = P - 16 * PASSES
 BANK_BYTES = 2048
-WARM_PASSES = 3
 
 DN_COL, W4_COL, W8_COL, TAB_COL, STAGE_COLS = 0, R, R + N, R + 2 * N, R + 2 * N + HALF
 
@@ -174,11 +173,16 @@ def tile_list_xcross_res_none_kernel(
 
         warm = in_bank([P, HALF], "warm", 7)
 
-        for repeat in range(WARM_PASSES):
+        def warm_up(codes, scales):
+            count = codes.shape[1] // 2
             nc.tensor.matmul_mx(
-                warm[:], lhsT=tab_rows[:, 0 : 2 * P].bitcast(FP4X4), lhsT_scale=tab_rows[:, 0:P],
-                rhs=tab[:, 0:QUART].bitcast(U8).bitcast(FP4X4), rhs_scale=tab_rows[:, 0:HALF], start=True, stop=True,
+                warm[:, 0:count], lhsT=tab_rows[:, 0 : 2 * P].bitcast(FP4X4), lhsT_scale=scales,
+                rhs=codes.bitcast(FP4X4), rhs_scale=tab_rows[:, 0:count], start=True, stop=True,
             )
+
+        warm_up(tab_rows[:, 0 : 2 * HALF], early[1][:, 0:P])
+        for count in (HALF, HALF, QUART):
+            warm_up(tab[:, 0 : count // 2].bitcast(U8), tab_rows[:, 0:P])
 
         def y_up(dst, u, h_q):
             nc.tensor.matmul_mx(

@@ -106,16 +106,16 @@ def tile_list_xcross_res_none_kernel(
             col = TAB_COL + c * QUART
             nc.vector.tensor_copy(stage[ROW0:P, col : col + QUART].bitcast(I32), early[c][ROW0:P, :].bitcast(I32))
         spread(planes[0], stage[:])
-        w4 = own([P, PASSES * 2 * N], U8, "w4")
-        nc.sync.dma_start(
-            w4[:].bitcast(I32).rearrange("p (a c) -> p a c", a=PASSES),
-            wb4_words.bitcast(I32).rearrange("a p c -> p a c"),
-        )
         late = shared([P, HALF], U8, "picked_late", AT_PICKED)
         nc.vector.tensor_copy(late[:], tab_rows[:].indirect(picks(HALF, HALF)))
         x0 = [own([P, T], F32, f"x0_{u}") for u in range(2)]
         nc.sync.dma_start(x0[0][:], x0T[0:P, :])
         spread(planes[1], late[:])
+        w4 = own([P, PASSES * 2 * N], U8, "w4")
+        nc.sync.dma_start(
+            w4[:].bitcast(I32).rearrange("p (a c) -> p a c", a=PASSES),
+            wb4_words.bitcast(I32).rearrange("a p c -> p a c"),
+        )
         up_raw = shared([P, PACK, N], F32, "up_raw", AT_H2)
         for i in range(2):
             nc.sync.dma_start(up_raw[i:P:2, :, :], upw.rearrange("(m t i) n -> i m t n", t=PACK, i=2)[i])
@@ -224,10 +224,9 @@ def tile_list_xcross_res_none_kernel(
             store(u, first, res)
 
         WIDE = PACK * BLOCK
-        h_bf = [own([P, QUART * PACK], BF16, f"h_bf{c}") for c in range(2)]
-        h_bf += [shared([P, QUART * PACK], BF16, "h_bf2", AT_H2), own([P, QUART * PACK], BF16, "h_bf3")]
+        h_bf = {q: own([P, QUART * PACK], BF16, f"h_bf{q}") for q in (0, 1, 3)}
         y_half = [in_bank([P, HALF], f"y_half{u}", u) for u in range(2)]
-        piece_bank = {(1, 2): 3, (0, 2): 2, (1, 3): 6, (0, 3): 7}
+        piece_bank = {(1, 2): 3, (0, 2): 2, (1, 3): 4, (0, 3): 5}
 
         def piece(u, q):
             return in_bank([P, QUART], f"y{u}_{q}", piece_bank[u, q])
@@ -254,14 +253,22 @@ def tile_list_xcross_res_none_kernel(
             copy_h(h_bf[0][:, c * WIDE : (c + 1) * WIDE], down_block(0, c, 4 + c))
         first_half = mx_pair(HALF, "h_q01")
         h_q = [quantise([side[:, 0:QUART] for side in first_half], h_bf[0])]
-        y_tier(y_half[0][:, 0:QUART], 0, 0, 4, True)
         for c in range(2):
             copy_h(h_bf[1][:, c * WIDE : (c + 1) * WIDE], down_block(0, 2 + c, 6 + c))
-        y_tier(y_half[0][:, QUART:HALF], 0, 1, 4, False)
-        y_tier(y_half[1][:], 1, 0, 4, True)
-        x_ahead = own([P, HALF + QUART], F32, "x_ahead")
-        nc.vector.tensor_copy(x_ahead[:], x0[0][:].indirect(picks(0, HALF + QUART)))
+        x_ahead = own([P, J], F32, "x_ahead")
+        nc.vector.tensor_copy(x_ahead[:], x0[0][:].indirect(entries[:]))
         h_q.append(quantise([side[:, QUART:HALF] for side in first_half], h_bf[1]))
+        third_banks = [down_block(1, c, 4 + c) for c in range(2)]
+        third_bf = [own([P, WIDE], BF16, "h_bf20"), shared([P, WIDE], BF16, "h_bf21", AT_H2 + 4 * QUART)]
+        h_q.append(mx_pair(QUART, "h_q2"))
+
+        def third_block(c):
+            copy_h(third_bf[c][:], third_banks[c])
+            quantise([side[:, c * BLOCK : (c + 1) * BLOCK] for side in h_q[2]], third_bf[c])
+
+        third_block(0)
+        for u in range(2):
+            y_tier(y_half[u][:], u, 0, 4, True)
         up_q = []
         for u in range(2):
             up_bf = shared([P, P * PACK], BF16, f"up_bf{u}", AT_UP_BF + 2 * WIDE * u)
@@ -270,25 +277,22 @@ def tile_list_xcross_res_none_kernel(
                 up_raw[:, :, u * P : (u + 1) * P].rearrange("p t (c i) -> p c t i", i=4),
             )
             up_q.append(quantise(mx_pair(P, f"up_q{u}"), up_bf))
-        v[HALF + QUART] = shared([P, PASSES * 2 * QUART], U8, "v3", AT_H2 + 3 * PACK * QUART)
+        v[HALF + QUART] = shared([P, PASSES * 2 * QUART], U8, "v3", AT_H2)
         part(HALF + QUART, last_pairs)
-        x_last = shared([P, QUART], F32, "x_last", AT_H2 + 2 * PACK * QUART)
-        nc.vector.tensor_copy(x_last[:], x0[0][:].indirect(picks(HALF + QUART, QUART)))
-        for c in range(2):
-            copy_h(h_bf[2][:, c * WIDE : (c + 1) * WIDE], down_block(1, c, 4 + c))
+        third_block(1)
 
         for u in range(2):
             y_tier(y_half[u][:], u, 0, 8, False)
+        for u in range(2):
             y_up(y_half[u][:], u, first_half)
         finish(0, 0, y_half[0][:], x_ahead[:, 0:HALF])
-        h_q.append(quantise(mx_pair(QUART, "h_q2"), h_bf[2]))
+        x_end = own([P, QUART], F32, "x_end")
+        nc.vector.tensor_copy(x_end[:], x0[1][:].indirect(picks(HALF + QUART, QUART)))
         finish_fused(1, 0, y_half[1][:])
         for c in range(2):
-            copy_h(h_bf[3][:, c * WIDE : (c + 1) * WIDE], down_block(1, 2 + c, 4 + c))
-        x_end = shared([P, QUART], F32, "x_end", AT_H2)
-        nc.vector.tensor_copy(x_end[:], x0[1][:].indirect(picks(HALF + QUART, QUART)))
+            copy_h(h_bf[3][:, c * WIDE : (c + 1) * WIDE], down_block(1, 2 + c, 6 + c))
         h_q.append(quantise(mx_pair(QUART, "h_q3"), h_bf[3]))
-        gathered = {(0, 2): x_ahead[:, HALF:], (0, 3): x_last[:], (1, 3): x_end[:]}
+        gathered = {(0, 2): x_ahead[:, HALF : HALF + QUART], (0, 3): x_ahead[:, HALF + QUART :], (1, 3): x_end[:]}
 
         def both_tiers(u, q):
             sums = piece(u, q)

@@ -33,6 +33,7 @@ AT_PICKED = 0
 AT_PAIRS = AT_PICKED + HALF
 AT_UP_BF = AT_PAIRS + 4 * HALF
 AT_H2 = AT_UP_BF + 2 * PACK * N
+AT_DN = AT_H2 + 4 * PACK * N
 
 
 def tile_list_xcross_res_none_kernel(
@@ -56,9 +57,9 @@ def tile_list_xcross_res_none_kernel(
         def load_scale_rows(queue, dst, scales):
             queue.dma_start(dst.bitcast(I32), scales.bitcast(I32).rearrange("a q n -> q a n"))
 
-        def spread(plane, rows):
+        def spread(plane, rows, queues):
             for quad in (0, 2, 1, 3):
-                nc.sync.dma_start(
+                queues[quad // 2].dma_start(
                     plane[32 * quad : 32 * quad + 4, :].bitcast(I32).rearrange("p (a c) -> p a c", a=PASSES),
                     rows[ROW0 + 8 * quad : ROW0 + 8 * quad + 8, :].bitcast(I32),
                 )
@@ -83,7 +84,7 @@ def tile_list_xcross_res_none_kernel(
         nc.scalar.dma_start(b_rows[0 : N // P, :], b.rearrange("(u p) -> u p", p=P))
         tab = own([P, T], U32, "tab")
         load_words(tab, tab_words[0])
-        dn_raw = [own([P, R], U32, f"dn_raw{a}") for a in range(PASSES)]
+        dn_raw = [own([P, R], U32, "dn_raw0"), shared([P, R], U32, "dn_raw1", AT_DN)]
         for a in range(PASSES):
             load_words(dn_raw[a], dn_words[a])
 
@@ -105,12 +106,12 @@ def tile_list_xcross_res_none_kernel(
         for c in range(2):
             col = TAB_COL + c * QUART
             nc.vector.tensor_copy(stage[ROW0:P, col : col + QUART].bitcast(I32), early[c][ROW0:P, :].bitcast(I32))
-        spread(planes[0], stage[:])
+        spread(planes[0], stage[:], (nc.sync, nc.scalar))
         late = shared([P, HALF], U8, "picked_late", AT_PICKED)
         nc.vector.tensor_copy(late[:], tab_rows[:].indirect(picks(HALF, HALF)))
         x0 = [own([P, T], F32, f"x0_{u}") for u in range(2)]
         nc.sync.dma_start(x0[0][:], x0T[0:P, :])
-        spread(planes[1], late[:])
+        spread(planes[1], late[:], (nc.sync, nc.sync))
         w4 = own([P, PASSES * 2 * N], U8, "w4")
         nc.sync.dma_start(
             w4[:].bitcast(I32).rearrange("p (a c) -> p a c", a=PASSES),
@@ -168,7 +169,7 @@ def tile_list_xcross_res_none_kernel(
 
         b_turned = in_bank([P, P], "b_turned", 3)
         nc.tensor.transpose(b_turned[:], b_rows[:], identity[:])
-        bias1 = own([P, N // P], F32, "bias1")
+        bias1 = shared([P, N // P], F32, "bias1", AT_DN)
         nc.scalar.activation(bias1[:], b_turned[:, 0 : N // P], IDENTITY, bias=1.0)
 
         warm = in_bank([P, HALF], "warm", 7)
@@ -260,13 +261,9 @@ def tile_list_xcross_res_none_kernel(
         h_q.append(quantise([side[:, QUART:HALF] for side in first_half], h_bf[1]))
         third_banks = [down_block(1, c, 4 + c) for c in range(2)]
         third_bf = [own([P, WIDE], BF16, "h_bf20"), shared([P, WIDE], BF16, "h_bf21", AT_H2 + 4 * QUART)]
-        h_q.append(mx_pair(QUART, "h_q2"))
+        h_q.append((shared([P, QUART], U32, "h_q2_codes", AT_H2 + 8 * QUART), own([P, QUART], U8, "h_q2_scales")))
 
-        def third_block(c):
-            copy_h(third_bf[c][:], third_banks[c])
-            quantise([side[:, c * BLOCK : (c + 1) * BLOCK] for side in h_q[2]], third_bf[c])
-
-        third_block(0)
+        copy_h(third_bf[0][:], third_banks[0])
         for u in range(2):
             y_tier(y_half[u][:], u, 0, 4, True)
         up_q = []
@@ -279,7 +276,9 @@ def tile_list_xcross_res_none_kernel(
             up_q.append(quantise(mx_pair(P, f"up_q{u}"), up_bf))
         v[HALF + QUART] = shared([P, PASSES * 2 * QUART], U8, "v3", AT_H2)
         part(HALF + QUART, last_pairs)
-        third_block(1)
+        copy_h(third_bf[1][:], third_banks[1])
+        for c in range(2):
+            quantise([side[:, c * BLOCK : (c + 1) * BLOCK] for side in h_q[2]], third_bf[c])
 
         for u in range(2):
             y_tier(y_half[u][:], u, 0, 8, False)

@@ -26,6 +26,8 @@ QUART = J // 4
 BLOCK = HALF // PACK
 ROW0 = P - 16 * PASSES
 BANK_BYTES = 2048
+MOVING_SKEW = 128
+SCALE_SKEW = 64
 
 DN_COL, W4_COL, W8_COL, TAB_COL, STAGE_COLS = 0, R, R + N, R + 2 * N, R + 2 * N + HALF
 
@@ -47,6 +49,9 @@ def tile_list_xcross_res_none_kernel(
 
         def own(shape, dtype, name):
             return held.tile(shape, dtype, name=name, align_bytes=256)
+
+        def skewed(count, dtype, size, skew, name):
+            return own([P, count + skew // size], dtype, name)[:, skew // size :]
 
         def shared(shape, dtype, name, offset, align=256):
             return reused.tile(shape, dtype, name=name, offset=offset, align_bytes=align)
@@ -89,9 +94,9 @@ def tile_list_xcross_res_none_kernel(
             load_words(dn_raw[a], dn_words[a])
 
         nc.vector.memset(tab_rows[0:ROW0, :].bitcast(I32), 0)
-        planes = [own([P, PASSES * STAGE_COLS], U8, "plane0"), own([P, PASSES * HALF], U8, "plane1")]
+        planes = [skewed(PASSES * cols, U8, 1, SCALE_SKEW, f"plane{h}") for h, cols in enumerate((STAGE_COLS, HALF))]
         for plane in planes:
-            nc.vector.memset(plane[:].bitcast(I32), 0)
+            nc.vector.memset(plane.bitcast(I32), 0)
 
         def picks(first, count):
             return entries[:, first // 16 : (first + count) // 16]
@@ -124,7 +129,7 @@ def tile_list_xcross_res_none_kernel(
         nc.sync.dma_start(w8[:], wb8_words.rearrange("a p n c -> p a (n c)").bitcast(I32))
         nc.sync.dma_start(x0[1][:], x0T[P : 2 * P, :])
 
-        v = {0: own([P, PASSES * 2 * HALF], U8, "v0"), HALF: own([P, PASSES * 2 * QUART], U8, "v2")}
+        v = {at: skewed(PASSES * 2 * count, U8, 1, MOVING_SKEW, f"v{at}") for at, count in ((0, HALF), (HALF, QUART))}
 
         def gather_words(first, count, at):
             pairs = shared([P, count], U32, f"pairs{first}", at)
@@ -135,7 +140,7 @@ def tile_list_xcross_res_none_kernel(
             base = max(key for key in v if key <= first)
             cols = slice(first - base, first - base + pairs.shape[1])
             nc.vector.tensor_copy(
-                v[base][:].bitcast(U16).rearrange("p (a j) -> p a j", a=PASSES)[:, :, cols],
+                v[base][:, :].bitcast(U16).rearrange("p (a j) -> p a j", a=PASSES)[:, :, cols],
                 pairs[:].bitcast(U16).rearrange("p (j a) -> p a j", a=PASSES),
             )
 
@@ -187,7 +192,7 @@ def tile_list_xcross_res_none_kernel(
 
         def y_up(dst, u, h_q):
             nc.tensor.matmul_mx(
-                dst, lhsT=up_q[u][0][:].bitcast(FP8X4), lhsT_scale=up_q[u][1][:],
+                dst, lhsT=up_q[u][0].bitcast(FP8X4), lhsT_scale=up_q[u][1],
                 rhs=h_q[0][:, :].bitcast(FP8X4), rhs_scale=h_q[1][:, :], start=False, stop=True,
             )
 
@@ -201,8 +206,8 @@ def tile_list_xcross_res_none_kernel(
         def copy_h(dst, bank):
             nc.scalar.copy(dst.rearrange("p (j t) -> p j t", t=PACK), bank[:].rearrange("p t j -> p j t"))
 
-        def mx_pair(width, name):
-            return own([P, width], U32, name + "_codes"), own([P, width], U8, name + "_scales")
+        def mx_pair(width, name, skew=MOVING_SKEW):
+            return skewed(width, U32, 4, skew, name + "_codes"), skewed(width, U8, 1, SCALE_SKEW, name + "_scales")
 
         def quantise(dst, src):
             nc.vector.quantize_mx(dst[0][:, :].bitcast(FP8X4), dst[1][:, :], src[:])
@@ -260,8 +265,8 @@ def tile_list_xcross_res_none_kernel(
         nc.vector.tensor_copy(x_ahead[:], x0[0][:].indirect(entries[:]))
         h_q.append(quantise([side[:, QUART:HALF] for side in first_half], h_bf[1]))
         third_banks = [down_block(1, c, 4 + c) for c in range(2)]
-        third_bf = [own([P, WIDE], BF16, "h_bf20"), shared([P, WIDE], BF16, "h_bf21", AT_H2 + 4 * QUART)]
-        h_q.append((shared([P, QUART], U32, "h_q2_codes", AT_H2 + 8 * QUART), own([P, QUART], U8, "h_q2_scales")))
+        third_bf = [own([P, WIDE], BF16, "h_bf20"), shared([P, WIDE], BF16, "h_bf21", AT_H2 + 5 * QUART)]
+        h_q.append((shared([P, QUART], U32, "h_q2_codes", AT_H2 + 10 * QUART + MOVING_SKEW, align=MOVING_SKEW), skewed(QUART, U8, 1, SCALE_SKEW, "h_q2_scales")))
 
         copy_h(third_bf[0][:], third_banks[0])
         for u in range(2):
@@ -273,8 +278,8 @@ def tile_list_xcross_res_none_kernel(
                 up_bf[:].rearrange("p (c i t) -> p c t i", t=PACK, i=4),
                 up_raw[:, :, u * P : (u + 1) * P].rearrange("p t (c i) -> p c t i", i=4),
             )
-            up_q.append(quantise(mx_pair(P, f"up_q{u}"), up_bf))
-        v[HALF + QUART] = shared([P, PASSES * 2 * QUART], U8, "v3", AT_H2)
+            up_q.append(quantise(mx_pair(P, f"up_q{u}", 0), up_bf))
+        v[HALF + QUART] = shared([P, PASSES * 2 * QUART], U8, "v3", AT_H2 + MOVING_SKEW, align=MOVING_SKEW)
         part(HALF + QUART, last_pairs)
         copy_h(third_bf[1][:], third_banks[1])
         for c in range(2):

from contextlib import ExitStack

import concourse.mybir as mybir
from concourse.masks import make_identity

K, R, N, T, J = 1024, 512, 256, 2048, 1024
FLOPS = 2 * J * (K * R + 2 * K * N + R * N)

F32 = mybir.dt.float32
BF16 = mybir.dt.bfloat16
I32 = mybir.dt.int32
U32 = mybir.dt.uint32
U16 = mybir.dt.uint16
U8 = mybir.dt.uint8
FP8X4 = mybir.dt.float8_e4m3fn_x4
FP4X4 = mybir.dt.float4_e2m1fn_x4
ADD = mybir.AluOpType.add
MULT = mybir.AluOpType.mult
IDENTITY = mybir.ActivationFunctionType.Identity

P = 128
PACK = 4
PASSES = K // (P * PACK)
HALF = J // 2
QUART = J // 4
BLOCK = HALF // PACK
ROW0 = P - 16 * PASSES
BANK_BYTES = 2048
MOVING_SKEW = 128
SCALE_SKEW = 64

DN_COL, W4_COL, W8_COL, TAB_COL, STAGE_COLS = 0, R, R + N, R + 2 * N, R + 2 * N + HALF

AT_PICKED = 0
AT_PAIRS = AT_PICKED + HALF
AT_UP_BF = AT_PAIRS + 4 * HALF
AT_H2 = AT_UP_BF + 2 * PACK * N
AT_DN = AT_H2 + 4 * PACK * N


def tile_list_xcross_res_none_kernel(
    tc, tab_words, tab_scales, wb4_words, wb4_scales, wb8_words, wb8_scales, dn_words, dn_scales, upw, x0T, b, offs, out
):
    nc = tc.nc
    with ExitStack() as ctx:
        held = ctx.enter_context(tc.tile_pool(name="held", bufs=1))
        reused = ctx.enter_context(tc.tile_pool(name="reused", bufs=1))
        psum = ctx.enter_context(tc.psum_pool(name="psum", bufs=1))

        def own(shape, dtype, name):
            return held.tile(shape, dtype, name=name, align_bytes=256)

        def skewed(count, dtype, size, skew, name):
            return own([P, count + skew // size], dtype, name)[:, skew // size :]

        def shared(shape, dtype, name, offset, align=256):
            return reused.tile(shape, dtype, name=name, offset=offset, align_bytes=align)

        def in_bank(shape, name, bank):
            return psum.tile(shape, F32, name=name, offset=bank * BANK_BYTES)

        def load_scale_rows(queue, dst, scales):
            queue.dma_start(dst.bitcast(I32), scales.bitcast(I32).rearrange("a q n -> q a n"))

        def spread(plane, rows, queues):
            for quad in (0, 2, 1, 3):
                queues[quad // 2].dma_start(
                    plane[32 * quad : 32 * quad + 4, :].bitcast(I32).rearrange("p (a c) -> p a c", a=PASSES),
                    rows[ROW0 + 8 * quad : ROW0 + 8 * quad + 8, :].bitcast(I32),
                )

        def load_words(dst, words):
            nc.sync.dma_start(dst[:].bitcast(I32), words.rearrange("p n c -> p (n c)").bitcast(I32))

        b_rows = own([P, P], F32, "b_rows")
        nc.vector.memset(b_rows[:], 0.0)
        identity = own([P, P], F32, "identity")
        make_identity(nc, identity[:])

        dn_rows = own([P, R], U8, "dn_rows")
        load_scale_rows(nc.scalar, dn_rows[ROW0:P, :], dn_scales)
        tab_rows = own([P, T], U8, "tab_rows")
        load_scale_rows(nc.sync, tab_rows[ROW0:P, :], tab_scales)
        entries = held.tile([P, J // 16], U16, name="entries")
        nc.sync.dma_start(entries[:], offs)
        stage = own([P, STAGE_COLS], U8, "stage")
        load_scale_rows(nc.scalar, stage[ROW0:P, W4_COL : W4_COL + N], wb4_scales)
        load_scale_rows(nc.sync, stage[ROW0:P, W8_COL : W8_COL + N], wb8_scales)
        nc.scalar.dma_start(b_rows[0 : N // P, :], b.rearrange("(u p) -> u p", p=P))
        tab = own([P, T], U32, "tab")
        load_words(tab, tab_words[0])
        dn_raw = [own([P, R], U32, "dn_raw0"), shared([P, R], U32, "dn_raw1", AT_DN)]
        for a in range(PASSES):
            load_words(dn_raw[a], dn_words[a])

        nc.vector.memset(tab_rows[0:ROW0, :].bitcast(I32), 0)
        planes = [skewed(PASSES * cols, U8, 1, SCALE_SKEW, f"plane{h}") for h, cols in enumerate((STAGE_COLS, HALF))]
        for plane in planes:
            nc.vector.memset(plane.bitcast(I32), 0)

        def picks(first, count):
            return entries[:, first // 16 : (first + count) // 16]

        nc.scalar.copy(
            stage[ROW0:P, DN_COL : DN_COL + R].bitcast(U16).rearrange("p (t m) -> p t m", t=PACK),
            dn_rows[ROW0:P, :].bitcast(U16).rearrange("p (m t) -> p t m", t=PACK),
        )
        early = [shared([P, QUART], U8, "picked_a", AT_PICKED), own([P, QUART], U8, "picked_b")]
        for c in range(2):
            nc.vector.tensor_copy(early[c][:], tab_rows[:].indirect(picks(c * QUART, QUART)))
        for c in range(2):
            col = TAB_COL + c * QUART
            nc.vector.tensor_copy(stage[ROW0:P, col : col + QUART].bitcast(I32), early[c][ROW0:P, :].bitcast(I32))
        spread(planes[0], stage[:], (nc.sync, nc.scalar))
        late = shared([P, HALF], U8, "picked_late", AT_PICKED)
        nc.vector.tensor_copy(late[:], tab_rows[:].indirect(picks(HALF, HALF)))
        x0 = [own([P, T], F32, f"x0_{u}") for u in range(2)]
        nc.sync.dma_start(x0[0][:], x0T[0:P, :])
        spread(planes[1], late[:], (nc.sync, nc.sync))
        w4 = own([P, PASSES * 2 * N], U8, "w4")
        nc.sync.dma_start(
            w4[:].bitcast(I32).rearrange("p (a c) -> p a c", a=PASSES),
            wb4_words.bitcast(I32).rearrange("a p c -> p a c"),
        )
        up_raw = shared([P, PACK, N], F32, "up_raw", AT_H2)
        for i in range(2):
            nc.sync.dma_start(up_raw[i:P:2, :, :], upw.rearrange("(m t i) n -> i m t n", t=PACK, i=2)[i])
        w8 = own([P, PASSES, N], I32, "w8")
        nc.sync.dma_start(w8[:], wb8_words.rearrange("a p n c -> p a (n c)").bitcast(I32))
        nc.sync.dma_start(x0[1][:], x0T[P : 2 * P, :])

        v = {at: skewed(PASSES * 2 * count, U8, 1, MOVING_SKEW, f"v{at}") for at, count in ((0, HALF), (HALF, QUART))}

        def gather_words(first, count, at):
            pairs = shared([P, count], U32, f"pairs{first}", at)
            nc.vector.tensor_copy(pairs[:], tab[:].indirect(picks(first, count)))
            return pairs

        def part(first, pairs):
            base = max(key for key in v if key <= first)
            cols = slice(first - base, first - base + pairs.shape[1])
            nc.vector.tensor_copy(
                v[base][:, :].bitcast(U16).rearrange("p (a j) -> p a j", a=PASSES)[:, :, cols],
                pairs[:].bitcast(U16).rearrange("p (j a) -> p a j", a=PASSES),
            )

        both = [gather_words(0, BLOCK, AT_PAIRS), gather_words(BLOCK, BLOCK, AT_PAIRS + 4 * QUART)]
        for c in range(2):
            part(c * BLOCK, both[c])
        middle = [gather_words(q * QUART, QUART, AT_PAIRS + 4 * QUART * (q - 1)) for q in (1, 2)]
        for q in (1, 2):
            part(q * QUART, middle[q - 1])
        last_pairs = gather_words(3 * QUART, QUART, AT_PAIRS)

        dn = [own([P, R], U32, f"dn{a}") for a in range(PASSES)]
        for a in range(PASSES):
            nc.scalar.copy(
                dn[a][:].rearrange("p (t g m i) -> p g t m i", t=PACK, m=2, i=2),
                dn_raw[a][:].rearrange("p (g m t i) -> p g t m i", t=PACK, m=2, i=2),
            )

        def v_operand(h, a, first, count):
            base = max(key for key in v if key <= h * HALF + first)
            at = a * v[base].shape[1] // PASSES + 2 * (h * HALF + first - base)
            codes = v[base][:, at : at + 2 * count].bitcast(FP4X4)
            col = a * STAGE_COLS + TAB_COL + first if h == 0 else a * HALF + first
            return codes, planes[h][:, col : col + count]

        def w_scales(a, col):
            return planes[0][:, a * STAGE_COLS + col : a * STAGE_COLS + col + P]

        def w4_codes(a, u):
            return w4[:, 2 * (a * N + u * P) : 2 * (a * N + (u + 1) * P)].bitcast(FP4X4)

        b_turned = in_bank([P, P], "b_turned", 3)
        nc.tensor.transpose(b_turned[:], b_rows[:], identity[:])
        bias1 = shared([P, N // P], F32, "bias1", AT_DN)
        nc.scalar.activation(bias1[:], b_turned[:, 0 : N // P], IDENTITY, bias=1.0)

        warm = in_bank([P, HALF], "warm", 7)

        def warm_up(codes, scales):
            count = codes.shape[1] // 2
            nc.tensor.matmul_mx(
                warm[:, 0:count], lhsT=tab_rows[:, 0 : 2 * P].bitcast(FP4X4), lhsT_scale=scales,
                rhs=codes.bitcast(FP4X4), rhs_scale=tab_rows[:, 0:count], start=True, stop=True,
            )

        warm_up(tab_rows[:, 0 : 2 * HALF], early[1][:, 0:P])
        for count in (HALF, HALF, QUART):
            warm_up(tab[:, 0 : count // 2].bitcast(U8), tab_rows[:, 0:P])

        def y_up(dst, u, h_q):
            nc.tensor.matmul_mx(
                dst, lhsT=up_q[u][0].bitcast(FP8X4), lhsT_scale=up_q[u][1],
                rhs=h_q[0][:, :].bitcast(FP8X4), rhs_scale=h_q[1][:, :], start=False, stop=True,
            )

        def down_pass(bank, h, c, a, t, start, stop):
            codes, scales = v_operand(h, a, c * BLOCK, BLOCK)
            nc.tensor.matmul_mx(
                bank[:, t, :], lhsT=dn[a][:, t * P : (t + 1) * P].bitcast(FP8X4),
                lhsT_scale=w_scales(a, DN_COL + t * P), rhs=codes, rhs_scale=scales, start=start, stop=stop,
            )

        def copy_h(dst, bank):
            nc.scalar.copy(dst.rearrange("p (j t) -> p j t", t=PACK), bank[:].rearrange("p t j -> p j t"))

        def mx_pair(width, name, skew=MOVING_SKEW):
            return skewed(width, U32, 4, skew, name + "_codes"), skewed(width, U8, 1, SCALE_SKEW, name + "_scales")

        def quantise(dst, src):
            nc.vector.quantize_mx(dst[0][:, :].bitcast(FP8X4), dst[1][:, :], src[:])
            return dst

        def store(u, first, res):
            nc.sync.dma_start(out[u * P : (u + 1) * P, first : first + res.shape[1]], res[:])

        def finish(u, first, sums, x_picked):
            res = own([P, sums.shape[1]], F32, f"res{u}_{first}")
            nc.vector.scalar_tensor_tensor(res[:], sums, bias1[:, u : u + 1], x_picked, ADD, MULT)
            store(u, first, res)

        def finish_fused(u, first, sums):
            count = sums.shape[1]
            factor = own([P, count], F32, f"factor{u}_{first}")
            nc.scalar.activation(factor[:], sums, IDENTITY, bias=bias1[:, u : u + 1])
            res = own([P, count], F32, f"res{u}_{first}")
            nc.vector.tensor_tensor(res[:], x0[u][:].indirect(picks(first, count)), factor[:], MULT)
            store(u, first, res)

        WIDE = PACK * BLOCK
        h_bf = {q: own([P, QUART * PACK], BF16, f"h_bf{q}") for q in (0, 1, 3)}
        y_half = [in_bank([P, HALF], f"y_half{u}", u) for u in range(2)]
        piece_bank = {(1, 2): 3, (0, 2): 2, (1, 3): 4, (0, 3): 5}

        def piece(u, q):
            return in_bank([P, QUART], f"y{u}_{q}", piece_bank[u, q])

        def y_tier(dst, u, q, tier, opens):
            for a in range(PASSES):
                codes, scales = v_operand(q // 2, a, (q % 2) * QUART, dst.shape[1])
                if tier == 4:
                    w, w_scale = w4_codes(a, u), w_scales(a, W4_COL + u * P)
                else:
                    w, w_scale = w8[:, a, u * P : (u + 1) * P].bitcast(FP8X4), w_scales(a, W8_COL + u * P)
                nc.tensor.matmul_mx(
                    dst, lhsT=w, lhsT_scale=w_scale, rhs=codes, rhs_scale=scales, start=(opens and a == 0), stop=False
                )

        def down_block(h, c, at):
            bank = in_bank([P, PACK, BLOCK], f"h{h}{c}", at)
            for a in range(PASSES):
                for t in range(PACK):
                    down_pass(bank, h, c, a, t, a == 0 and t == 0, a == PASSES - 1 and t == PACK - 1)
            return bank

        for c in range(2):
            copy_h(h_bf[0][:, c * WIDE : (c + 1) * WIDE], down_block(0, c, 4 + c))
        first_half = mx_pair(HALF, "h_q01")
        h_q = [quantise([side[:, 0:QUART] for side in first_half], h_bf[0])]
        for c in range(2):
            copy_h(h_bf[1][:, c * WIDE : (c + 1) * WIDE], down_block(0, 2 + c, 6 + c))
        x_ahead = own([P, J], F32, "x_ahead")
        nc.vector.tensor_copy(x_ahead[:], x0[0][:].indirect(entries[:]))
        h_q.append(quantise([side[:, QUART:HALF] for side in first_half], h_bf[1]))
        third_banks = [down_block(1, c, 4 + c) for c in range(2)]
        third_bf = [own([P, WIDE], BF16, "h_bf20"), shared([P, WIDE], BF16, "h_bf21", AT_H2 + 5 * QUART)]
        h_q.append((shared([P, QUART], U32, "h_q2_codes", AT_H2 + 10 * QUART + MOVING_SKEW, align=MOVING_SKEW), skewed(QUART, U8, 1, SCALE_SKEW, "h_q2_scales")))

        copy_h(third_bf[0][:], third_banks[0])
        for u in range(2):
            y_tier(y_half[u][:], u, 0, 4, True)
        up_q = []
        for u in range(2):
            up_bf = shared([P, P * PACK], BF16, f"up_bf{u}", AT_UP_BF + 2 * WIDE * u)
            nc.scalar.copy(
                up_bf[:].rearrange("p (c i t) -> p c t i", t=PACK, i=4),
                up_raw[:, :, u * P : (u + 1) * P].rearrange("p t (c i) -> p c t i", i=4),
            )
            up_q.append(quantise(mx_pair(P, f"up_q{u}", 0), up_bf))
        v[HALF + QUART] = shared([P, PASSES * 2 * QUART], U8, "v3", AT_H2 + MOVING_SKEW, align=MOVING_SKEW)
        part(HALF + QUART, last_pairs)
        copy_h(third_bf[1][:], third_banks[1])
        for c in range(2):
            quantise([side[:, c * BLOCK : (c + 1) * BLOCK] for side in h_q[2]], third_bf[c])

        for u in range(2):
            y_tier(y_half[u][:], u, 0, 8, False)
        for u in range(2):
            y_up(y_half[u][:], u, first_half)
        finish(0, 0, y_half[0][:], x_ahead[:, 0:HALF])
        x_end = own([P, QUART], F32, "x_end")
        nc.vector.tensor_copy(x_end[:], x0[1][:].indirect(picks(HALF + QUART, QUART)))
        finish_fused(1, 0, y_half[1][:])
        for c in range(2):
            copy_h(h_bf[3][:, c * WIDE : (c + 1) * WIDE], down_block(1, 2 + c, 6 + c))
        h_q.append(quantise(mx_pair(QUART, "h_q3"), h_bf[3]))
        gathered = {(0, 2): x_ahead[:, HALF : HALF + QUART], (0, 3): x_ahead[:, HALF + QUART :], (1, 3): x_end[:]}

        def both_tiers(u, q):
            sums = piece(u, q)
            y_tier(sums[:], u, q, 8, True)
            y_tier(sums[:], u, q, 4, False)
            return sums

        def close(sums, u, q):
            y_up(sums[:], u, h_q[q])
            if (u, q) in gathered:
                finish(u, q * QUART, sums[:], gathered[u, q])
            else:
                finish_fused(u, q * QUART, sums[:])

        for u, q in ((1, 2), (0, 2), (1, 3), (0, 3)):
            close(both_tiers(u, q), u, q)
